import numpy as np, ml_dtypes
CORES = [2,3,42,43,82,83,122,123]
N = 8
BF = ml_dtypes.bfloat16
def gentries(a):
    return np.ascontiguousarray(a.reshape(8, 16, -1).transpose(0, 2, 1)).reshape(8, -1)
def gtable(e):
    e = np.asarray(e); return np.ascontiguousarray(e.reshape(8, -1, 16).transpose(0, 2, 1)).reshape(128, -1).astype(np.int32)
M, D, SD, Q, SQ, L, V = 128, 32, 7, 8, 9, 128, 5
W, P = M * D, M * Q
def unpack(x):
    x = np.ascontiguousarray(x.astype(np.int64).reshape(N, 8, 16, -1).transpose(0, 1, 3, 2)); return x >> 8, x & 255
def pick(x, i):
    return np.take_along_axis(x, i[..., None], 2)
def cut(lb, lm, pb, pm):
    o = np.argsort(np.concatenate([2 * lb, 2 * pb + 1], axis=-1), axis=-1, kind="stable")
    z = np.take_along_axis(np.concatenate([lb, pb], axis=-1), o, -1); lane = (o < 16).astype(np.int64)
    na = np.add.accumulate(lane, axis=-1) - 1; nb = np.maximum(np.add.accumulate(1 - lane, axis=-1) - 1, 0)
    ln = np.concatenate([z[..., 1:], np.full(z.shape[:-1] + (1,), 4096)], axis=-1) - z
    return z, ln, np.take_along_axis(lm, na, -1), np.take_along_axis(pm, nb, -1)
def weigh(tot, z, ln, a, b):
    ia = D * a + (z >> SD); ib = D * b + (z >> SD)
    sa = np.take_along_axis(tot, ia.reshape(N, 8, -1), 2).reshape(z.shape); sb = np.take_along_axis(tot, ib.reshape(N, 8, -1), 2).reshape(z.shape)
    w = ln * (sa + sb)
    return ia, ib, np.where(sb > sa, b, a), w, np.add.accumulate(w, axis=-1)
def remake(z, ln, den, vis, pb, pm):
    live = vis & (ln > 0)
    last = np.maximum.accumulate(np.where(live, np.arange(32), -1), axis=-1); e = last[..., -1:]
    zz = np.take_along_axis(z, e, -1); name = (Q * np.take_along_axis(den, e, -1) + (zz >> SQ))[..., 0]
    before = np.concatenate([np.full_like(e, -1), last[..., :-1]], axis=-1)
    new = live & ((before < 0) | (den != np.take_along_axis(den, np.maximum(before, 0), -1)))
    place = np.add.accumulate(new.astype(np.int64), axis=-1) - 1
    tb, tm = pick(pb, name), pick(pm, name); late = tb > zz
    tp = place[..., -1:] + np.add.accumulate(late.astype(np.int64), axis=-1)
    to = np.minimum(np.concatenate([np.where(new, place, 16), np.where(late, tp, 16)], axis=-1), 16)
    fb = np.full(z.shape[:-1] + (17,), 4095, np.int64); fm = np.zeros(fb.shape, np.int64)
    np.put_along_axis(fb, to, np.concatenate([z, tb], axis=-1), -1); np.put_along_axis(fm, to, np.concatenate([den, tm], axis=-1), -1)
    return fb[..., :16], fm[..., :16], name
def hand(fb, fm, name):
    return np.roll(fb, 1, axis=0), np.roll(fm, 1, axis=0), np.roll(name, (1, 1), axis=(0, 1))
def begins(rng, *shape):
    b = np.sort((4096 * rng.random(shape + (16,)) ** rng.choice(np.array([1, 1, 2, 3]), shape + (1,))).astype(np.int64), axis=-1); b[..., 0] = 0
    again = rng.random(b.shape) < 0.06; again[..., 0] = False
    b = np.where(again, np.concatenate([b[..., :1], b[..., :-1]], axis=-1), b)
    return np.where(rng.random(shape + (1,)) < 0.3, b & ~31, b)
def media(rng, *shape):
    m = rng.integers(0, M, shape + (16,)); same = rng.random(m.shape) < 0.15; same[..., 0] = False
    return np.where(same, np.concatenate([m[..., :1], m[..., :-1]], axis=-1), m)
def level(rng, t):
    return (t + (np.arange(16)[:, None] + rng.integers(0, 16, (N, 8, 1, W))) % 16) // 16
def paint(rng, share, own):
    return np.exp2(2 * (share * rng.random(own) + (1 - share) * rng.random((N, 8, 16, W))) - 1)
def parts(rng):
    lb, lm, pb, pm = begins(rng, N, 8, L), media(rng, N, 8, L), begins(rng, N, 8, P), media(rng, N, 8, P)
    sg = (rng.random((N, 8, 16, W)) * (rng.integers(1, 16, (N, 8, 1, W)) + 1)).astype(np.int64)
    co = paint(rng, 0.5, (N, 8, 16, 1)).reshape(N, 128, W).astype(np.float32).astype(BF)
    u = rng.random((N, 8, V, L)); om = np.where(rng.random(u.shape) < 0.5, np.exp2(12 + 9 * u), 1 + 2 ** 20 * u).astype(np.int64)
    return lb, lm, pb, pm, rng.integers(0, P, (N, 8, L)), sg, co, np.minimum(om, 2 ** 21)
def pack(lb, lm, pb, pm, fp, sg, co, om):
    ls, px = [np.ascontiguousarray((256 * b + m).transpose(0, 1, 3, 2).reshape(N, 128, -1)).astype(np.int32) for b, m in ((lb, lm), (pb, pm))]
    return {"sg": np.ascontiguousarray(sg.reshape(N, 128, W)).astype(np.float32).astype(BF), "co": co, "px": px, "ls": ls,
            "fp": np.stack([gtable(a) for a in fp]), "om": np.stack([gtable(a.reshape(8, -1)) for a in om])}
def plant(lb, lm, pb, pm, pn, sg, choose):
    tot = np.add.reduce(sg, axis=2); om = []
    for v in range(V):
        z, ln, a, b = cut(lb, lm, pick(pb, pn), pick(pm, pn)); ia, ib, den, w, cum = weigh(tot, z, ln, a, b)
        t = np.clip(choose(ln, w, cum), 1, 2 ** 21); om.append(t)
        lb, lm, pn = hand(*remake(z, ln, den, cum - w < t[..., None], pb, pm))
    return np.stack(om, axis=2)
def setup_inputs(rng):
    return pack(*parts(rng))
def setup_inputs_spread(rng):
    lb, lm, pb, pm, fp, sg, co, om = parts(rng)
    hi = np.minimum(np.exp2(2.1 + 2.1 * rng.random((N, 8, 1, W))).astype(np.int64) - 1, 15)
    sg = (rng.random((N, 8, 16, W)) * (hi + 1)).astype(np.int64) * (rng.random((N, 8, 1, W)) > 0.0625)
    co = paint(rng, 0.8, (N, 8, 1, W)).reshape(N, 128, W).astype(np.float32).astype(BF)
    u = rng.random((N, 8, V, L)); om = np.minimum(np.where(rng.random(u.shape) < 0.5, np.exp2(21 * u), 1 + 2 ** 21 * u).astype(np.int64), 2 ** 21)
    return pack(lb, lm, pb, pm, fp, sg, co, om)
def setup_inputs_ends(rng):
    lb, lm, pb, pm, fp, sg, co, om = parts(rng); i = np.arange(16)
    t = ((N - 1 - np.arange(N)[:, None] + 7 - np.arange(8)[None, :]) % 4)[:, :, None, None]
    sg = 15 * np.where(t == 0, 1, np.where(t == 1, rng.integers(0, 2, (N, 8, 1, W)), np.where(t == 2, rng.integers(0, 2, (N, 8, 16, W)), 0)))
    def some(n):
        first = i < rng.integers(1, 16, (N, 8, n, 1)); u = rng.random((N, 8, n, 1))
        b = np.where(u < 0.83, np.where(first, 0, 4095), begins(rng, N, 8, n))
        m = np.where(u < 0.66, np.where(first, 0, M - 1), np.where(u < 0.83, np.where(first, M - 1, 0), (M - 1) * rng.integers(0, 2, (N, 8, n, 16))))
        return b, m
    lb, lm = some(L); pb, pm = some(P); b0 = np.where(i < 15, 0, 4095); m0 = np.where(i < 15, 0, M - 1)
    lb[:, :, [0, 1, L - 2, L - 1]] = b0; lm[:, :, [0, 1, L - 2, L - 1]] = m0; pb[:, :, [0, P - 1]] = b0; pm[:, :, [0, P - 1]] = m0
    pb[:, :, [1, 2, P - 3, P - 2]] = begins(rng, N, 8, 4); pm[:, :, [1, 2, P - 3, P - 2]] = (M - 1) * rng.integers(0, 2, (N, 8, 4, 16))
    fp = (P - 1) * rng.integers(0, 2, (N, 8, L))
    whole = [2, 3, L - 4, L - 3]; pb[:, :, P - 1] = 0
    lb[:, :, whole] = 0; lm[:, :, whole] = m0; fp[:, :, whole] = P - 1
    om = np.where(rng.random(om.shape) < 0.7, np.where(rng.random(om.shape) < 0.4, 1, 2 ** 21), rng.choice(np.array([479, 480, 481, 480 * 4095, 480 * 4095 + 1, 480 * 4096 - 1, 480 * 4096, 480 * 4096 + 1]), om.shape))
    om[..., [0, L - 1]] = 480 * 4095 + 1; om[..., [1, L - 2]] = 480 * 4095
    om[:, :, 0, 2] = 480 * 4096; om[:, :, 0, L - 3] = 480 * 4096; om[:, :, 0, 3] = 2 ** 21; om[:, :, 0, L - 4] = 2 ** 21
    return pack(lb, lm, pb, pm, fp, sg, co, om)
def setup_inputs_corners(rng):
    lb, lm, pb, pm, fp, sg, co, om = parts(rng); i = np.arange(16)
    kind = (np.arange(N)[:, None] + np.arange(8)[None, :]) % 4; k4 = kind[:, :, None, None]
    sg = np.where(k4 == 0, level(rng, np.arange(W) // D * 240 // (M - 1)), np.where(k4 == 2, level(rng, rng.integers(1, 240, (N, 8, 1, 1))), sg))
    runs = rng.choice(np.array([1, 2, 3, 15, 16, 16, 17, 31]), (N, 8, L, 1)); own = rng.integers(np.maximum(1, runs - 15), np.minimum(16, runs) + 1)
    steps = 120 * i + rng.integers(0, 100, (N, 8, L, 16)); steps[..., 0] = 0
    lb = np.where(k4 == 0, steps, lb); lm = np.where(k4 == 0, rng.integers(2, M // 4, (N, 8, L, 1)) + 4 * (np.minimum(i, own - 1) % 2), lm)
    kk = np.arange(16)[:, None]; late = i >= 16 - kk
    pb[:, :, P - 16:] = np.where(k4 == 0, np.where(late, 2100 + 120 * (i - 16 + kk) + rng.integers(0, 100, (N, 8, 16, 16)), 0), pb[:, :, P - 16:])
    pm[:, :, P - 16:] = np.where(k4 == 0, np.where(late, M // 2 + 4 + 4 * (i % 2), 0), pm[:, :, P - 16:])
    one = np.repeat(fp[:, :, :1], L, axis=2); one[:, :, L - 1] = (one[:, :, L - 1] + 1) % P
    fp = np.where(kind[:, :, None] == 0, P - 16 + (runs - own)[..., 0], np.where(kind[:, :, None] == 1, one, fp))
    sel = rng.integers(0, 4, (N, 8, L, 1)); at = np.where(sel == 0, 0, np.where(sel == 1, 4095, rng.integers(1, 4096, (N, 8, L, 1))))
    lb = np.where((k4 == 1) & (sel < 3), np.where(i == 0, 0, at), lb)
    lb = np.where(k4 == 3, pick(pb, fp), lb)
    om = np.where((k4 == 1) & (rng.random(om.shape) < 0.5), 1, om)
    om[:, :, 0] = np.where((kind[:, :, None] == 0) & (rng.random((N, 8, L)) < 0.75), 2 ** 21, om[:, :, 0])
    return pack(lb, lm, pb, pm, fp, sg, co, om)
def setup_inputs_ties(rng):
    lb, lm, pb, pm, fp, sg, co, om = parts(rng); lb = lb & ~255; pb = np.where(rng.random((N, 8, P, 1)) < 0.8, pb & ~255, pb)
    sg = level(rng, rng.choice(np.array([40, 41, 120, 239, 240]), (N, 8, 1, W)))
    def choose(ln, w, cum):
        e = rng.integers(0, 32, (N, 8, L, 1)); return (np.take_along_axis(cum, e, -1) + rng.integers(0, 2, e.shape))[..., 0]
    return pack(lb, lm, pb, pm, fp, sg, co, plant(lb, lm, pb, pm, fp, sg, choose))
def setup_inputs_calm(rng):
    lb, lm, pb, pm, fp, sg, co, om = parts(rng); low = np.where(np.arange(8) % 2 == 0, 0, M - 2)[None, :, None, None]
    sg = rng.integers(4, 16, (N, 8, 16, W))
    def near(n):
        u = rng.integers(0, 3, (N, 8, n, 1)); x = np.sort(rng.integers(0, 26, (N, 8, n, 16)), axis=-1)
        b = np.where(u == 0, x, np.where(u == 1, 4070 + x, begins(rng, N, 8, n))); b[..., 0] = 0
        return b, low + rng.integers(0, 2, (N, 8, n, 16))
    lb, lm = near(L); pb, pm = near(P); fp = rng.choice(np.array([0, 1, 2, 3, P - 2, P - 1]), (N, 8, L))
    def choose(ln, w, cum):
        o = np.argsort(ln == 0, axis=-1, kind="stable"); n = np.add.reduce((ln > 0).astype(np.int64), axis=-1, keepdims=True)
        k = rng.integers(0, 6, n.shape); k = np.maximum(np.where(k < 4, np.minimum(k, n - 1), n - 1 - (k - 4)), 0)
        e = np.take_along_axis(o, k, -1); hit = np.take_along_axis(cum, e, -1)
        return np.where(rng.random(n.shape) < 0.5, hit, hit - np.take_along_axis(w, e, -1) + 1)[..., 0]
    return pack(lb, lm, pb, pm, fp, sg, co, plant(lb, lm, pb, pm, fp, sg, choose))
def check_ranges(d):
    bad = []; s = d["sg"].astype(np.float32); c = d["co"].astype(np.float32)
    if not np.all((s >= 0) & (s <= 15) & (s == np.floor(s))): bad.append("range of sg")
    if not np.all((c >= 0.5) & (c <= 2)): bad.append("range of co")
    for k, lo, hi in (("px", 0, 4095 * 256 + M - 1), ("ls", 0, 4095 * 256 + M - 1), ("fp", 0, P - 1), ("om", 1, 2 ** 21)):
        if np.min(d[k]) < lo or np.max(d[k]) > hi: bad.append("range of " + k)
    for k in ("px", "ls"):
        b, m = unpack(d[k])
        if np.max(m) >= M: bad.append("media of " + k)
        if np.any(b[..., 0] != 0) or np.any(b[..., 1:] < b[..., :-1]): bad.append("begins of " + k)
    return bad
def reference(sg, co, px, ls, fp, om):
    s = sg.astype(np.float64).reshape(N, 8, 16, W); c = co.astype(np.float64).reshape(N, 8, 16, W); tot = np.add.reduce(s, axis=2).astype(np.int64)
    pb, pm = unpack(px); lb, lm = unpack(ls); pn = np.stack([gentries(a) for a in fp]).astype(np.int64)
    bound = np.stack([gentries(a) for a in om]).astype(np.int64).reshape(N, 8, V, L)
    yc = np.zeros((N, 8, 16, V, L), np.float32); yt = np.zeros((N, 8, 16, V, L), np.float32)
    for v in range(V):
        z, ln, a, b = cut(lb, lm, pick(pb, pn), pick(pm, pn)); ia, ib, den, w, cum = weigh(tot, z, ln, a, b)
        vis = cum - w < bound[:, :, v, :, None]; seen = np.where(vis, ln, 0)
        for q in range(N):
            for g in range(8):
                ja, jb = ia[q, g].reshape(-1), ib[q, g].reshape(-1)
                tau = ((np.take(s[q, g], ja, 1) + np.take(s[q, g], jb, 1)) * seen[q, g].reshape(-1) * 2.0 ** -14).reshape(16, L, 32)
                al = tau * 0.125; tr = np.ones_like(al); tr[..., 1:] = np.multiply.accumulate(1.0 - al, axis=-1)[..., :-1]
                cc = (np.take(c[q, g], ja, 1) + np.take(c[q, g], jb, 1)).reshape(16, L, 32)
                yc[q, g, :, v] = np.add.reduce(tr * al * cc, axis=-1); yt[q, g, :, v] = np.add.reduce(tau, axis=-1)
        if v < V - 1: lb, lm, pn = hand(*remake(z, ln, den, vis, pb, pm))
    return {"yc": yc.reshape(N, 128, V * L), "yt": yt.reshape(N, 128, V * L)}

def check_inputs(d):
    bad = list(check_ranges(d))
    if not bad:
        for name, y in reference(**d).items():
            for q in range(N):
                v = np.abs(np.asarray(y[q], np.float64)); s = np.sqrt(np.mean(v * v))
                if v.max() > 7 * s or s < 2.0 ** -3: bad.append('%s of rank %d is uneven or too small' % (name, q))
    return bad

@@ -1,0 +1,565 @@
+from concourse.bass import DstId, RemoteDMATransfer
+from concourse.mybir import dt, AluOpType, AxisListType, ActivationFunctionType
+
+ALU = AluOpType
+ACT = ActivationFunctionType
+NV = 5
+FILL = 4095 * 4096 + 15 * 128
+VADD = (0, 0, 0, 0, 1)
+VSHARE = (8, 6, 6, 6, 6)
+YT_PE = (1, 1, 1, 1, 0)
+
+F32, BF, I32, U16, F16 = "float32", "bfloat16", "int32", "uint16", "float16"
+SCRATCH = {}
+
+
+def _sb(name, shape, d):
+    SCRATCH[name] = ("sbuf", [128] + list(shape), d)
+
+
+for _n, _s, _d in [
+    ("SG", [4112], BF), ("CO", [4112], BF), ("PXI", [1024], I32), ("PK", [1024], F32),
+    ("PXM", [1024], I32), ("MI", [1024], F32),
+    ("RAW", [256], I32), ("RM", [256], I32), ("RK", [256], F32),
+    ("FPI", [8], I32), ("FPU", [8], U16), ("OMI", [40], I32), ("OMB", [640], F32),
+    ("ONE", [128], F32), ("IDF", [128], F32), ("PERM", [128], F32), ("IH", [128], F16), ("IH32", [128], F16),
+    ("IB", [128], BF), ("NIB", [128], BF), ("CSEL", [2048], BF), ("SEL", [2048], BF),
+    ("PI", [8], I32), ("PJ", [8], I32), ("PCOL", [8], F32), ("IO8", [8], F32), ("IO144", [144], F32), ("MK", [144], F32),
+    ("BLK", [8], F32), ("BLKB", [8], F32), ("RMA", [16], BF), ("RMB", [16], BF), ("RMA2", [16], BF),
+    ("CZ", [512], BF), ("CY", [128], BF), ("MASK", [1024], F32), ("POSI", [128], F32), ("POSC", [128], BF),
+    ("LI", [64], I32), ("LU", [64], U16),
+    ("L0", [8, 16], F32), ("PG", [128], F32), ("M0", [8, 32], F32), ("M1", [8, 32], F32), ("K", [8, 32], I32),
+    ("ZK", [8, 33], I32), ("YI", [256], I32), ("YF", [256], F16), ("D0", [256], F16),
+    ("A16", [256], F16), ("B16", [256], F16), ("SLAB", [8, 32], F16), ("IDX0", [512], U16), ("IDX1", [512], U16),
+    ("LEN", [256], F32), ("LB", [256], F32), ("W", [256], F32), ("TT", [256], F32), ("OA", [4096], F32),
+    ("XI", [256], I32), ("DEN", [256], I32), ("LE", [256], F32), ("G", [256], F32),
+    ("GI", [8], I32), ("NA", [8], I32), ("NB", [8], I32), ("NB8", [8], F32), ("NM", [8], F32), ("NX", [144], F32),
+    ("DF", [256], I32), ("LOW", [256], I32), ("EQ", [256], F32), ("T2", [256], F32), ("VV", [8, 32], I32),
+    ("MB", [8, 32], I32), ("C8", [8], F32), ("XS", [128], I32), ("UJ", [128], BF), ("XM", [128], F32),
+    ("PG2", [128], F32), ("Y2", [128], F32), ("U2", [128], F32), ("V2", [128], F32),
+    ("Q0", [8, 16], F32), ("Q1", [8, 16], F32),
+    ("SL", [256], F32), ("HI", [256], BF), ("LO", [256], BF),
+    ("SA0", [4096], BF), ("SB0", [4096], BF), ("SA1", [4096], BF), ("SB1", [4096], BF),
+    ("CA0", [4112], BF), ("CB0", [4112], BF), ("CA1", [4112], BF), ("CB1", [4112], BF),
+    ("AB", [4096], F32), ("WO", [4096], F32), ("WT", [4096], F32), ("YC", [640], F32), ("YT", [640], F32),
+    ("RN", [32], U16), ("NU", [64], U16),
+]:
+    _sb(_n, _s, _d)
+for _v in range(NV - 1):
+    _sb("OUT%d" % _v, [8, 16], F32)
+    _sb("RL%d" % _v, [8, 16], F32)
+for _n in ("pS", "pT"):
+    SCRATCH[_n] = ("psum", [128, 16, 32], F32)
+for _n in ("pI", "pL0", "pL1", "pV", "pC0", "pC1"):
+    SCRATCH[_n] = ("psum", [128, 512], F32)
+
+SEMAPHORES = (["cV", "cS", "cP", "cG", "dls", "dfp", "dpx", "dom", "dsg", "dco", "dst", "sent"]
+              + ["add%d" % v for v in range(NV)] + ["rn%d" % v for v in range(NV - 1)] + ["rl%d" % v for v in range(NV - 1)])
+
+CYC = 1.0
+PCYC = 0.52
+GA = 1.55
+HOP = 80.0
+
+
+def sweep(ops, pred, succ, prio, ahead, back):
+    n = len(ops)
+    left = [len(p) for p in pred]
+    ready = [0.0] * n
+    start = [0.0] * n
+    avail, free = {}, {}
+    for i, o in enumerate(ops):
+        avail.setdefault(o["q"], [])
+        free[o["q"]] = 0.0
+        if back:
+            ready[i] = o["lat"] - o["busy"]
+        if left[i] == 0:
+            avail[o["q"]].append(i)
+    order = []
+    while len(order) < n:
+        best = None
+        for q, lst in avail.items():
+            if not lst:
+                continue
+            t0 = max(free[q], min(ready[i] for i in lst))
+            c = max((i for i in lst if ready[i] <= t0 + ahead), key=lambda i: (prio[i], -i))
+            st = max(free[q], ready[c])
+            if best is None or st < best[0]:
+                best = (st, q, c)
+        st, q, c = best
+        avail[q].remove(c)
+        free[q] = st + ops[c]["busy"]
+        start[c] = st
+        order.append(c)
+        for s in succ[c]:
+            if back:
+                t = st + ops[c]["busy"] + HOP + ops[s]["lat"] - ops[s]["busy"]
+            else:
+                t = st + ops[c]["lat"] + HOP
+            ready[s] = max(ready[s], t)
+            left[s] -= 1
+            if left[s] == 0:
+                avail[ops[s]["q"]].append(s)
+    return order, start
+
+
+PLANS = {}
+FIFO = False
+ROUNDS = 40
+CLIMB = 1200
+NOISE = 1000.0
+AHEAD = 160.0
+
+
+def plan(ops):
+    n = len(ops)
+    key = tuple((o["q"], o["busy"], tuple(o["deps"])) for o in ops)
+    if key not in PLANS:
+        pred = [o["deps"] for o in ops]
+        succ = [[] for _ in range(n)]
+        for i, o in enumerate(ops):
+            for d in o["deps"]:
+                succ[d].append(i)
+        prio = [0.0] * n
+        for i in range(n - 1, -1, -1):
+            prio[i] = ops[i]["lat"] + HOP + max([prio[s] for s in succ[i]] + [0.0])
+        if FIFO:
+            lead = [False] * n
+            lead[max(i for i in range(n) if ops[i]["name"] == "['TT']")] = True
+            for i in range(n - 1, -1, -1):
+                if lead[i]:
+                    for d in ops[i]["raw"]:
+                        lead[d] = True
+            prio = [1e9 + prio[i] if lead[i] else -float(i) for i in range(n)]
+        best = None
+        x = 12345
+        for r in range(ROUNDS):
+            order, start = sweep(ops, pred, succ, prio, AHEAD, False)
+            end = max(start[i] + ops[i]["lat"] for i in range(n))
+            if best is None or end < best[0]:
+                best = (end, order, start)
+            if r % 4 == 3:
+                start = best[2]
+            amp = (0.0, NOISE, 0.0, 4.0 * NOISE)[r % 4]
+            back = []
+            for i in range(n):
+                x = (x * 1103515245 + 12345) % 2147483648
+                back.append(start[i] + ops[i]["busy"] + amp * x / 2147483648)
+            _o, st = sweep(ops, succ, pred, back, AHEAD, True)
+            prio = [st[i] + ops[i]["busy"] for i in range(n)]
+        for r in range(CLIMB):
+            x = (x * 1103515245 + 12345) % 2147483648
+            a = (x >> 8) % n
+            x = (x * 1103515245 + 12345) % 2147483648
+            w = 1 + (x >> 8) % 24
+            x = (x * 1103515245 + 12345) % 2147483648
+            d = ((x >> 8) % 2001 - 1000) * (1.0, 4.0, 12.0)[r % 3]
+            prio = [-t for t in best[2]]
+            for i in range(a, min(n, a + w)):
+                if ops[i]["q"] == ops[a]["q"] or r % 2:
+                    prio[i] += d
+            order, start = sweep(ops, pred, succ, prio, AHEAD, False)
+            end = max(start[i] + ops[i]["lat"] for i in range(n))
+            if end <= best[0]:
+                best = (end, order, start)
+        PLANS[key] = best
+    for i, o in enumerate(ops):
+        o["t"] = PLANS[key][2][i]
+    return PLANS[key][1]
+
+
+def build(g, core, T, topo):
+    rank = T.rank_of(core)
+    nxt = T.cores[(rank + 1) % len(T.cores)]
+    prv = T.cores[(rank - 1) % len(T.cores)]
+    rid, pid, _ = topo.addr(nxt)
+    omask, n_out, n_in = topo.mask(core, nxt), len(topo.engines(core, nxt)), len(topo.engines(prv, core))
+    V, S, P, Y = g.vector, g.scalar, g.tensor, g.sync
+    ops = []
+    lastw, readers, bankers = {}, {}, {}
+
+    def op(q, fn, busy, r=(), w=(), bank=None, lat=None, sem=None, inc=1, name=""):
+        i = len(ops)
+        deps = set()
+        for k in r:
+            if k in lastw:
+                deps.add(lastw[k])
+        raw = sorted(deps)
+        if q == "P":
+            raw += [lastw[k] for k in w if k in lastw and ops[lastw[k]]["q"] == "P"]
+        for k in w:
+            if k in lastw:
+                deps.add(lastw[k])
+            deps.update(readers.get(k, ()))
+        for k in r:
+            readers.setdefault(k, []).append(i)
+        for k in w:
+            lastw[k] = i
+            readers[k] = []
+        for bank1 in sorted(set([] if bank is None else bank if isinstance(bank, list) else [bank])):
+            b = bankers.setdefault(bank1, [None, [], []])
+            if b[0] != q:
+                b[:] = [q, [], b[1]]
+            deps.update(b[2])
+            if q == "P":
+                deps.update(b[1])
+            b[1].append(i)
+        deps.discard(i)
+        ops.append({"q": q, "fn": fn, "busy": busy, "lat": busy if lat is None else lat, "deps": sorted(deps), "raw": raw,
+                    "sem": sem or "c" + q, "inc": inc, "name": name})
+        return i
+
+    def vc(n):
+        return 50.0 + max(n, 32) * CYC
+
+    def ts(out, in0, s1, s2, o0, o1, n, r, w, bank=None):
+        if o1 is None:
+            return op("V", lambda: V.tensor_scalar(out, in0, s1, None, o0), vc(n), r, w, bank, name=str(w))
+        return op("V", lambda: V.tensor_scalar(out, in0, s1, s2, o0, o1), vc(n), r, w, bank, name=str(w))
+
+    def tt(out, a, b, o, n, r, w, bank=None):
+        return op("V", lambda: V.tensor_tensor(out, a, b, o), vc(n), r, w, bank, name=str(w))
+
+    def cp(out, a, n, r, w, bank=None):
+        return op("V", lambda: V.tensor_copy(out, a), vc(n), r, w, bank, name=str(w))
+
+    def ms(ap, c, n, w):
+        return op("V", lambda: V.memset(ap, c), vc(n), (), w, name=str(w))
+
+    def scan(out, d0, d1, init, o0, o1, n, r, w, bank=None):
+        return op("V", lambda: V.tensor_tensor_scan(out, d0, d1, init, o0, o1), vc(n), r, w, bank, name=str(w))
+
+    def act(out, a, n, r, w, bank=None, func=ACT.Identity, scale=1.0, bias=0.0):
+        return op("S", lambda: S.activation(out, a, func, bias=bias, scale=scale), 65.0 + max(n, 32) * CYC, r, w, bank, name=str(w))
+
+    def mm(items, cyc, r, w, bank):
+        def fn():
+            for it in items:
+                ins = P.matmul(*it)
+            return ins
+        return op("P", fn, 30.0 + cyc * PCYC, r, w, bank, lat=100.0 + cyc * PCYC, name=str(w))
+
+    def dma(q, eng, out, a, nbytes, r, w, sem, **kw):
+        return op(q, lambda: eng.dma_start(out, a, **kw), 1000.0 if q == "G" else 60.0, r, w, lat=2000.0 + nbytes / 150.0, sem=sem, inc=16, name=str(w))
+
+    def iota(out, pat, base, cm, n, w, small):
+        if small:
+            return op("G", lambda: g.iota(out, pat, base, cm, allow_small_or_imprecise_dtypes=True), 130.0 + 2 * n * CYC, (), w)
+        return op("G", lambda: g.iota(out, pat, base, cm), 130.0 + 2 * n * CYC, (), w)
+
+    def asel(out, a, pat, base, n, r, w):
+        return op("G", lambda: g.affine_select(out, a, pat, ALU.is_equal, 0.0, base, 1), 170.0 + 2 * n * CYC, r, w)
+
+    def send(src, dst, nbytes, r, w, sem):
+        op("G", lambda: g.remote_dma(dst, src, T.sem[sem], T.sem.sent, pid, rid, omask), 300.0, r, [("sent", sem)],
+           lat=3000.0 + nbytes / 40.0, sem="*")
+        op("R", None, 0.0, [("sent", sem)], w, sem=sem, inc=n_in)
+
+    dma("Y", Y, T.RAW[:, 0:128], T.ls[:], 65536, (), ["RAW0"], "dls")
+    dma("S", S, T.FPI[:], T.fp[:], 4096, (), ["FPI"], "dfp")
+    dma("Y", Y, T.PXI[:], T.px[:], 524288 + 65536, (), ["PXI"], "dpx")
+    dma("S", S, T.OMI[:], T.om[:], 20480, (), ["OMI"], "dom")
+    dma("Y", Y, T.SG[:, 0:4096], T.sg[:], 1638400, (), ["SG"], "dsg")
+    dma("Y", Y, T.CO[:, 0:4096], T.co[:], 2686976, (), ["CO"], "dco")
+
+    ms(T.ONE[:], 1.0, 128, ["ONE"])
+    iota(T.PI[:, 0:1], [[0, 1]], 0, 1, 1, ["PI"], False)
+    asel(T.PERM[:], T.ONE[:], [[-16, 8], [1, 16]], -15, 128, ["ONE"], ["PERM"])
+    asel(T.IDF[:], T.ONE[:], [[-1, 128]], 0, 128, ["ONE"], ["IDF"])
+    iota(T.LI[:, 0:40], [[1, 40]], 0, 0, 40, ["LI0"], False)
+    iota(T.LI[:, 40:48], [[32, 8]], 31, 0, 8, ["LI1"], False)
+    iota(T.LI[:, 48:64], [[1, 16]], -1, 0, 16, ["LI2"], False)
+    iota(T.IO8[:], [[1, 8]], 0, 0, 8, ["IO8"], True)
+    iota(T.IO144[:], [[0, 9], [1, 16]], 0, 0, 144, ["IO144"], True)
+    iota(T.POSI[:], [[0, 8], [128, 16]], -3904, 0, 128, ["POSI"], True)
+    iota(T.CZ[:], [[-2304, 2], [0, 256]], 0, 0, 512, ["CZ"], True)
+    iota(T.CY[:], [[0, 128]], -2176, 0, 128, ["CY"], True)
+    iota(T.MI[:], [[0, 32], [1, 32]], 0, 0, 1024, ["MI"], True)
+    act(T.MASK[:], T.MI[:], 1024, ["MI"], ["MASK"], func=ACT.Sign)
+    iota(T.CSEL[:], [[0, 2048]], 1, 0, 2048, ["CSEL"], True)
+    asel(T.SEL[:], T.CSEL[:], [[-1, 16], [-16, 8], [0, 16]], 0, 2048, ["CSEL"], ["SEL"])
+    ts(T.PJ[:, 0:1], T.PI[:, 0:1], 15, None, ALU.bitwise_and, None, 1, ["PI"], ["PJ0"])
+    ts(T.PJ[:, 1:2], T.PI[:, 0:1], 4, None, ALU.arith_shift_right, None, 1, ["PI"], ["PJ1"])
+    cp(T.PCOL[:, 0:2], T.PJ[:, 0:2], 2, ["PJ0", "PJ1"], ["PC0"])
+    ts(T.PCOL[:, 2:3], T.PJ[:, 0:1], 128.0, None, ALU.mult, None, 1, ["PJ0"], ["PC2"])
+    ts(T.PCOL[:, 3:4], T.PJ[:, 0:1], 128.0, 2048.0, ALU.mult, ALU.add, 1, ["PJ0"], ["PC3"])
+    cp(T.LU[:], T.LI[:], 64, ["LI0", "LI1", "LI2"], ["LU"])
+    ms(T.LU[:, 48:49], 7, 1, ["LU"])
+    cp(T.FPU[:], T.FPI[:], 8, ["FPI"], ["FPU"])
+    ts(T.MK[:], T.IO144[:], T.PCOL[:, 0:1], None, ALU.is_equal, None, 144, ["IO144", "PC0"], ["MK"])
+    ts(T.BLK[:], T.IO8[:], T.PCOL[:, 1:2], None, ALU.is_equal, None, 8, ["IO8", "PC0"], ["BLK"])
+    for buf, key, c0, c1 in ((T.RMA, "RMA", -4096.0, -512.0), (T.RMB, "RMB", -4096.0, 512.0), (T.RMA2, "RMA2", 0.0, -1024.0)):
+        act(buf[:, 0:8], T.BLK[:], 8, ["BLK"], [key + "a"], scale=c0)
+        act(buf[:, 8:16], T.BLK[:], 8, ["BLK"], [key + "b"], scale=c1)
+    act(T.BLKB[:], T.BLK[:], 8, ["BLK"], ["BLKB"], scale=2.0 ** 36)
+    ts(T.IH[:], T.IDF[:], 1.0, None, ALU.mult, None, 128, ["IDF"], ["IH"])
+    ts(T.IH32[:], T.IDF[:], 32.0, None, ALU.mult, None, 128, ["IDF"], ["IH32"])
+    act(T.IB[:], T.IDF[:], 128, ["IDF"], ["IB"])
+    act(T.NIB[:], T.IDF[:], 128, ["IDF"], ["NIB"], scale=-1.0)
+    act(T.POSC[:], T.POSI[:], 128, ["POSI"], ["POSC"], scale=2.0 ** 18)
+    ms(T.SG[:, 4096:4112], 0.5, 16, ["SGz"])
+    ms(T.CO[:, 4096:4112], 0.0, 16, ["COz"])
+    for b in ("CA0", "CB0", "CA1", "CB1"):
+        act(T[b][:, 4096:4104], T.IO8[:], 8, ["IO8"], [b + "z"], scale=0.0)
+    ms(T.ZK[:, :, 32], 16777216, 8, ["ZKe"])
+    ts(T.SLAB[:, :, 0], T.IO8[:], 0.0, 5196.0, ALU.mult, ALU.add, 8, ["IO8"], ["SLAB0"])
+    ms(T.TT[:, 0:1], 0.0, 1, ["TT0"])
+    ms(T.DF[:, 0:1], 0, 1, ["DF0"])
+
+    cp(T.RAW[:, 128:256], T.PXI[:].indirect(T.FPU[:]), 128 * GA, ["PXI", "FPU"], ["RAW1"])
+    for h in range(2):
+        c = slice(128 * h, 128 * h + 128)
+        ts(T.RM[:, c], T.RAW[:, c], 0xFFF00, None, ALU.bitwise_and, None, 128, ["RAW%d" % h], ["RM%d" % h])
+        ts(T.pV[:, c], T.RM[:, c], 15.0, T.PCOL[:, 2 + h:3 + h], ALU.mult, ALU.add, 128, ["RM%d" % h, "PC2", "PC3"], ["pVa"], "pV")
+        tt(T.RK[:, c], T.RAW[:, c], T.pV[:, c], ALU.add, 128, ["RAW%d" % h, "pVa"], ["RK%d" % h], "pV")
+    mm([(T.pS[:, 4:8, :], T.RK[:, 0:128], T.IDF[:], True, True)], 512, ["RK0", "IDF"], ["pS"], "pS")
+    act(T.L0[:], T.pS[:, 4:8, :], 128, ["pS"], ["L0"], "pS")
+    for v in range(NV):
+        tt(T.OMB[:, 128 * v:128 * v + 128], T.OMI[:].indirect(T.LU[:, 8 * v:8 * v + 8]), T.MK[:, 0:128], ALU.mult, 256,
+           ["OMI", "LU", "MK"], [("OMB", v)])
+    for c4 in range(4):
+        c = slice(256 * c4, 256 * c4 + 256)
+        bk = "pC%d" % (c4 % 2)
+        ts(T.PXM[:, c], T.PXI[:, c], 0xFFF00, None, ALU.bitwise_and, None, 256, ["PXI"], [("PXM", c4)])
+        ts(T[bk][:, 0:256], T.PXM[:, c], 15.0, T.PCOL[:, 3:4], ALU.mult, ALU.add, 256, [("PXM", c4), "PC3"], [bk], bk)
+        tt(T.PK[:, c], T.PXI[:, c], T[bk][:, 0:256], ALU.add, 256, ["PXI", bk], [("PK", c4)], bk)
+    PKK = [("PK", c4) for c4 in range(4)]
+    PTA = [("pTa", a, x) for a in range(2) for x in range(2)]
+
+    def stage(dst, dk, src, sk, half, lo, hi):
+        tt(dst[:, :, 0:2 * half:2], src[:, :, 0:half], src[:, :, half:2 * half], lo, 16 * half, [sk + "a", sk + "b"], [dk + "a"])
+        tt(dst[:, :, 1:2 * half:2], src[:, :, 0:half], src[:, :, half:2 * half], hi, 16 * half, [sk + "a", sk + "b"], [dk + "b"])
+
+    for v in range(NV):
+        e = v % 2
+        IDX, SA, SB, CA, CB = T["IDX%d" % e], T["SA%d" % e], T["SB%d" % e], T["CA%d" % e], T["CB%d" % e]
+        if v == 0:
+            lane, lk, pg, pk = T.L0, "L0", T.RK[:, 128:256], "RK1"
+        else:
+            lane, lk, pg, pk = T["RL%d" % (v - 1)], ("RL", v - 1), T.PG[:], "PG"
+            act(T.PG[:], T.PK[:].indirect(T.RN[:, 8 * v - 8:8 * v]), 128 * GA, PKK + [("RN", v - 1)], ["PG"])
+        mm([(T.pS[:, 8:16, 0:16], pg, T.PERM[:], True, True)], 512, [pk, "PERM"], ["pS"], "pS")
+        for k in range(4):
+            a, b = k % 2, 16 * (k % 2)
+            for hf in range(2):
+                for x, o in enumerate((ALU.min, ALU.max)):
+                    if k == 0:
+                        i0, i1, rk, bk = lane[:, :, 8 * hf:8 * hf + 8], T.pS[:, 8:16, 8 * hf:8 * hf + 8], [lk, "pS"], ["pS"]
+                    else:
+                        i0, i1 = T.M0[:, :, 16 - b + 8 * hf:24 - b + 8 * hf], T.pT[:, 0:8, 16 - b + 8 * hf:24 - b + 8 * hf]
+                        rk, bk = [("M", 1 - a, y) for y in range(2)] + [("pTa", 1 - a, y) for y in range(2)], ["pT"]
+                    if hf == 0:
+                        tt(T.pT[:, 0:8, b + x:b + 16:2], i0, i1, o, 64, rk, [("pTa", a, x)], bk + ["pT"])
+                    else:
+                        tt(T.M0[:, :, b + x:b + 16:2], i0, i1, o, 64, rk, [("M", a, x)], bk)
+        for x, o in enumerate((ALU.min, ALU.max)):
+            tt(T.K[:, :, x:32:2], T.M0[:, :, 16:32], T.pT[:, 0:8, 16:32], o, 128,
+               [("M", 1, y) for y in range(2)] + [("pTa", 1, y) for y in range(2)], ["K" + "ab"[x]], "pT")
+        KK = ["Ka", "Kb"]
+        ts(T.YI[:], T.K[:], 2175, None, ALU.bitwise_and, None, 256, KK, ["YI"])
+        ts(T.ZK[:, :, 0:32], T.K[:], 0xFFF000, None, ALU.bitwise_and, None, 256, KK, ["ZK"])
+        ts(T.YF[:], T.YI[:], -1920.0, None, ALU.add, None, 256, ["YI"], ["YF"])
+        ts(T.SLAB[:, :, 1:32], T.ZK[:, :, 1:32], 2.0 ** -19, 1099.50390625, ALU.mult, ALU.add, 248, ["ZK"], ["SLAB"])
+        ts(T.D0[:], T.YF[:], 0.0, 4096.0, ALU.is_lt, ALU.mult, 128, ["YF"], ["D0"])
+        scan(T.A16[:], T.D0[:], T.YF[:], 0.0, ALU.add, ALU.min, 128, ["D0", "YF"], ["A16"])
+        scan(T.B16[:], T.D0[:], T.YF[:], 128.0, ALU.min, ALU.max, 128, ["D0", "YF"], ["B16"])
+        for x, (src, sk, add) in enumerate(((T.A16, "A16", 61440.0 - 1100.0), (T.B16, "B16", -4096.0 - 1100.0))):
+            its = []
+            for h in range(2):
+                o = T.pI[:, 256 * x + 128 * h:256 * x + 128 * h + 128]
+                its.append((o, src[:, h:256:2], T.IH32[:], True, False))
+                its.append((o, T.SLAB[:, :, h:32:2], T.IH[:], False, True))
+            mm(its, 512, [sk, "SLAB", "SLAB0", "IH", "IH32"], [("pI", x)], "pI")
+        for x, add in enumerate((61440.0 - 1100.0, -4096.0 - 1100.0)):
+            ts(IDX[:, 256 * x:256 * x + 256], T.pI[:, 256 * x:256 * x + 256], add, 4096.0, ALU.add, ALU.min, 256,
+               [("pI", x)], [("IDX", e, x)], "pI")
+        tt(T.LEN[:], T.ZK[:, :, 1:33], T.ZK[:, :, 0:32], ALU.subtract, 512, ["ZK", "ZKe"], ["LEN"])
+        act(T.LB[:], T.LEN[:], 256, ["LEN"], ["LB"], scale=4096.0)
+        act(T.LB[:, 0:256:32], T.ONE[:, 0:8], 8, ["ONE"], ["LB"])
+        NC = 8
+        cw, kw = 4096 // NC, 256 // NC
+        for c in range(NC):
+            act(SA[:, cw * c:cw * c + cw], T.SG[:].indirect(IDX[:, kw * c:kw * c + kw]), cw * GA,
+                ["SG", "SGz", ("IDX", e, 0)], [("SA", e, c)])
+        for c in range(NC):
+            src, dst = T.SG[:].indirect(IDX[:, 256 + kw * c:256 + kw * c + kw]), SB[:, cw * c:cw * c + cw]
+            if VADD[v]:
+                tt(dst, src, SA[:, cw * c:cw * c + cw], ALU.add, cw * 2, ["SG", "SGz", ("IDX", e, 1), ("SA", e, c)], [("SB", e, c)])
+            elif c < VSHARE[v]:
+                cp(dst, src, cw * GA, ["SG", "SGz", ("IDX", e, 1)], [("SB", e, c)])
+            else:
+                act(dst, src, cw * GA, ["SG", "SGz", ("IDX", e, 1)], [("SB", e, c)])
+        SAK, SBK = [("SA", e, c) for c in range(NC)], [("SB", e, c) for c in range(NC)]
+        mm([(T.pS[:], T.IB[:], T.CZ[:], True, False), (T.pS[:, 8:16, :], T.IH[:], T.B16[:], False, False),
+            (T.pS[:, 0:8, 0], T.OMB[:, 128 * v:128 * v + 128], T.BLKB[:], False, False)], 1024,
+           ["IB", "IH", "CZ", "B16", ("OMB", v), "BLKB"], ["pS"], "pS")
+        ra, rak = (T.RMA2, "RMA2") if VADD[v] else (T.RMA, "RMA")
+        for src, keys, rm, rk, x in ((SA, SAK, ra, rak, 0), (SB, SBK, T.RMB, "RMB", 1)):
+            for h in range(2):
+                mm([(T.pS[:, :, 2 * j + h], src[:, 2048 * h + j:2048 * h + 2048:16], rm[:], False, x + h == 2 and j == 15)
+                    for j in range(1 - h, 16)], 16 * 64, keys[NC // 2 * h:NC // 2 * (h + 1)] + [rk + "a", rk + "b"], ["pS"], "pS")
+        if not VADD[v]:
+            dma("G", g, SB[:], SA[:], 2 * 1048576, SAK, SBK, "add%d" % v, accum_op=ALU.add, max_dma_last_dim=4096)
+        tt(T.W[:], T.LB[:], T.pS[:, 0:8, :], ALU.mult, 256, ["LB", "pS"], ["W"], "pS")
+        if v < NV - 1:
+            tt(T.XI[:], T.A16[:], T.pS[:, 8:16, :], ALU.max, 256, ["A16", "pS"], ["XI"], "pS")
+        scan(T.pV[:, 0:256], T.MASK[:, 0:256], T.W[:], 0.0, ALU.mult, ALU.add, 256, ["MASK", "W"], ["pVa"], "pV")
+        if v < NV - 1:
+            ts(T.DEN[:], T.XI[:], 255, None, ALU.bitwise_and, None, 256, ["XI"], ["DEN"])
+        tt(T.TT[:, 1:256], T.LB[:, 1:256], T.pV[:, 0:255], ALU.min, 256, ["LB", "pVa"], ["TT"], "pV")
+        act(T.SL[:], T.TT[:], 256, ["TT", "TT0"], ["SL"], func=ACT.Relu, scale=2.0 ** -41)
+        act(T.SL[:, 0:256:32], T.ONE[:, 0:8], 8, ["ONE"], ["SL"])
+        if v < NV - 1:
+            tt(T.pV[:, 256:512], T.DEN[:], T.ZK[:, :, 0:32], ALU.add, 512, ["DEN", "ZK"], ["pVb"], "pV")
+            tt(T.LE[:], T.TT[:], T.pV[:, 256:512], ALU.min, 256, ["TT", "TT0", "pVb"], ["LE"], "pV")
+            scan(T.G[:], T.MASK[:, 0:256], T.LE[:], 0.0, ALU.mult, ALU.max, 256, ["MASK", "LE"], ["G"])
+            cp(T.GI[:], T.G[:, 31:256:32], 8, ["G"], ["GI"])
+            ts(T.NB[:], T.GI[:], 127, None, ALU.bitwise_and, None, 8, ["GI"], ["NB"])
+            ts(T.NA[:], T.GI[:], 21, None, ALU.arith_shift_right, None, 8, ["GI"], ["NA"])
+            ts(T.NB8[:], T.NB[:], 8.0, None, ALU.mult, None, 8, ["NB"], ["NB8"])
+            tt(T.NM[:], T.NA[:], T.NB8[:], ALU.add, 16, ["NA", "NB8"], ["NM"])
+            tt(T.NX[:], T.NM[:].indirect(T.LU[:, 48:57]), T.MK[:], ALU.mult, 288, ["NM", "LU", "MK"], ["NX"])
+            mm([(T.pS[:, 0, 0:8], T.NX[:, 16:144], T.BLK[:], True, True), (T.pS[:, 0, 8:16], T.NX[:, 0:128], T.BLK[:], True, True)],
+               512, ["NX", "BLK"], ["pS"], "pS")
+            cp(T.NU[:, 16 * v:16 * v + 16], T.pS[:, 0, 0:16], 16, ["pS"], [("NU", v)], "pS")
+            send(T.NU[:, 16 * v + 8:16 * v + 16], T.RN[:, 8 * v:8 * v + 8], 2048, [("NU", v)], [("RN", v)], "rn%d" % v)
+            act(T.PG2[:], T.PK[:].indirect(T.NU[:, 16 * v:16 * v + 8]), 128 * GA, PKK + [("NU", v)], ["PG2"])
+            mm([(T.pS[:, 4:8, :], T.PG2[:], T.IDF[:], True, False), (T.pS[:, 4:8, :], T.IB[:], T.CY[:], False, True)], 640,
+               ["PG2", "IDF", "IB", "CY"], ["pS"], "pS")
+            act(T.Y2[:], T.G[:].indirect(T.LU[:, 40:48]), 128 * GA, ["G", "LU"], ["Y2"], scale=-1.0, bias=-2048.0)
+            mm([(T.pS[:, 8:16, 0:16], T.PG2[:], T.IDF[:], True, False), (T.pS[:, 8:16, 0:16], T.IB[:], T.CY[:], False, False),
+                (T.pS[:, 8:16, 0:16], T.IDF[:], T.Y2[:], False, True)], 1152, ["PG2", "IDF", "IB", "CY", "Y2"], ["pS2"], "pS")
+            act(T.U2[:], T.pS[:, 8:16, 0:16], 128, ["pS2"], ["U2"], "pS", func=ACT.Sign)
+            act(T.V2[:], T.U2[:], 128, ["U2"], ["V2"], func=ACT.Relu, scale=-float(FILL))
+            tt(T.DF[:, 1:256], T.G[:, 1:256], T.G[:, 0:255], ALU.subtract, 510, ["G", "DF0"], ["DF"])
+            ts(T.LOW[:], T.DF[:], 4095, None, ALU.bitwise_and, None, 256, ["DF", "DF0"], ["LOW"])
+            ts(T.EQ[:], T.LOW[:], 0.0, 128.0, ALU.is_equal, ALU.mult, 256, ["LOW"], ["EQ"])
+            act(T.pT[:, 8:16, :], T.EQ[:], 256, ["EQ"], ["pTb"], "pT", scale=-2.0 ** 17, bias=16777216.0)
+            scan(T.pV[:, 0:256], T.EQ[:], T.MASK[:, 0:256], 0.0, ALU.add, ALU.mult, 256, ["EQ", "MASK"], ["pVa"], "pV")
+            tt(T.T2[:], T.G[:], T.pV[:, 0:256], ALU.add, 256, ["G", "pVa"], ["T2"], "pV")
+            act(T.C8[:], T.pV[:, 31:256:32], 8, ["pVa"], ["C8"], "pV", scale=2.0 ** 18)
+            tt(T.VV[:], T.T2[:], T.pT[:, 8:16, :], ALU.min, 256, ["T2", "pTb"], ["VV"], "pT")
+            for k in range(5):
+                sh = 1 << k
+                n = 8 * (32 - sh)
+                ts(T.MB[:, :, sh:32], T.VV[:, :, sh:32], 7 + k, 1, ALU.arith_shift_right, ALU.bitwise_and, n, ["VV"], ["MB"])
+                tt(T.pT[:, 0:8, sh:32], T.VV[:, :, sh:32], T.MB[:, :, sh:32], ALU.mult, 2 * n, ["VV", "MB"], PTA, "pT")
+                tt(T.VV[:, :, 0:32 - sh], T.VV[:, :, 0:32 - sh], T.pT[:, 0:8, sh:32], ALU.max, n, ["VV"] + PTA, ["VV"], "pT")
+            ts(T.XS[:], T.VV[:, :, 0:16], 0xFFF07F, None, ALU.bitwise_and, None, 128, ["VV"], ["XS"])
+            tt(T.Q0[:], T.V2[:], T.pS[:, 4:8, :], ALU.max, 128, ["V2", "pS"], ["Q0a", "Q0b"], "pS")
+            act(T.UJ[:], T.C8[:].indirect(T.LU[:, 0:8]), 128 * GA, ["C8", "LU"], ["UJ"])
+            mm([(T.pS[:, 8:16, 16:32], T.IB[:], T.UJ[:], True, False), (T.pS[:, 8:16, 16:32], T.IB[:], T.POSC[:], False, True)], 256,
+               ["IB", "UJ", "POSC"], ["pS3"], "pS")
+            tt(T.XM[:], T.XS[:], T.pS[:, 8:16, 16:32], ALU.max, 128, ["XS", "pS3"], ["XM"], "pS")
+            for k in range(2):
+                stage(T.Q1, "Q1", T.Q0, "Q0", 8, ALU.max, ALU.min)
+                stage(T.Q0, "Q0", T.Q1, "Q1", 8, ALU.max, ALU.min)
+            tt(T.Q1[:], T.Q0[:], T.XM[:], ALU.min, 256, ["Q0a", "Q0b", "XM"], ["Q1a", "Q1b"])
+            stage(T.Q0, "Q0", T.Q1, "Q1", 8, ALU.min, ALU.max)
+            stage(T.Q1, "Q1", T.Q0, "Q0", 8, ALU.min, ALU.max)
+            stage(T.Q0, "Q0", T.Q1, "Q1", 8, ALU.min, ALU.max)
+            stage(T["OUT%d" % v], "OUT%d" % v, T.Q0, "Q0", 8, ALU.min, ALU.max)
+            send(T["OUT%d" % v][:], T["RL%d" % v][:], 65536, ["OUT%da" % v, "OUT%db" % v], [("RL", v)], "rl%d" % v)
+        for x, (dst, key) in enumerate(((CA, "CA"), (CB, "CB"))):
+            for c in range(8):
+                c4, h = c // 2, c % 2
+                o = 256 * x + 128 * h + 32 * c4
+                act(dst[:, 1024 * c4 + h:1024 * c4 + 1024:2], T.CO[:].indirect(IDX[:, o:o + 32]), 512 * GA,
+                    ["CO", "COz", ("IDX", e, x)], [(key, e, c)])
+        mm([(T.pI[:, 128 * h:128 * h + 128], T.SL[:, h:256:2], T.IDF[:], True, True) for h in range(2)], 1024,
+           ["SL", "IDF"], [("pI", 0)], "pI")
+        act(T.HI[:], T.pI[:, 0:256], 256, [("pI", 0)], ["HI"], "pI")
+        its = []
+        for h in range(2):
+            its.append((T.pI[:, 256 + 128 * h:384 + 128 * h], T.SL[:, h:256:2], T.IDF[:], True, False))
+            its.append((T.pI[:, 256 + 128 * h:384 + 128 * h], T.NIB[:], T.HI[:, 128 * h:128 * h + 128], False, True))
+        mm(its, 1280, ["SL", "IDF", "NIB", "HI"], [("pI", 1)], "pI")
+        act(T.LO[:], T.pI[:, 256:512], 256, [("pI", 1)], ["LO"], "pI")
+        for jp in range(8):
+            bk = "pL%d" % (jp % 2)
+            its = []
+            for jj in range(2):
+                j = 2 * jp + jj
+                its.append((T[bk][:, 256 * jj:256 * jj + 256], T.SEL[:, 128 * j:128 * j + 128], T.HI[:], True, False))
+                its.append((T[bk][:, 256 * jj:256 * jj + 256], T.SEL[:, 128 * j:128 * j + 128], T.LO[:], False, True))
+            mm(its, 1024, ["SEL", "HI", "LO"], [bk], bk)
+            for jj in range(2):
+                j = 2 * jp + jj
+                tt(T.AB[:, j:4096:16], SB[:, j:4096:16], T[bk][:, 256 * jj:256 * jj + 256], ALU.mult, 256, SBK + [bk], [("AB", j)], bk)
+        ABK = [("AB", j) for j in range(16)]
+        for c in range(8):
+            bk = "pC%d" % (c % 2)
+            lo = 512 * c
+            if c % 2 == 0:
+                for h in range(2):
+                    act(T.OA[:, lo + h:lo + 1024:2], T.AB[:, 2048 * h + lo // 2:2048 * h + lo // 2 + 512], 512, ABK,
+                        [("OA", c // 2, h)], scale=-1.0, bias=1.0)
+            rk = [(key, e, 2 * c4 + h) for key in ("CA", "CB") for c4 in set([c // 2, min((c + 1) // 2, 3)]) for h in range(2)]
+            mm([(T[bk][:], T.IB[:], CA[:, lo + 1:lo + 513], True, False), (T[bk][:], T.IB[:], CB[:, lo + 1:lo + 513], False, False),
+                (T[bk][:], T.NIB[:], CA[:, lo:lo + 512], False, False), (T[bk][:], T.NIB[:], CB[:, lo:lo + 512], False, True)],
+               2048, rk + ["CA%dz" % e, "CB%dz" % e, "IB", "NIB"], [bk], bk)
+            back = slice(lo + 511, lo - 1 if lo else None, -1)
+            ok = [("OA", c // 2, 0), ("OA", c // 2, 1)]
+            scan(T.WO[:, back], T[bk][:, ::-1], T.OA[:, back], 0.0, ALU.add, ALU.mult, 512, ok + [bk], [("WO", c)], bk)
+            if not YT_PE[v]:
+                scan(T.WT[:, lo:lo + 512], T.MASK[:, 0:512], T.OA[:, lo:lo + 512], 0.0, ALU.mult, ALU.add, 512, ok + ["MASK"], [("WT", c)])
+        yo = slice(128 * v, 128 * v + 128)
+        mm([(T.pC0[:, 0:128], T.IB[:], CA[:, 1:4096:32], True, False), (T.pC0[:, 0:128], T.IB[:], CB[:, 1:4096:32], False, True)], 256,
+           [(key, e, cc) for key in ("CA", "CB") for cc in range(8)] + ["IB"], ["pC0"], "pC0")
+        tt(T.YC[:, yo], T.WO[:, 1:4096:32], T.pC0[:, 0:128], ALU.add, 128, [("WO", c) for c in range(8)] + ["pC0"], [("YC", v)], "pC0")
+        if YT_PE[v]:
+            for j in range(16):
+                ss = [s for s in (j, j + 16) if s]
+                mm([(T.pL0[:, 0:128], T.IDF[:], T.AB[:, 2048 * (s // 16) + j:2048 * (s // 16) + 2048:16], s == 16, s == 31) for s in ss], 512 * len(ss),
+                   ABK + ["IDF"], ["pL0"], "pL0")
+            act(T.YT[:, yo], T.pL0[:, 0:128], 128, ["pL0"], [("YT", v)], "pL0", scale=8.0)
+        else:
+            act(T.YT[:, yo], T.WT[:, 31:4096:32], 128, [("WT", c) for c in range(8)], [("YT", v)], scale=-8.0, bias=248.0)
+        dma("Y", Y, T.yc[:, yo], T.YC[:, yo], 65536, [("YC", v)], [], "dst")
+        dma("Y", Y, T.yt[:, yo], T.YT[:, yo], 65536, [("YT", v)], [], "dst")
+    return ops, n_out
+
+
+def rank_program(g, core, T, topo):
+    if T.rank_of(core) is None:
+        return
+    ops, n_out = build(g, core, T, topo)
+    order = plan(ops)
+    queues = {"V": g.vector, "S": g.scalar, "P": g.tensor, "G": g, "Y": g.sync}
+    count = {}
+    known = {q: {} for q in queues}
+    for i in order:
+        o = ops[i]
+        q = o["q"]
+        if q == "R":
+            o["at"] = (o["sem"], o["inc"])
+            o["clock"] = {o["sem"]: o["inc"]}
+            count[o["sem"]] = o["inc"]
+            continue
+        kn = known[q]
+        need = {}
+        for d in o["deps"]:
+            od = ops[d]
+            if q == "P" and od["q"] == "P":
+                continue
+            s, c = od["at"]
+            if kn.get(s, 0) < c and need.get(s, (0, 0))[0] < c:
+                need[s] = (c, d)
+        for s, (c, d) in sorted(need.items(), key=lambda x: -ops[x[1][1]]["t"]):
+            if kn.get(s, 0) >= c:
+                continue
+            queues[q].wait_ge(T.sem[s], c)
+            for s2, c2 in ops[d]["clock"].items():
+                if kn.get(s2, 0) < c2:
+                    kn[s2] = c2
+        ins = o["fn"]()
+        if o["sem"] == "*":
+            count["sent"] = count.get("sent", 0) + n_out
+            continue
+        ins.then_inc(T.sem[o["sem"]], o["inc"])
+        count[o["sem"]] = count.get(o["sem"], 0) + o["inc"]
+        o["at"] = (o["sem"], count[o["sem"]])
+        o["clock"] = dict(kn)
+        o["clock"][o["sem"]] = count[o["sem"]]
+    for s, c in count.items():
+        g.wait_ge(T.sem[s], c)

@@ -4,10 +4,17 @@ from concourse.mybir import dt, AluOpType, AxisListType, ActivationFunctionType
 ALU = AluOpType
 ACT = ActivationFunctionType
 NV = 5
-FILL = 4095 * 4096 + 15 * 128
+FILL = 4095 * 256
+TOP = 2.0 ** 20 - 1
+M256 = 1.5 * 2.0 ** 31
+M4096 = 2.0 ** 35 + 8192
 VADD = (0, 0, 0, 0, 1)
-VSHARE = (8, 6, 6, 6, 6)
+VSHARE = (8, 7, 7, 7, 8)
 YT_PE = (1, 1, 1, 1, 0)
+ONE_S = (4, 4, 4, 8, 8)
+SGW, COW, ONEW = (2, 2, 2, 2, 1), (1, 1, 1, 1, 1), (2, 2, 2, 2, 1)
+CADD = (1, 1, 1, 1, 0)
+FLOOR_V = (1, 1, 1, 1)
 
 F32, BF, I32, U16, F16 = "float32", "bfloat16", "int32", "uint16", "float16"
 SCRATCH = {}
@@ -17,155 +24,238 @@ def _sb(name, shape, d):
     SCRATCH[name] = ("sbuf", [128] + list(shape), d)
 
 
+IDS = {"IB": 1.0, "NIB": -1.0, "I3": 3 * 2.0 ** 20, "I1": 2.0 ** 20, "NI1": -2.0 ** 20, "I28": 2.0 ** 28,
+       "IC": -4.3125 * 2.0 ** 20, "NI8": -0.125, "IW": -2.0 ** 23, "I64": 64.0, "I2": 2.0, "NI2": -2.0}
+IDH = {"IH32": 32.0, "IH": 1.0, "NIH": -1.0}
+
 for _n, _s, _d in [
-    ("SG", [4112], BF), ("CO", [4112], BF), ("PXI", [1024], I32), ("PK", [1024], F32),
-    ("PXM", [1024], I32), ("MI", [1024], F32),
-    ("RAW", [256], I32), ("RM", [256], I32), ("RK", [256], F32),
+    ("SG", [4112], BF), ("CO", [4112], BF), ("PXI", [1024], I32), ("PF", [1024], F32), ("PK", [1024], F32),
+    ("LSI", [128], I32), ("RAWF", [256], F32), ("AQ", [256], F32),
     ("FPI", [8], I32), ("FPU", [8], U16), ("OMI", [40], I32), ("OMB", [640], F32),
-    ("ONE", [128], F32), ("IDF", [128], F32), ("PERM", [128], F32), ("IH", [128], F16), ("IH32", [128], F16),
-    ("IB", [128], BF), ("NIB", [128], BF), ("CSEL", [2048], BF), ("SEL", [2048], BF),
+    ("ONE", [128], F32), ("IDF", [128], F32), ("NIF", [128], F32), ("I15", [128], F32), ("PERM", [128], F32), ("PERM15", [128], F32),
+    ("IDS", [128 * len(IDS)], BF), ("IDH", [128 * len(IDH)], F16), ("SEL", [2048], BF), ("ONES", [2048], BF),
     ("PI", [8], I32), ("PJ", [8], I32), ("PCOL", [8], F32), ("IO8", [8], F32), ("IO144", [144], F32), ("MK", [144], F32),
-    ("BLK", [8], F32), ("BLKB", [8], F32), ("RMA", [16], BF), ("RMB", [16], BF), ("RMA2", [16], BF),
-    ("CZ", [512], BF), ("CY", [128], BF), ("MASK", [1024], F32), ("POSI", [128], F32), ("POSC", [128], BF),
-    ("LI", [64], I32), ("LU", [64], U16),
-    ("L0", [8, 16], F32), ("PG", [128], F32), ("M0", [8, 32], F32), ("M1", [8, 32], F32), ("K", [8, 32], I32),
-    ("ZK", [8, 33], I32), ("YI", [256], I32), ("YF", [256], F16), ("D0", [256], F16),
-    ("A16", [256], F16), ("B16", [256], F16), ("SLAB", [8, 32], F16), ("IDX0", [512], U16), ("IDX1", [512], U16),
-    ("LEN", [256], F32), ("LB", [256], F32), ("W", [256], F32), ("TT", [256], F32), ("OA", [4096], F32),
-    ("XI", [256], I32), ("DEN", [256], I32), ("LE", [256], F32), ("G", [256], F32),
-    ("GI", [8], I32), ("NA", [8], I32), ("NB", [8], I32), ("NB8", [8], F32), ("NM", [8], F32), ("NX", [144], F32),
-    ("DF", [256], I32), ("LOW", [256], I32), ("EQ", [256], F32), ("T2", [256], F32), ("VV", [8, 32], I32),
-    ("MB", [8, 32], I32), ("C8", [8], F32), ("XS", [128], I32), ("UJ", [128], BF), ("XM", [128], F32),
-    ("PG2", [128], F32), ("Y2", [128], F32), ("U2", [128], F32), ("V2", [128], F32),
-    ("Q0", [8, 16], F32), ("Q1", [8, 16], F32),
-    ("SL", [256], F32), ("HI", [256], BF), ("LO", [256], BF),
-    ("SA0", [4096], BF), ("SB0", [4096], BF), ("SA1", [4096], BF), ("SB1", [4096], BF),
-    ("CA0", [4112], BF), ("CB0", [4112], BF), ("CA1", [4112], BF), ("CB1", [4112], BF),
-    ("AB", [4096], F32), ("WO", [4096], F32), ("WT", [4096], F32), ("YC", [640], F32), ("YT", [640], F32),
+    ("BLK", [8], F32), ("BLKB", [16], F32), ("RMA", [16], BF), ("RMB", [16], BF),
+    ("C1024", [256], BF), ("MI", [512], F32), ("MASK", [512], F32), ("MASKB", [256], BF),
+    ("RV", [8, 4, 4], F32), ("RD", [128], F32), ("CP1", [128], BF), ("CP2", [128], BF), ("CP3", [128], BF), ("JC", [128], BF),
+    ("GX", [128], F32), ("BDG", [128], BF), ("LI", [72], I32), ("LU", [72], U16),
+    ("PG", [128], F32), ("PGS", [8, 16], F32), ("M0", [8, 32], F32), ("K", [8, 32], I32),
+    ("ZF", [8, 32], F32), ("Z0", [8, 33], F32), ("YI", [256], I32), ("YF", [256], F16), ("D0", [256], F16),
+    ("A16", [256], F16), ("B16", [256], F16), ("SLAB", [8, 32], BF), ("IDX0", [512], U16), ("IDX1", [512], U16),
+    ("LB", [8, 32], F32), ("W", [256], F32), ("TT", [8, 32], F32), ("SN", [256], BF), ("UU", [256], BF),
+    ("LE", [256], F32), ("G", [264], F32),
+    ("GI", [8], I32), ("NA", [8], I32), ("NB", [8], I32), ("NM", [8], F32), ("NX", [144], F32),
+    ("DF", [8, 32], I32), ("LOW", [8, 32], I32), ("INV", [256], BF), ("EE", [256], F32), ("CI", [256], BF), ("YY", [256], BF),
+    ("FL", [1024], BF), ("XP", [8, 32], F32), ("UJ", [128], BF),
+    ("PG2", [128], F32), ("Y2", [128], F32), ("U2", [128], BF), ("T0", [128], F32), ("V2", [128], F32), ("WN", [128], BF),
+    ("TS", [8, 8], F32), ("Q0", [8, 16], F32), ("Q1", [8, 16], F32),
+    ("SL", [8, 32], F32), ("HI", [256], BF), ("LO", [256], BF),
+    ("SA0", [2048, 2], BF), ("SB0", [2048, 2], BF), ("SA1", [2048, 2], BF), ("SB1", [2048, 2], BF),
+    ("CA0", [4096], F16), ("CB0", [4096], F16), ("CA1", [4096], F16), ("CB1", [4096], F16),
+    ("AB0", [4096], F32), ("AB1", [4096], F32), ("WO", [4096], F32), ("YC", [640], F32), ("YT", [640], F32),
     ("RN", [32], U16), ("NU", [64], U16),
 ]:
     _sb(_n, _s, _d)
 for _v in range(NV - 1):
     _sb("OUT%d" % _v, [8, 16], F32)
     _sb("RL%d" % _v, [8, 16], F32)
-for _n in ("pS", "pT"):
+for _n in ("pS", "pT", "pI", "pK"):
     SCRATCH[_n] = ("psum", [128, 16, 32], F32)
-for _n in ("pI", "pL0", "pL1", "pV", "pC0", "pC1"):
+for _n in ("pV", "pF0", "pF1", "pY"):
     SCRATCH[_n] = ("psum", [128, 512], F32)
 
 SEMAPHORES = (["cV", "cS", "cP", "cG", "dls", "dfp", "dpx", "dom", "dsg", "dco", "dst", "sent"]
-              + ["add%d" % v for v in range(NV)] + ["rn%d" % v for v in range(NV - 1)] + ["rl%d" % v for v in range(NV - 1)])
+              + ["add%d" % v for v in range(NV)] + ["one%d" % v for v in range(NV)] + ["cadd%d" % v for v in range(2 * NV)]
+              + ["rn%d" % v for v in range(NV - 1)] + ["rl%d" % v for v in range(NV - 1)])
 
-CYC = 1.0
-PCYC = 0.52
-GA = 1.55
-HOP = 80.0
-
-
-def sweep(ops, pred, succ, prio, ahead, back):
-    n = len(ops)
-    left = [len(p) for p in pred]
-    ready = [0.0] * n
-    start = [0.0] * n
-    avail, free = {}, {}
-    for i, o in enumerate(ops):
-        avail.setdefault(o["q"], [])
-        free[o["q"]] = 0.0
-        if back:
-            ready[i] = o["lat"] - o["busy"]
-        if left[i] == 0:
-            avail[o["q"]].append(i)
-    order = []
-    while len(order) < n:
-        best = None
-        for q, lst in avail.items():
-            if not lst:
-                continue
-            t0 = max(free[q], min(ready[i] for i in lst))
-            c = max((i for i in lst if ready[i] <= t0 + ahead), key=lambda i: (prio[i], -i))
-            st = max(free[q], ready[c])
-            if best is None or st < best[0]:
-                best = (st, q, c)
-        st, q, c = best
-        avail[q].remove(c)
-        free[q] = st + ops[c]["busy"]
-        start[c] = st
-        order.append(c)
-        for s in succ[c]:
-            if back:
-                t = st + ops[c]["busy"] + HOP + ops[s]["lat"] - ops[s]["busy"]
-            else:
-                t = st + ops[c]["lat"] + HOP
-            ready[s] = max(ready[s], t)
-            left[s] -= 1
-            if left[s] == 0:
-                avail[ops[s]["q"]].append(s)
-    return order, start
-
-
-PLANS = {}
-FIFO = False
-ROUNDS = 40
-CLIMB = 1200
+CASES = ((1.0, 1.55, 70.0, 3000.0, 250.0), (1.25, 1.15, 80.0, 3000.0, 300.0), (1.35, 2.0, 90.0, 3500.0, 200.0))
+ROUNDS = 100
+CLIMB = 40000
 NOISE = 1000.0
-AHEAD = 160.0
+SLACK = 200.0
+PLANS = {}
+
+
+def costs(ops, case):
+    f, ga, hop, way, rate = case
+    busy, lat = [], []
+    for o in ops:
+        fix, n, gat, kind = o["cost"]
+        if kind == "dma":
+            b = fix + n / rate
+            l = b + 1000.0
+        elif kind == "send":
+            b = n / 40.0
+            l = b + way - 1300.0
+        elif kind == "pe":
+            b = f * (fix + 0.42 * n)
+            l = b + 70.0
+        else:
+            b = l = f * (fix + 0.83 * max(n + gat * ga, 32))
+        busy.append(b)
+        lat.append(l + hop)
+    return busy, lat
+
+
+def replay(qs, pred, order, busy, lat, first=0, known=None):
+    free = [0.0] * 8
+    start, done = (list(known[0]), list(known[1])) if first else ([0.0] * len(qs), [0.0] * len(qs))
+    for i in order[max(first - 300, 0):first]:
+        free[qs[i]] = start[i] + busy[i]
+    for i in order[first:]:
+        q = qs[i]
+        t = free[q]
+        for d in pred[i]:
+            if done[d] > t:
+                t = done[d]
+        start[i] = t
+        free[q] = t + busy[i]
+        done[i] = t + lat[i]
+    return max(done), start, done
+
+
+def sweep(qs, pred, succ, prio, busy, lat, back):
+    n = len(qs)
+    left = [len(p) for p in pred]
+    ready = [lat[i] - busy[i] if back else 0.0 for i in range(n)]
+    start = [0.0] * n
+    slots = {}
+    held = [False] * n
+    for first in sorted(range(n), key=lambda i: -prio[i]):
+        if left[first]:
+            held[first] = True
+            continue
+        todo = [first]
+        while todo:
+            todo.sort(key=lambda i: prio[i])
+            c = todo.pop()
+            row = slots.setdefault(qs[c], [])
+            t, b = ready[c], busy[c]
+            lo, hi = 0, len(row)
+            while lo < hi:
+                m = (lo + hi) // 2
+                if row[m][1] <= t:
+                    lo = m + 1
+                else:
+                    hi = m
+            while lo < len(row) and row[lo][0] < t + b:
+                t = max(t, row[lo][1])
+                lo += 1
+            row.insert(lo, (t, t + b))
+            start[c] = t
+            for s in succ[c]:
+                u = t + b + lat[s] - busy[s] if back else t + lat[c]
+                if u > ready[s]:
+                    ready[s] = u
+                left[s] -= 1
+                if left[s] == 0 and held[s]:
+                    todo.append(s)
+    return sorted(range(n), key=lambda i: (start[i], i)), start
 
 
 def plan(ops):
     n = len(ops)
-    key = tuple((o["q"], o["busy"], tuple(o["deps"])) for o in ops)
+    key = tuple((o["q"], o["cost"], tuple(o["deps"])) for o in ops)
     if key not in PLANS:
-        pred = [o["deps"] for o in ops]
+        qs = ["VSPGYD".index(o["q"]) for o in ops]
+        above = []
+        pred = []
         succ = [[] for _ in range(n)]
         for i, o in enumerate(ops):
-            for d in o["deps"]:
-                succ[d].append(i)
+            seen, keep = 0, []
+            for d in reversed(o["deps"]):
+                if not seen >> d & 1:
+                    keep.append(d)
+                    succ[d].append(i)
+                    seen |= above[d] | 1 << d
+            above.append(seen)
+            pred.append(keep)
+        cs = [costs(ops, c) for c in CASES]
+        busy, lat = cs[0]
+        seed = [12345]
+
+        def rnd(m):
+            seed[0] = (seed[0] * 1103515245 + 12345) % 2147483648
+            return (seed[0] >> 8) % m
+
+        def score(order, first=0, known=None):
+            got = [replay(qs, pred, order, b, l, first, known and known[k]) for k, (b, l) in enumerate(cs)]
+            return sum(r[0] / c[0] for r, c in zip(got, CASES)) / len(cs), [r[1:] for r in got]
+
         prio = [0.0] * n
         for i in range(n - 1, -1, -1):
-            prio[i] = ops[i]["lat"] + HOP + max([prio[s] for s in succ[i]] + [0.0])
-        if FIFO:
-            lead = [False] * n
-            lead[max(i for i in range(n) if ops[i]["name"] == "['TT']")] = True
-            for i in range(n - 1, -1, -1):
-                if lead[i]:
-                    for d in ops[i]["raw"]:
-                        lead[d] = True
-            prio = [1e9 + prio[i] if lead[i] else -float(i) for i in range(n)]
+            prio[i] = lat[i] + max([prio[s] for s in succ[i]] + [0.0])
         best = None
-        x = 12345
         for r in range(ROUNDS):
-            order, start = sweep(ops, pred, succ, prio, AHEAD, False)
-            end = max(start[i] + ops[i]["lat"] for i in range(n))
+            order, start = sweep(qs, pred, succ, prio, busy, lat, False)
+            end = score(order)[0]
             if best is None or end < best[0]:
                 best = (end, order, start)
             if r % 4 == 3:
                 start = best[2]
             amp = (0.0, NOISE, 0.0, 4.0 * NOISE)[r % 4]
-            back = []
-            for i in range(n):
-                x = (x * 1103515245 + 12345) % 2147483648
-                back.append(start[i] + ops[i]["busy"] + amp * x / 2147483648)
-            _o, st = sweep(ops, succ, pred, back, AHEAD, True)
-            prio = [st[i] + ops[i]["busy"] for i in range(n)]
+            back = [start[i] + busy[i] + amp * rnd(1000) / 1000.0 for i in range(n)]
+            _o, st = sweep(qs, succ, pred, back, busy, lat, True)
+            prio = [st[i] + busy[i] for i in range(n)]
+        order = best[1]
+        end, starts = score(order)
+        best = (end, order, starts[0][0])
+        links = None
         for r in range(CLIMB):
-            x = (x * 1103515245 + 12345) % 2147483648
-            a = (x >> 8) % n
-            x = (x * 1103515245 + 12345) % 2147483648
-            w = 1 + (x >> 8) % 24
-            x = (x * 1103515245 + 12345) % 2147483648
-            d = ((x >> 8) % 2001 - 1000) * (1.0, 4.0, 12.0)[r % 3]
-            prio = [-t for t in best[2]]
-            for i in range(a, min(n, a + w)):
-                if ops[i]["q"] == ops[a]["q"] or r % 2:
-                    prio[i] += d
-            order, start = sweep(ops, pred, succ, prio, AHEAD, False)
-            end = max(start[i] + ops[i]["lat"] for i in range(n))
-            if end <= best[0]:
-                best = (end, order, start)
+            if links is None:
+                pos = [0] * n
+                before = [-1] * n
+                tail = [-1] * 8
+                for k, i in enumerate(order):
+                    pos[i] = k
+                    before[i] = tail[qs[i]]
+                    tail[qs[i]] = i
+                links = []
+                for (st, _d), (b, l) in zip(starts, cs):
+                    i = max(range(n), key=lambda j: st[j] + l[j])
+                    while i >= 0:
+                        a = before[i]
+                        if a >= 0 and st[a] + b[a] >= st[i] - 1e-6:
+                            if a not in pred[i]:
+                                links.append((a, i))
+                            i = a
+                        else:
+                            i = max(pred[i], key=lambda d: st[d] + l[d]) if pred[i] and st[i] > 0 else -1
+            a, i = links[rnd(len(links))]
+            new = list(order)
+            if rnd(2):
+                for _ in range((0, 0, 1, 2, 4, 8, 16, 32)[rnd(8)]):
+                    if before[a] >= 0:
+                        a = before[a]
+                to = max([pos[a]] + [pos[d] + 1 for d in pred[i]])
+                if to > pos[before[i]]:
+                    continue
+                del new[pos[i]]
+                new.insert(to, i)
+                first = to
+            else:
+                to = min([pos[i] + (0, 0, 2, 5, 10, 20, 40, 80)[rnd(8)], n - 1] + [pos[s] - 1 for s in succ[a]])
+                if to < pos[i]:
+                    continue
+                del new[pos[a]]
+                new.insert(to, a)
+                first = pos[a]
+            e2, s2 = score(new, first, starts)
+            if e2 <= end + SLACK * (1.0 - r / CLIMB) * rnd(1000) / 1000.0:
+                place = {i: k for k, i in enumerate(new)}
+                end, starts, links = e2, s2, None
+                order = sorted(new, key=lambda i: (s2[0][0][i], place[i]))
+                if end < best[0]:
+                    best = (end, order, s2[0][0])
         PLANS[key] = best
     for i, o in enumerate(ops):
         o["t"] = PLANS[key][2][i]
     return PLANS[key][1]
+
+
+def runs(a, b, w):
+    cuts = [a] + [c for c in range(a + 1, b) if c % w == 0] + [b]
+    return [(c, d - c) for c, d in zip(cuts, cuts[1:]) if d > c]
 
 
 def build(g, core, T, topo):
@@ -178,15 +268,12 @@ def build(g, core, T, topo):
     ops = []
     lastw, readers, bankers = {}, {}, {}
 
-    def op(q, fn, busy, r=(), w=(), bank=None, lat=None, sem=None, inc=1, name=""):
+    def op(q, fn, cost, r=(), w=(), bank=None, sem=None, inc=1):
         i = len(ops)
         deps = set()
         for k in r:
             if k in lastw:
                 deps.add(lastw[k])
-        raw = sorted(deps)
-        if q == "P":
-            raw += [lastw[k] for k in w if k in lastw and ops[lastw[k]]["q"] == "P"]
         for k in w:
             if k in lastw:
                 deps.add(lastw[k])
@@ -205,62 +292,68 @@ def build(g, core, T, topo):
                 deps.update(b[1])
             b[1].append(i)
         deps.discard(i)
-        ops.append({"q": q, "fn": fn, "busy": busy, "lat": busy if lat is None else lat, "deps": sorted(deps), "raw": raw,
-                    "sem": sem or "c" + q, "inc": inc, "name": name})
+        ops.append({"q": q, "fn": fn, "cost": cost, "deps": sorted(deps), "sem": sem or "c" + q, "inc": inc, "name": str(w)})
         return i
-
-    def vc(n):
-        return 50.0 + max(n, 32) * CYC
 
     def ts(out, in0, s1, s2, o0, o1, n, r, w, bank=None):
         if o1 is None:
-            return op("V", lambda: V.tensor_scalar(out, in0, s1, None, o0), vc(n), r, w, bank, name=str(w))
-        return op("V", lambda: V.tensor_scalar(out, in0, s1, s2, o0, o1), vc(n), r, w, bank, name=str(w))
+            return op("V", lambda: V.tensor_scalar(out, in0, s1, None, o0), (50.0, n, 0, ""), r, w, bank)
+        return op("V", lambda: V.tensor_scalar(out, in0, s1, s2, o0, o1), (50.0, n, 0, ""), r, w, bank)
 
     def tt(out, a, b, o, n, r, w, bank=None):
-        return op("V", lambda: V.tensor_tensor(out, a, b, o), vc(n), r, w, bank, name=str(w))
+        return op("V", lambda: V.tensor_tensor(out, a, b, o), (50.0, n, 0, ""), r, w, bank)
 
-    def cp(out, a, n, r, w, bank=None):
-        return op("V", lambda: V.tensor_copy(out, a), vc(n), r, w, bank, name=str(w))
+    def cp(out, a, n, r, w, bank=None, gat=0):
+        return op("V", lambda: V.tensor_copy(out, a), (50.0, n, gat, ""), r, w, bank)
 
     def ms(ap, c, n, w):
-        return op("V", lambda: V.memset(ap, c), vc(n), (), w, name=str(w))
+        return op("V", lambda: V.memset(ap, c), (50.0, n, 0, ""), (), w)
 
     def scan(out, d0, d1, init, o0, o1, n, r, w, bank=None):
-        return op("V", lambda: V.tensor_tensor_scan(out, d0, d1, init, o0, o1), vc(n), r, w, bank, name=str(w))
+        return op("V", lambda: V.tensor_tensor_scan(out, d0, d1, init, o0, o1), (50.0, n, 0, ""), r, w, bank)
 
-    def act(out, a, n, r, w, bank=None, func=ACT.Identity, scale=1.0, bias=0.0):
-        return op("S", lambda: S.activation(out, a, func, bias=bias, scale=scale), 65.0 + max(n, 32) * CYC, r, w, bank, name=str(w))
+    def act(out, a, n, r, w, bank=None, func=ACT.Identity, scale=1.0, bias=0.0, gat=0):
+        return op("S", lambda: S.activation(out, a, func, bias=bias, scale=scale), (65.0, n, gat, ""), r, w, bank)
 
     def mm(items, cyc, r, w, bank):
         def fn():
             for it in items:
                 ins = P.matmul(*it)
             return ins
-        return op("P", fn, 30.0 + cyc * PCYC, r, w, bank, lat=100.0 + cyc * PCYC, name=str(w))
+        return op("P", fn, (30.0, cyc, 0, "pe"), r, w, bank)
+
+    def group(out, terms, start, r, w, bank, stop=True):
+        its = [(out, a, b, start and k == 0, stop and k == len(terms) - 1) for k, (a, b, c) in enumerate(terms)]
+        return mm(its, sum(c for a, b, c in terms), r, w, bank)
 
     def dma(q, eng, out, a, nbytes, r, w, sem, **kw):
-        return op(q, lambda: eng.dma_start(out, a, **kw), 1000.0 if q == "G" else 60.0, r, w, lat=2000.0 + nbytes / 150.0, sem=sem, inc=16, name=str(w))
+        key = ("dma", len(ops))
+        op(q, lambda: eng.dma_start(out, a, **kw), (1000.0 if q == "G" else 60.0, 0, 0, "dma"), r, list(w) + [key], sem=sem, inc=16)
+        op("D", None, (0.0, nbytes, 0, "dma"), list(r) + [key], w)
 
-    def iota(out, pat, base, cm, n, w, small):
+    def iota(out, pat, base, cm, n, w, small=True):
         if small:
-            return op("G", lambda: g.iota(out, pat, base, cm, allow_small_or_imprecise_dtypes=True), 130.0 + 2 * n * CYC, (), w)
-        return op("G", lambda: g.iota(out, pat, base, cm), 130.0 + 2 * n * CYC, (), w)
+            return op("G", lambda: g.iota(out, pat, base, cm, allow_small_or_imprecise_dtypes=True), (130.0, 2 * n, 0, ""), (), w)
+        return op("G", lambda: g.iota(out, pat, base, cm), (130.0, 2 * n, 0, ""), (), w)
 
     def asel(out, a, pat, base, n, r, w):
-        return op("G", lambda: g.affine_select(out, a, pat, ALU.is_equal, 0.0, base, 1), 170.0 + 2 * n * CYC, r, w)
+        return op("G", lambda: g.affine_select(out, a, pat, ALU.is_equal, 0.0, base, 1), (170.0, 2 * n, 0, ""), r, w)
 
     def send(src, dst, nbytes, r, w, sem):
-        op("G", lambda: g.remote_dma(dst, src, T.sem[sem], T.sem.sent, pid, rid, omask), 300.0, r, [("sent", sem)],
-           lat=3000.0 + nbytes / 40.0, sem="*")
-        op("R", None, 0.0, [("sent", sem)], w, sem=sem, inc=n_in)
+        op("G", lambda: g.remote_dma(dst, src, T.sem[sem], T.sem.sent, pid, rid, omask), (300.0, 0, 0, "dma"), r, [("sent", sem)], sem="*")
+        op("D", None, (0.0, nbytes, 0, "send"), [("sent", sem)], w, sem=sem, inc=n_in)
 
-    dma("Y", Y, T.RAW[:, 0:128], T.ls[:], 65536, (), ["RAW0"], "dls")
+    I = {}
+    for names, buf in ((IDS, T.IDS), (IDH, T.IDH)):
+        for k, name in enumerate(names):
+            I[name] = buf[:, 128 * k:128 * k + 128]
+
+    dma("Y", Y, T.LSI[:], T.ls[:], 65536, (), ["LSI"], "dls")
     dma("S", S, T.FPI[:], T.fp[:], 4096, (), ["FPI"], "dfp")
-    dma("Y", Y, T.PXI[:], T.px[:], 524288 + 65536, (), ["PXI"], "dpx")
+    dma("Y", Y, T.PXI[:], T.px[:], 524288, (), ["PXI"], "dpx")
     dma("S", S, T.OMI[:], T.om[:], 20480, (), ["OMI"], "dom")
-    dma("Y", Y, T.SG[:, 0:4096], T.sg[:], 1638400, (), ["SG"], "dsg")
-    dma("Y", Y, T.CO[:, 0:4096], T.co[:], 2686976, (), ["CO"], "dco")
+    dma("Y", Y, T.SG[:, 0:4096], T.sg[:], 1048576, (), ["SG"], "dsg")
+    dma("Y", Y, T.CO[:, 0:4096], T.co[:], 1048576, (), ["CO"], "dco")
 
     ms(T.ONE[:], 1.0, 128, ["ONE"])
     iota(T.PI[:, 0:1], [[0, 1]], 0, 1, 1, ["PI"], False)
@@ -269,252 +362,298 @@ def build(g, core, T, topo):
     iota(T.LI[:, 0:40], [[1, 40]], 0, 0, 40, ["LI0"], False)
     iota(T.LI[:, 40:48], [[32, 8]], 31, 0, 8, ["LI1"], False)
     iota(T.LI[:, 48:64], [[1, 16]], -1, 0, 16, ["LI2"], False)
-    iota(T.IO8[:], [[1, 8]], 0, 0, 8, ["IO8"], True)
-    iota(T.IO144[:], [[0, 9], [1, 16]], 0, 0, 144, ["IO144"], True)
-    iota(T.POSI[:], [[0, 8], [128, 16]], -3904, 0, 128, ["POSI"], True)
-    iota(T.CZ[:], [[-2304, 2], [0, 256]], 0, 0, 512, ["CZ"], True)
-    iota(T.CY[:], [[0, 128]], -2176, 0, 128, ["CY"], True)
-    iota(T.MI[:], [[0, 32], [1, 32]], 0, 0, 1024, ["MI"], True)
-    act(T.MASK[:], T.MI[:], 1024, ["MI"], ["MASK"], func=ACT.Sign)
-    iota(T.CSEL[:], [[0, 2048]], 1, 0, 2048, ["CSEL"], True)
-    asel(T.SEL[:], T.CSEL[:], [[-1, 16], [-16, 8], [0, 16]], 0, 2048, ["CSEL"], ["SEL"])
+    iota(T.LI[:, 64:72], [[32, 8]], 32, 0, 8, ["LI3"], False)
+    iota(T.IO8[:], [[1, 8]], 0, 0, 8, ["IO8"])
+    iota(T.IO144[:], [[0, 9], [1, 16]], 0, 0, 144, ["IO144"])
+    iota(T.CP2[:], [[0, 8], [128, 16]], 0, 0, 128, ["CP2"])
+    iota(T.CP3[:], [[0, 8], [-128, 16]], 3968, 0, 128, ["CP3"])
+    iota(T.JC[:], [[0, 8], [1, 16]], 8, 0, 128, ["JC"])
+    iota(T.GX[:], [[1, 8], [0, 16]], 0, 0, 128, ["GX"])
+    for u in range(4):
+        iota(T.RV[:, :, u, :], [[0, 8], [4, 2], [8, 2]], (0, 2, 1, 3)[u], 0, 32, [("RV", u)])
+    RVK = [("RV", u) for u in range(4)]
+    iota(T.C1024[:], [[0, 256]], 1024, 0, 256, ["C1024"])
+    iota(T.MI[:], [[0, 16], [1, 32]], 0, 0, 512, ["MI"])
+    act(T.MASK[:], T.MI[:], 512, ["MI"], ["MASK"], func=ACT.Sign)
+    act(T.MASKB[:], T.MI[:, 0:256], 256, ["MI"], ["MASKB"], func=ACT.Sign)
+    act(T.pT[:, 8:16, :], T.MI[:, 0:256], 256, ["MI"], ["SC"], "pT", scale=2.0 ** -5)
+    iota(T.ONES[:], [[0, 2048]], 1, 0, 2048, ["ONES"])
+    asel(T.SEL[:], T.ONES[:], [[-1, 16], [-16, 8], [0, 16]], 0, 2048, ["ONES"], ["SEL"])
     ts(T.PJ[:, 0:1], T.PI[:, 0:1], 15, None, ALU.bitwise_and, None, 1, ["PI"], ["PJ0"])
     ts(T.PJ[:, 1:2], T.PI[:, 0:1], 4, None, ALU.arith_shift_right, None, 1, ["PI"], ["PJ1"])
     cp(T.PCOL[:, 0:2], T.PJ[:, 0:2], 2, ["PJ0", "PJ1"], ["PC0"])
-    ts(T.PCOL[:, 2:3], T.PJ[:, 0:1], 128.0, None, ALU.mult, None, 1, ["PJ0"], ["PC2"])
     ts(T.PCOL[:, 3:4], T.PJ[:, 0:1], 128.0, 2048.0, ALU.mult, ALU.add, 1, ["PJ0"], ["PC3"])
-    cp(T.LU[:], T.LI[:], 64, ["LI0", "LI1", "LI2"], ["LU"])
+    cp(T.LU[:], T.LI[:], 72, ["LI0", "LI1", "LI2", "LI3"], ["LU"])
     ms(T.LU[:, 48:49], 7, 1, ["LU"])
     cp(T.FPU[:], T.FPI[:], 8, ["FPI"], ["FPU"])
     ts(T.MK[:], T.IO144[:], T.PCOL[:, 0:1], None, ALU.is_equal, None, 144, ["IO144", "PC0"], ["MK"])
     ts(T.BLK[:], T.IO8[:], T.PCOL[:, 1:2], None, ALU.is_equal, None, 8, ["IO8", "PC0"], ["BLK"])
-    for buf, key, c0, c1 in ((T.RMA, "RMA", -4096.0, -512.0), (T.RMB, "RMB", -4096.0, 512.0), (T.RMA2, "RMA2", 0.0, -1024.0)):
+    ts(T.BDG[:], T.GX[:], T.PCOL[:, 1:2], 2.0 ** 19, ALU.is_equal, ALU.mult, 128, ["GX", "PC0"], ["BDG"])
+    for buf, key, c0, c1 in ((T.RMA, "RMA", -4096.0, -1.0), (T.RMB, "RMB", -4096.0, 1.0), (T.BLKB, "BLKB", 2.0 ** 36, 0.0)):
         act(buf[:, 0:8], T.BLK[:], 8, ["BLK"], [key + "a"], scale=c0)
         act(buf[:, 8:16], T.BLK[:], 8, ["BLK"], [key + "b"], scale=c1)
-    act(T.BLKB[:], T.BLK[:], 8, ["BLK"], ["BLKB"], scale=2.0 ** 36)
-    ts(T.IH[:], T.IDF[:], 1.0, None, ALU.mult, None, 128, ["IDF"], ["IH"])
-    ts(T.IH32[:], T.IDF[:], 32.0, None, ALU.mult, None, 128, ["IDF"], ["IH32"])
-    act(T.IB[:], T.IDF[:], 128, ["IDF"], ["IB"])
-    act(T.NIB[:], T.IDF[:], 128, ["IDF"], ["NIB"], scale=-1.0)
-    act(T.POSC[:], T.POSI[:], 128, ["POSI"], ["POSC"], scale=2.0 ** 18)
+    for name, c in IDS.items():
+        act(I[name], T.IDF[:], 128, ["IDF"], [name], scale=c)
+    for name, c in IDH.items():
+        ts(I[name], T.IDF[:], c, None, ALU.mult, None, 128, ["IDF"], [name])
+    act(T.NIF[:], T.IDF[:], 128, ["IDF"], ["NIF"], scale=-1.0)
+    act(T.I15[:], T.IDF[:], 128, ["IDF"], ["I15"], scale=15.0)
+    act(T.PERM15[:], T.PERM[:], 128, ["PERM"], ["PERM15"], scale=15.0)
+    act(T.CP1[:], T.RV[:], 128, RVK, ["CP1"], scale=-2.0 ** 24)
+    tt(T.RD[:], T.RV[:], T.IO144[:, 0:128], ALU.subtract, 256, RVK + ["IO144"], ["RD"])
+    ts(T.pV[:, 384:512], T.RD[:], 2.0 ** 20, 128.0, ALU.mult, ALU.add, 128, ["RD"], ["TC"], "pV")
+    ts(T.pV[:, 0:8], T.IO8[:], 0.0, None, ALU.mult, None, 8, ["IO8"], ["pVa"], "pV")
     ms(T.SG[:, 4096:4112], 0.5, 16, ["SGz"])
     ms(T.CO[:, 4096:4112], 0.0, 16, ["COz"])
-    for b in ("CA0", "CB0", "CA1", "CB1"):
-        act(T[b][:, 4096:4104], T.IO8[:], 8, ["IO8"], [b + "z"], scale=0.0)
-    ms(T.ZK[:, :, 32], 16777216, 8, ["ZKe"])
-    ts(T.SLAB[:, :, 0], T.IO8[:], 0.0, 5196.0, ALU.mult, ALU.add, 8, ["IO8"], ["SLAB0"])
-    ms(T.TT[:, 0:1], 0.0, 1, ["TT0"])
-    ms(T.DF[:, 0:1], 0, 1, ["DF0"])
+    for buf, at, c, key in ((T.Z0, 32, 2.0 ** 20, "Z0e"), (T.SLAB, 0, 4224.0, "SLAB0"), (T.LB, 0, 1.0, "LB0"), (T.SL, 0, 1.0, "SL0")):
+        act(buf[:, :, at], T.IO8[:], 8, ["IO8"], [key], scale=0.0, bias=c)
+    ms(T.G[:, 0:1], 0.0, 1, ["G0"])
+    ms(T.LOW[:, :, 0], 0, 8, ["LOW0"])
 
-    cp(T.RAW[:, 128:256], T.PXI[:].indirect(T.FPU[:]), 128 * GA, ["PXI", "FPU"], ["RAW1"])
+    cp(T.RAWF[:, 0:128], T.LSI[:], 128, ["LSI"], ["RAW0"])
+    cp(T.RAWF[:, 128:256], T.PXI[:].indirect(T.FPU[:]), 0, ["PXI", "FPU"], ["RAW1"], gat=128)
     for h in range(2):
         c = slice(128 * h, 128 * h + 128)
-        ts(T.RM[:, c], T.RAW[:, c], 0xFFF00, None, ALU.bitwise_and, None, 128, ["RAW%d" % h], ["RM%d" % h])
-        ts(T.pV[:, c], T.RM[:, c], 15.0, T.PCOL[:, 2 + h:3 + h], ALU.mult, ALU.add, 128, ["RM%d" % h, "PC2", "PC3"], ["pVa"], "pV")
-        tt(T.RK[:, c], T.RAW[:, c], T.pV[:, c], ALU.add, 128, ["RAW%d" % h, "pVa"], ["RK%d" % h], "pV")
-    mm([(T.pS[:, 4:8, :], T.RK[:, 0:128], T.IDF[:], True, True)], 512, ["RK0", "IDF"], ["pS"], "pS")
-    act(T.L0[:], T.pS[:, 4:8, :], 128, ["pS"], ["L0"], "pS")
+        ts(T.AQ[:, c], T.RAWF[:, c], M256, -M256, ALU.add, ALU.add, 128, ["RAW%d" % h], ["AQ%d" % h])
     for v in range(NV):
         tt(T.OMB[:, 128 * v:128 * v + 128], T.OMI[:].indirect(T.LU[:, 8 * v:8 * v + 8]), T.MK[:, 0:128], ALU.mult, 256,
            ["OMI", "LU", "MK"], [("OMB", v)])
-    for c4 in range(4):
-        c = slice(256 * c4, 256 * c4 + 256)
-        bk = "pC%d" % (c4 % 2)
-        ts(T.PXM[:, c], T.PXI[:, c], 0xFFF00, None, ALU.bitwise_and, None, 256, ["PXI"], [("PXM", c4)])
-        ts(T[bk][:, 0:256], T.PXM[:, c], 15.0, T.PCOL[:, 3:4], ALU.mult, ALU.add, 256, [("PXM", c4), "PC3"], [bk], bk)
-        tt(T.PK[:, c], T.PXI[:, c], T[bk][:, 0:256], ALU.add, 256, ["PXI", bk], [("PK", c4)], bk)
-    PKK = [("PK", c4) for c4 in range(4)]
-    PTA = [("pTa", a, x) for a in range(2) for x in range(2)]
+    for c2 in range(2):
+        c = slice(512 * c2, 512 * c2 + 512)
+        bk = "pF%d" % c2
+        cp(T.PF[:, c], T.PXI[:, c], 512, ["PXI"], [("PF", c2)])
+        act(T.WO[:, c], T.PF[:, c], 512, [("PF", c2)], [("WO", c2)], bias=M256)
+        act(T.WO[:, c], T.WO[:, c], 512, [], [("WO", c2)], bias=-M256)
+        group(T[bk][:], [(T.I15[:], T.WO[:, c], 2048), (T.IDF[:], T.PF[:, c], 2048)], True, [("WO", c2), ("PF", c2), "I15", "IDF"], [bk], bk)
+        act(T.PK[:, c], T[bk][:], 512, [bk, "PC3"], [("PK", c2)], bk, bias=T.PCOL[:, 3:4])
+    PKK, PFK = [("PK", c2) for c2 in range(2)], [("PF", c2) for c2 in range(2)]
 
-    def stage(dst, dk, src, sk, half, lo, hi):
-        tt(dst[:, :, 0:2 * half:2], src[:, :, 0:half], src[:, :, half:2 * half], lo, 16 * half, [sk + "a", sk + "b"], [dk + "a"])
-        tt(dst[:, :, 1:2 * half:2], src[:, :, 0:half], src[:, :, half:2 * half], hi, 16 * half, [sk + "a", sk + "b"], [dk + "b"])
+    def stage(dst, dk, lo, hi, n, rk, bank=None):
+        tt(dst[:, :, 0:16:2], lo, hi, ALU.min, n, rk, [dk + "a"], bank)
+        tt(dst[:, :, 1:16:2], lo, hi, ALU.max, n, rk, [dk + "b"], bank)
+
+    EVK = [[("pTa", a, x) for x in range(4)] for a in range(2)]
+    ODK = [[("M", a, x) for x in range(4)] for a in range(2)]
 
     for v in range(NV):
         e = v % 2
+        last = v == NV - 1
+        AB, WT = T["AB%d" % e], T["AB%d" % (1 - e)]
         IDX, SA, SB, CA, CB = T["IDX%d" % e], T["SA%d" % e], T["SB%d" % e], T["CA%d" % e], T["CB%d" % e]
+        pix, lane = T.pK[:, 8:16, 0:16], T.pK[:, 0:8, 0:16]
         if v == 0:
-            lane, lk, pg, pk = T.L0, "L0", T.RK[:, 128:256], "RK1"
+            group(pix, [(T.AQ[:, 128:256], T.PERM15[:], 512), (T.RAWF[:, 128:256], T.PERM[:], 512), (I["IB"], T.CP3[:], 128)], True,
+                  ["AQ1", "RAW1", "PERM", "PERM15", "IB", "CP3"], ["pKb"], "pK")
         else:
-            lane, lk, pg, pk = T["RL%d" % (v - 1)], ("RL", v - 1), T.PG[:], "PG"
-            act(T.PG[:], T.PK[:].indirect(T.RN[:, 8 * v - 8:8 * v]), 128 * GA, PKK + [("RN", v - 1)], ["PG"])
-        mm([(T.pS[:, 8:16, 0:16], pg, T.PERM[:], True, True)], 512, [pk, "PERM"], ["pS"], "pS")
+            act(T.PG[:], T.PK[:].indirect(T.RN[:, 8 * v - 8:8 * v]), 0, PKK + [("RN", v - 1)], ["PG"], gat=128)
+            group(pix, [(T.PG[:], T.PERM[:], 512)], True, ["PG", "PERM"], ["pKb"], "pK")
+        act(T.PGS[:], pix, 128, ["pKb"], ["PGS"], "pK")
+        if v == 0:
+            group(lane, [(T.AQ[:, 0:128], T.I15[:], 512), (T.RAWF[:, 0:128], T.IDF[:], 512), (I["IB"], T.CP2[:], 128)], True,
+                  ["AQ0", "RAW0", "IDF", "I15", "IB", "CP2"], ["pKa"], "pK")
+        else:
+            RL = T["RL%d" % (v - 1)]
+            group(lane, [(I["IB"], T.CP1[:], 128), (I["IB"], T.CP2[:], 128)], True, ["IB", "CP1", "CP2"], ["pKa"], "pK", False)
+            ts(T.AQ[:, 0:128], RL[:], M256, -M256, ALU.add, ALU.add, 128, [("RL", v - 1)], ["AQ0"])
+            group(lane, [(T.I15[:], T.AQ[:, 0:128], 512), (T.IDF[:], RL[:], 512)], False, ["AQ0", ("RL", v - 1), "I15", "IDF"], ["pKa"], "pK")
         for k in range(4):
             a, b = k % 2, 16 * (k % 2)
             for hf in range(2):
                 for x, o in enumerate((ALU.min, ALU.max)):
                     if k == 0:
-                        i0, i1, rk, bk = lane[:, :, 8 * hf:8 * hf + 8], T.pS[:, 8:16, 8 * hf:8 * hf + 8], [lk, "pS"], ["pS"]
+                        i0, i1, rk, bk = T.PGS[:, :, 8 * hf:8 * hf + 8], T.pK[:, 0:8, 8 * hf:8 * hf + 8], ["PGS", "pKa"], ["pK"]
                     else:
                         i0, i1 = T.M0[:, :, 16 - b + 8 * hf:24 - b + 8 * hf], T.pT[:, 0:8, 16 - b + 8 * hf:24 - b + 8 * hf]
-                        rk, bk = [("M", 1 - a, y) for y in range(2)] + [("pTa", 1 - a, y) for y in range(2)], ["pT"]
+                        rk, bk = EVK[1 - a] + ODK[1 - a], ["pT"]
                     if hf == 0:
-                        tt(T.pT[:, 0:8, b + x:b + 16:2], i0, i1, o, 64, rk, [("pTa", a, x)], bk + ["pT"])
+                        tt(T.pT[:, 0:8, b + x:b + 16:2], i0, i1, o, 64, rk, EVK[a][2 * x:2 * x + 2], bk + ["pT"])
                     else:
-                        tt(T.M0[:, :, b + x:b + 16:2], i0, i1, o, 64, rk, [("M", a, x)], bk)
+                        tt(T.M0[:, :, b + x:b + 16:2], i0, i1, o, 64, rk, ODK[a][2 * x:2 * x + 2], bk)
         for x, o in enumerate((ALU.min, ALU.max)):
-            tt(T.K[:, :, x:32:2], T.M0[:, :, 16:32], T.pT[:, 0:8, 16:32], o, 128,
-               [("M", 1, y) for y in range(2)] + [("pTa", 1, y) for y in range(2)], ["K" + "ab"[x]], "pT")
+            tt(T.K[:, :, x:32:2], T.M0[:, :, 16:32], T.pT[:, 0:8, 16:32], o, 128, EVK[1] + ODK[1], ["K" + "ab"[x]], "pT")
         KK = ["Ka", "Kb"]
+        ts(T.ZF[:], T.K[:], -2048.0, M4096, ALU.add, ALU.add, 256, KK, ["ZF"])
         ts(T.YI[:], T.K[:], 2175, None, ALU.bitwise_and, None, 256, KK, ["YI"])
-        ts(T.ZK[:, :, 0:32], T.K[:], 0xFFF000, None, ALU.bitwise_and, None, 256, KK, ["ZK"])
         ts(T.YF[:], T.YI[:], -1920.0, None, ALU.add, None, 256, ["YI"], ["YF"])
-        ts(T.SLAB[:, :, 1:32], T.ZK[:, :, 1:32], 2.0 ** -19, 1099.50390625, ALU.mult, ALU.add, 248, ["ZK"], ["SLAB"])
+        act(T.SLAB[:, :, 1:32], T.ZF[:, :, 1:32], 248, ["ZF"], ["SLAB"], scale=2.0 ** -19, bias=127.50390625 - M4096 * 2.0 ** -19)
+        act(T.Z0[:, :, 0:32], T.ZF[:], 256, ["ZF"], ["Z0"], scale=2.0 ** -4, bias=-M4096 * 2.0 ** -4)
         ts(T.D0[:], T.YF[:], 0.0, 4096.0, ALU.is_lt, ALU.mult, 128, ["YF"], ["D0"])
         scan(T.A16[:], T.D0[:], T.YF[:], 0.0, ALU.add, ALU.min, 128, ["D0", "YF"], ["A16"])
         scan(T.B16[:], T.D0[:], T.YF[:], 128.0, ALU.min, ALU.max, 128, ["D0", "YF"], ["B16"])
-        for x, (src, sk, add) in enumerate(((T.A16, "A16", 61440.0 - 1100.0), (T.B16, "B16", -4096.0 - 1100.0))):
+        for x, (src, sk, add, bk, keys) in enumerate(((T.A16, "A16", 61440.0 - 128.0, "pI", [("pI", 0), ("pI", 1)]),
+                                                      (T.B16, "B16", -4096.0 - 128.0, "pS", ["pSa"]))):
             its = []
             for h in range(2):
-                o = T.pI[:, 256 * x + 128 * h:256 * x + 128 * h + 128]
-                its.append((o, src[:, h:256:2], T.IH32[:], True, False))
-                its.append((o, T.SLAB[:, :, h:32:2], T.IH[:], False, True))
-            mm(its, 512, [sk, "SLAB", "SLAB0", "IH", "IH32"], [("pI", x)], "pI")
-        for x, add in enumerate((61440.0 - 1100.0, -4096.0 - 1100.0)):
-            ts(IDX[:, 256 * x:256 * x + 256], T.pI[:, 256 * x:256 * x + 256], add, 4096.0, ALU.add, ALU.min, 256,
-               [("pI", x)], [("IDX", e, x)], "pI")
-        tt(T.LEN[:], T.ZK[:, :, 1:33], T.ZK[:, :, 0:32], ALU.subtract, 512, ["ZK", "ZKe"], ["LEN"])
-        act(T.LB[:], T.LEN[:], 256, ["LEN"], ["LB"], scale=4096.0)
-        act(T.LB[:, 0:256:32], T.ONE[:, 0:8], 8, ["ONE"], ["LB"])
-        NC = 8
-        cw, kw = 4096 // NC, 256 // NC
-        for c in range(NC):
-            act(SA[:, cw * c:cw * c + cw], T.SG[:].indirect(IDX[:, kw * c:kw * c + kw]), cw * GA,
-                ["SG", "SGz", ("IDX", e, 0)], [("SA", e, c)])
-        for c in range(NC):
-            src, dst = T.SG[:].indirect(IDX[:, 256 + kw * c:256 + kw * c + kw]), SB[:, cw * c:cw * c + cw]
+                o = T[bk][:, 4 * h:4 * h + 4, :]
+                its.append((o, T.SLAB[:, :, h:32:2], I["IB"], True, False))
+                its.append((o, src[:, h:256:2], I["IH32"], False, True))
+            mm(its, 512, [sk, "SLAB", "SLAB0", "IB", "IH32"], keys, bk)
+            ts(IDX[:, 256 * x:256 * x + 256], T[bk][:, 0:8, :], add, 4096.0, ALU.add, ALU.min, 256, keys, [("IDX", e, x)], bk)
+        group(T.pI[:, 0:8, :], [(T.IDF[:], T.Z0[:, :, 1:33], 1024), (T.NIF[:], T.Z0[:, :, 0:32], 1024)], True,
+              ["Z0", "Z0e", "IDF", "NIF"], [("pI", 0), ("pI", 1)], "pI")
+        act(T.LB[:, :, 1:32], T.pI[:, 0:8, 1:32], 248, [("pI", 0), ("pI", 1)], ["LB"], "pI", scale=65536.0)
+        if not last:
+            group(T.pK[:, 8:16, :], [(I["IH"], T.B16[:], 256), (I["NIH"], T.A16[:], 256), (I["NI2"], T.C1024[:], 256)], True,
+                  ["A16", "B16", "IH", "NIH", "NI2", "C1024"], ["pKb"], "pK")
+            group(T.pK[:, 0:8, :], [(T.IDF[:], T.Z0[:, :, 0:32], 1024), (I["IH"], T.A16[:], 256), (I["I2"], T.C1024[:], 256)], True,
+                  ["Z0", "A16", "IDF", "IH", "I2", "C1024"], ["pKa"], "pK", False)
+        def piece(buf, c, n):
+            return buf[:, 512 * (c % 4):512 * (c % 4 + n), c // 4]
+
+        for c, n in runs(0, 8, SGW[v]):
+            act(piece(SA, c, n), T.SG[:].indirect(IDX[:, 32 * c:32 * (c + n)]), 0, ["SG", "SGz", ("IDX", e, 0)],
+                [("SA", e, cc) for cc in range(c, c + n)], gat=512 * n)
+        for c, n in runs(0, VSHARE[v], SGW[v]) + runs(VSHARE[v], 8, SGW[v]):
+            src, rk = T.SG[:].indirect(IDX[:, 256 + 32 * c:256 + 32 * (c + n)]), ["SG", "SGz", ("IDX", e, 1)]
+            wk = [("SB", e, cc) for cc in range(c, c + n)]
             if VADD[v]:
-                tt(dst, src, SA[:, cw * c:cw * c + cw], ALU.add, cw * 2, ["SG", "SGz", ("IDX", e, 1), ("SA", e, c)], [("SB", e, c)])
+                tt(piece(SB, c, n), src, piece(SA, c, n), ALU.add, 1024 * n, rk + [("SA", e, cc) for cc in range(c, c + n)], wk)
             elif c < VSHARE[v]:
-                cp(dst, src, cw * GA, ["SG", "SGz", ("IDX", e, 1)], [("SB", e, c)])
+                cp(piece(SB, c, n), src, 0, rk, wk, gat=512 * n)
             else:
-                act(dst, src, cw * GA, ["SG", "SGz", ("IDX", e, 1)], [("SB", e, c)])
-        SAK, SBK = [("SA", e, c) for c in range(NC)], [("SB", e, c) for c in range(NC)]
-        mm([(T.pS[:], T.IB[:], T.CZ[:], True, False), (T.pS[:, 8:16, :], T.IH[:], T.B16[:], False, False),
-            (T.pS[:, 0:8, 0], T.OMB[:, 128 * v:128 * v + 128], T.BLKB[:], False, False)], 1024,
-           ["IB", "IH", "CZ", "B16", ("OMB", v), "BLKB"], ["pS"], "pS")
-        ra, rak = (T.RMA2, "RMA2") if VADD[v] else (T.RMA, "RMA")
-        for src, keys, rm, rk, x in ((SA, SAK, ra, rak, 0), (SB, SBK, T.RMB, "RMB", 1)):
-            for h in range(2):
-                mm([(T.pS[:, :, 2 * j + h], src[:, 2048 * h + j:2048 * h + 2048:16], rm[:], False, x + h == 2 and j == 15)
-                    for j in range(1 - h, 16)], 16 * 64, keys[NC // 2 * h:NC // 2 * (h + 1)] + [rk + "a", rk + "b"], ["pS"], "pS")
+                act(piece(SB, c, n), src, 0, rk, wk, gat=512 * n)
+        SAK, SBK = [("SA", e, c) for c in range(8)], [("SB", e, c) for c in range(8)]
+        nr = 8 if last else 16
+        mm([(T.pS[:, 0:nr, 0], T.OMB[:, 128 * v:128 * v + 128], T.BLKB[:, 0:nr], True, False)], 256,
+           [("OMB", v), "BLKBa", "BLKBb"], ["pSa", "pSb"], "pS")
+        sums = ((SA, SAK, T.RMA, "RMA"), (SB, SBK, T.RMB, "RMB"))[VADD[v]:]
+        for h in range(2):
+            for x, (src, keys, rm, rk) in enumerate(sums):
+                mm([(T.pS[:, 0:nr, s], src[:, s // 2:2048:16, h], rm[:, 0:nr], False, x == len(sums) - 1 and s == 31)
+                    for s in range(2 - h, 32, 2)], 16 * 64, keys[4 * h:4 * h + 4] + [rk + "a", rk + "b"], ["pSa", "pSb"], "pS")
         if not VADD[v]:
             dma("G", g, SB[:], SA[:], 2 * 1048576, SAK, SBK, "add%d" % v, accum_op=ALU.add, max_dma_last_dim=4096)
-        tt(T.W[:], T.LB[:], T.pS[:, 0:8, :], ALU.mult, 256, ["LB", "pS"], ["W"], "pS")
-        if v < NV - 1:
-            tt(T.XI[:], T.A16[:], T.pS[:, 8:16, :], ALU.max, 256, ["A16", "pS"], ["XI"], "pS")
-        scan(T.pV[:, 0:256], T.MASK[:, 0:256], T.W[:], 0.0, ALU.mult, ALU.add, 256, ["MASK", "W"], ["pVa"], "pV")
-        if v < NV - 1:
-            ts(T.DEN[:], T.XI[:], 255, None, ALU.bitwise_and, None, 256, ["XI"], ["DEN"])
-        tt(T.TT[:, 1:256], T.LB[:, 1:256], T.pV[:, 0:255], ALU.min, 256, ["LB", "pVa"], ["TT"], "pV")
-        act(T.SL[:], T.TT[:], 256, ["TT", "TT0"], ["SL"], func=ACT.Relu, scale=2.0 ** -41)
-        act(T.SL[:, 0:256:32], T.ONE[:, 0:8], 8, ["ONE"], ["SL"])
-        if v < NV - 1:
-            tt(T.pV[:, 256:512], T.DEN[:], T.ZK[:, :, 0:32], ALU.add, 512, ["DEN", "ZK"], ["pVb"], "pV")
-            tt(T.LE[:], T.TT[:], T.pV[:, 256:512], ALU.min, 256, ["TT", "TT0", "pVb"], ["LE"], "pV")
-            scan(T.G[:], T.MASK[:, 0:256], T.LE[:], 0.0, ALU.mult, ALU.max, 256, ["MASK", "LE"], ["G"])
-            cp(T.GI[:], T.G[:, 31:256:32], 8, ["G"], ["GI"])
-            ts(T.NB[:], T.GI[:], 127, None, ALU.bitwise_and, None, 8, ["GI"], ["NB"])
-            ts(T.NA[:], T.GI[:], 21, None, ALU.arith_shift_right, None, 8, ["GI"], ["NA"])
-            ts(T.NB8[:], T.NB[:], 8.0, None, ALU.mult, None, 8, ["NB"], ["NB8"])
-            tt(T.NM[:], T.NA[:], T.NB8[:], ALU.add, 16, ["NA", "NB8"], ["NM"])
+        tt(T.W[:], T.LB[:], T.pS[:, 0:8, :], ALU.mult, 256, ["LB", "LB0", "pSa"], ["W"], "pS")
+        if not last:
+            ts(T.SN[:], T.pS[:, 8:16, :], 0.5, None, ALU.is_gt, None, 256, ["pSb"], ["SN"], "pS")
+        scan(T.pV[:, 1:257], T.MASK[:, 0:256], T.W[:], 0.0, ALU.mult, ALU.add, 256, ["MASK", "W"], ["pVa"], "pV")
+        if not last:
+            tt(T.UU[:], T.SN[:], T.pK[:, 8:16, :], ALU.mult, 256, ["SN", "pKb"], ["UU"], "pK")
+            group(T.pK[:, 0:8, :], [(I["IB"], T.UU[:], 256)], False, ["IB", "UU"], ["pKa"], "pK")
+        tt(T.TT[:], T.LB[:], T.pV[:, 0:256], ALU.min, 256, ["LB", "LB0", "pVa"], ["TT"], "pV")
+        act(T.SL[:, :, 1:32], T.TT[:, :, 1:32], 248, ["TT"], ["SL"], func=ACT.Relu, scale=2.0 ** -41)
+        hk, lk = [("pI", 0), ("pI", 1)], [("pI", 2), ("pI", 3)]
+        mm([(T.pI[:, 4 * h:4 * h + 4, :], T.SL[:, :, h:32:2], T.NIF[:], True, True) for h in range(2)], 1024, ["SL", "SL0", "NIF"], hk, "pI")
+        act(T.HI[:], T.pI[:, 0:8, :], 256, hk, ["HI"], "pI")
+        mm([(T.pI[:, 8:16, :], I["NIB"], T.HI[:], True, False)]
+           + [(T.pI[:, 8 + 4 * h:12 + 4 * h, :], T.SL[:, :, h:32:2], T.NIF[:], False, h == 1) for h in range(2)], 1280,
+           ["SL", "SL0", "NIF", "NIB", "HI"], lk, "pI")
+        act(T.LO[:], T.pI[:, 8:16, :], 256, lk, ["LO"], "pI")
+        if not last:
+            tt(T.LE[:], T.TT[:], T.pK[:, 0:8, :], ALU.min, 256, ["TT", "pKa"], ["LE"], "pK")
+            scan(T.G[:, 1:257], T.MASK[:, 0:256], T.LE[:], 0.0, ALU.mult, ALU.max, 256, ["MASK", "LE"], ["G"])
+            ts(T.GI[:], T.G[:, 32:257:32], 8.0, None, ALU.mult, None, 8, ["G"], ["GI"])
+            ts(T.NB[:], T.GI[:], 0x3F8, None, ALU.bitwise_and, None, 8, ["GI"], ["NB"])
+            ts(T.NA[:], T.GI[:], 20, None, ALU.arith_shift_right, None, 8, ["GI"], ["NA"])
+            tt(T.NM[:], T.NA[:], T.NB[:], ALU.add, 16, ["NA", "NB"], ["NM"])
             tt(T.NX[:], T.NM[:].indirect(T.LU[:, 48:57]), T.MK[:], ALU.mult, 288, ["NM", "LU", "MK"], ["NX"])
             mm([(T.pS[:, 0, 0:8], T.NX[:, 16:144], T.BLK[:], True, True), (T.pS[:, 0, 8:16], T.NX[:, 0:128], T.BLK[:], True, True)],
-               512, ["NX", "BLK"], ["pS"], "pS")
-            cp(T.NU[:, 16 * v:16 * v + 16], T.pS[:, 0, 0:16], 16, ["pS"], [("NU", v)], "pS")
+               512, ["NX", "BLK"], ["pSa"], "pS")
+            cp(T.NU[:, 16 * v:16 * v + 16], T.pS[:, 0, 0:16], 16, ["pSa"], [("NU", v)], "pS")
             send(T.NU[:, 16 * v + 8:16 * v + 16], T.RN[:, 8 * v:8 * v + 8], 2048, [("NU", v)], [("RN", v)], "rn%d" % v)
-            act(T.PG2[:], T.PK[:].indirect(T.NU[:, 16 * v:16 * v + 8]), 128 * GA, PKK + [("NU", v)], ["PG2"])
-            mm([(T.pS[:, 4:8, :], T.PG2[:], T.IDF[:], True, False), (T.pS[:, 4:8, :], T.IB[:], T.CY[:], False, True)], 640,
-               ["PG2", "IDF", "IB", "CY"], ["pS"], "pS")
-            act(T.Y2[:], T.G[:].indirect(T.LU[:, 40:48]), 128 * GA, ["G", "LU"], ["Y2"], scale=-1.0, bias=-2048.0)
-            mm([(T.pS[:, 8:16, 0:16], T.PG2[:], T.IDF[:], True, False), (T.pS[:, 8:16, 0:16], T.IB[:], T.CY[:], False, False),
-                (T.pS[:, 8:16, 0:16], T.IDF[:], T.Y2[:], False, True)], 1152, ["PG2", "IDF", "IB", "CY", "Y2"], ["pS2"], "pS")
-            act(T.U2[:], T.pS[:, 8:16, 0:16], 128, ["pS2"], ["U2"], "pS", func=ACT.Sign)
+            tt(T.DF[:], T.G[:, 1:257], T.G[:, 0:256], ALU.subtract, 512, ["G", "G0"], ["DF"])
+            ts(T.LOW[:, :, 1:32], T.DF[:, :, 1:32], 255, None, ALU.bitwise_and, None, 248, ["DF"], ["LOW"])
+            ts(T.INV[:], T.LOW[:], 0.0, 2.0 ** -5, ALU.is_equal, ALU.mult, 256, ["LOW", "LOW0"], ["INV"])
+            tt(T.pV[:, 0:256], T.LOW[:], T.pT[:, 8:16, :], ALU.min, 256, ["LOW", "LOW0", "SC"], ["pVa"], ["pV", "pT"])
+            act(T.EE[:], T.INV[:], 256, ["INV"], ["EE"], scale=32.0 * TOP)
+            scan(T.CI[:], T.MASKB[:], T.INV[:], 0.0, ALU.mult, ALU.add, 128, ["MASKB", "INV"], ["CI"])
+            tt(T.YY[:], T.pV[:, 0:256], T.CI[:], ALU.subtract, 256, ["pVa", "CI"], ["YY"], "pV")
+            tt(T.XP[:], T.EE[:], T.pK[:, 0:8, :], ALU.max, 256, ["EE", "pKa"], ["XP"], "pK")
+            R = T.pS[:, 8:16, :]
+            group(R, [(I["IC"], T.C1024[:], 256)], True, ["IC", "C1024"], ["pSb"], "pS", False)
+            group(R, [(I["I28"], T.YY[:], 256)], False, ["I28", "YY"], ["pSb"], "pS", False)
+            for k, (c1, c0, ident) in enumerate(((-64.0, 769.0, "I3"), (-16.0, 384.75, "I3"), (-4.0, 192.4375, "I3"), (-4.0, 384.9375, "I1"))):
+                f = T.FL[:, 256 * k:256 * k + 256]
+                if FLOOR_V[k]:
+                    ts(f, T.YY[:], c1, c0, ALU.mult, ALU.add, 128, ["YY"], [("FL", k)])
+                else:
+                    act(f, T.YY[:], 256, ["YY"], [("FL", k)], scale=c1, bias=c0)
+                group(R, [(I[ident], f, 256)] + [(I["NI8"], T.C1024[:], 256)] * (k == 3), False, [ident, ("FL", k), "NI8"], ["pSb"], "pS", k == 3)
+            tt(T.pT[:, 0:8, 0:16], T.XP[:, :, 0:32:2], T.pS[:, 8:16, 0:32:2], ALU.add, 128, ["XP", "pSb"], EVK[0], ["pS", "pT"])
+            tt(T.M0[:, :, 0:16], T.XP[:, :, 1:32:2], T.pS[:, 8:16, 1:32:2], ALU.add, 128, ["XP", "pSb"], ODK[0], "pS")
+            for k in range(4):
+                a, b, d = k % 2, 16 * (k % 2), 16 - 16 * (k % 2)
+                for par in range(2):
+                    for x, o in enumerate((ALU.min, ALU.max)):
+                        dst = T.M0[:, :, d + 8 * x:d + 8 * x + 8] if par else T.pT[:, 0:8, d + 8 * x:d + 8 * x + 8]
+                        tt(dst, T.M0[:, :, b + par:b + 16:2], T.pT[:, 0:8, b + par:b + 16:2], o, 64, EVK[a] + ODK[a],
+                           (ODK if par else EVK)[1 - a][2 * x:2 * x + 2], "pT")
+            tt(T.pV[:, 0:128], T.M0[:, :, 0:16], T.pT[:, 0:8, 0:16], ALU.min, 128, EVK[0] + ODK[0], ["pVa"], ["pT", "pV"])
+            act(T.PG2[:], T.PF[:].indirect(T.NU[:, 16 * v:16 * v + 8]), 0, PFK + [("NU", v)], ["PG2"], bias=-128.0, gat=128)
+            act(T.Y2[:], T.G[:, 0:257].indirect(T.LU[:, 64:72]), 0, ["G", "G0", "LU"], ["Y2"], bias=-128.0, gat=128)
+            group(T.pI[:, 0:4, :], [(T.Y2[:], T.NIF[:], 512), (T.IDF[:], T.PG2[:], 512)], True, ["PG2", "Y2", "IDF", "NIF"], [("pI", 0)], "pI")
+            act(T.U2[:], T.pI[:, 0:4, :], 128, [("pI", 0)], ["U2"], "pI", func=ACT.Sign)
             act(T.V2[:], T.U2[:], 128, ["U2"], ["V2"], func=ACT.Relu, scale=-float(FILL))
-            tt(T.DF[:, 1:256], T.G[:, 1:256], T.G[:, 0:255], ALU.subtract, 510, ["G", "DF0"], ["DF"])
-            ts(T.LOW[:], T.DF[:], 4095, None, ALU.bitwise_and, None, 256, ["DF", "DF0"], ["LOW"])
-            ts(T.EQ[:], T.LOW[:], 0.0, 128.0, ALU.is_equal, ALU.mult, 256, ["LOW"], ["EQ"])
-            act(T.pT[:, 8:16, :], T.EQ[:], 256, ["EQ"], ["pTb"], "pT", scale=-2.0 ** 17, bias=16777216.0)
-            scan(T.pV[:, 0:256], T.EQ[:], T.MASK[:, 0:256], 0.0, ALU.add, ALU.mult, 256, ["EQ", "MASK"], ["pVa"], "pV")
-            tt(T.T2[:], T.G[:], T.pV[:, 0:256], ALU.add, 256, ["G", "pVa"], ["T2"], "pV")
-            act(T.C8[:], T.pV[:, 31:256:32], 8, ["pVa"], ["C8"], "pV", scale=2.0 ** 18)
-            tt(T.VV[:], T.T2[:], T.pT[:, 8:16, :], ALU.min, 256, ["T2", "pTb"], ["VV"], "pT")
-            for k in range(5):
-                sh = 1 << k
-                n = 8 * (32 - sh)
-                ts(T.MB[:, :, sh:32], T.VV[:, :, sh:32], 7 + k, 1, ALU.arith_shift_right, ALU.bitwise_and, n, ["VV"], ["MB"])
-                tt(T.pT[:, 0:8, sh:32], T.VV[:, :, sh:32], T.MB[:, :, sh:32], ALU.mult, 2 * n, ["VV", "MB"], PTA, "pT")
-                tt(T.VV[:, :, 0:32 - sh], T.VV[:, :, 0:32 - sh], T.pT[:, 0:8, sh:32], ALU.max, n, ["VV"] + PTA, ["VV"], "pT")
-            ts(T.XS[:], T.VV[:, :, 0:16], 0xFFF07F, None, ALU.bitwise_and, None, 128, ["VV"], ["XS"])
-            tt(T.Q0[:], T.V2[:], T.pS[:, 4:8, :], ALU.max, 128, ["V2", "pS"], ["Q0a", "Q0b"], "pS")
-            act(T.UJ[:], T.C8[:].indirect(T.LU[:, 0:8]), 128 * GA, ["C8", "LU"], ["UJ"])
-            mm([(T.pS[:, 8:16, 16:32], T.IB[:], T.UJ[:], True, False), (T.pS[:, 8:16, 16:32], T.IB[:], T.POSC[:], False, True)], 256,
-               ["IB", "UJ", "POSC"], ["pS3"], "pS")
-            tt(T.XM[:], T.XS[:], T.pS[:, 8:16, 16:32], ALU.max, 128, ["XS", "pS3"], ["XM"], "pS")
-            for k in range(2):
-                stage(T.Q1, "Q1", T.Q0, "Q0", 8, ALU.max, ALU.min)
-                stage(T.Q0, "Q0", T.Q1, "Q1", 8, ALU.max, ALU.min)
-            tt(T.Q1[:], T.Q0[:], T.XM[:], ALU.min, 256, ["Q0a", "Q0b", "XM"], ["Q1a", "Q1b"])
-            stage(T.Q0, "Q0", T.Q1, "Q1", 8, ALU.min, ALU.max)
-            stage(T.Q1, "Q1", T.Q0, "Q0", 8, ALU.min, ALU.max)
-            stage(T.Q0, "Q0", T.Q1, "Q1", 8, ALU.min, ALU.max)
-            stage(T["OUT%d" % v], "OUT%d" % v, T.Q0, "Q0", 8, ALU.min, ALU.max)
-            send(T["OUT%d" % v][:], T["RL%d" % v][:], 65536, ["OUT%da" % v, "OUT%db" % v], [("RL", v)], "rl%d" % v)
+            act(T.UJ[:], T.CI[:].indirect(T.LU[:, 40:48]), 0, ["CI", "LU"], ["UJ"], func=ACT.Relu, scale=32.0, bias=-16.0, gat=128)
+            ta, tk = T.pI[:, 8:16, 0:16], [("pI", 2), ("pI", 3)]
+            for out in (T.pI[:, 8:16, 16:32], ta):
+                group(out, [(I["I1"], T.JC[:], 128), (I["NI1"], T.UJ[:], 128), (T.U2[:], T.BDG[:], 128), (T.U2[:], I["IW"], 128)], True,
+                      ["I1", "NI1", "JC", "UJ", "U2", "BDG", "IW"], tk, "pI", out is not ta)
+            act(T.WN[:], T.pI[:, 8:16, 16:32], 128, tk, ["WN"], "pI", func=ACT.Sign, scale=2.0 ** -20, bias=-7.5)
+            tt(T.T0[:], T.PG2[:], T.V2[:], ALU.max, 256, ["PG2", "V2"], ["T0"])
+            group(ta, [(I["IW"], T.WN[:], 128), (I["I64"], T.WN[:], 128), (T.U2[:], I["I64"], 128), (T.T0[:], T.IDF[:], 512)], False,
+                  ["IW", "I64", "WN", "U2", "T0", "IDF"], tk, "pI")
+            act(T.TS[:], T.pI[:, 8:16, 8:16], 64, tk, ["TS"], "pI")
+            stage(T.Q1, "Q1", T.TS[:], T.pI[:, 8:16, 0:8], 64, tk + ["TS"], "pI")
+            for dst, dk, src, sk in ((T.Q0, "Q0", T.Q1, "Q1"), (T.Q1, "Q1", T.Q0, "Q0"), (T.Q0, "Q0", T.Q1, "Q1")):
+                stage(dst, dk, src[:, :, 0:8], src[:, :, 8:16], 128, [sk + "a", sk + "b"])
+            tt(T.Q1[:], T.Q0[:], T.pV[:, 384:512], ALU.add, 128, ["Q0a", "Q0b", "TC"], ["Q1a", "Q1b"], "pV")
+            tt(T["OUT%d" % v][:], T.Q1[:], T.pV[:, 0:128], ALU.min, 128, ["Q1a", "Q1b", "pVa"], [("OUT", v)], "pV")
+            send(T["OUT%d" % v][:], T["RL%d" % v][:], 65536, [("OUT", v)], [("RL", v)], "rl%d" % v)
         for x, (dst, key) in enumerate(((CA, "CA"), (CB, "CB"))):
-            for c in range(8):
-                c4, h = c // 2, c % 2
-                o = 256 * x + 128 * h + 32 * c4
-                act(dst[:, 1024 * c4 + h:1024 * c4 + 1024:2], T.CO[:].indirect(IDX[:, o:o + 32]), 512 * GA,
-                    ["CO", "COz", ("IDX", e, x)], [(key, e, c)])
-        mm([(T.pI[:, 128 * h:128 * h + 128], T.SL[:, h:256:2], T.IDF[:], True, True) for h in range(2)], 1024,
-           ["SL", "IDF"], [("pI", 0)], "pI")
-        act(T.HI[:], T.pI[:, 0:256], 256, [("pI", 0)], ["HI"], "pI")
-        its = []
-        for h in range(2):
-            its.append((T.pI[:, 256 + 128 * h:384 + 128 * h], T.SL[:, h:256:2], T.IDF[:], True, False))
-            its.append((T.pI[:, 256 + 128 * h:384 + 128 * h], T.NIB[:], T.HI[:, 128 * h:128 * h + 128], False, True))
-        mm(its, 1280, ["SL", "IDF", "NIB", "HI"], [("pI", 1)], "pI")
-        act(T.LO[:], T.pI[:, 256:512], 256, [("pI", 1)], ["LO"], "pI")
-        for jp in range(8):
-            bk = "pL%d" % (jp % 2)
-            its = []
-            for jj in range(2):
-                j = 2 * jp + jj
-                its.append((T[bk][:, 256 * jj:256 * jj + 256], T.SEL[:, 128 * j:128 * j + 128], T.HI[:], True, False))
-                its.append((T[bk][:, 256 * jj:256 * jj + 256], T.SEL[:, 128 * j:128 * j + 128], T.LO[:], False, True))
-            mm(its, 1024, ["SEL", "HI", "LO"], [bk], bk)
-            for jj in range(2):
-                j = 2 * jp + jj
-                tt(T.AB[:, j:4096:16], SB[:, j:4096:16], T[bk][:, 256 * jj:256 * jj + 256], ALU.mult, 256, SBK + [bk], [("AB", j)], bk)
-        ABK = [("AB", j) for j in range(16)]
-        for c in range(8):
-            bk = "pC%d" % (c % 2)
-            lo = 512 * c
-            if c % 2 == 0:
+            for c4, n in runs(0, 4, COW[v]):
                 for h in range(2):
-                    act(T.OA[:, lo + h:lo + 1024:2], T.AB[:, 2048 * h + lo // 2:2048 * h + lo // 2 + 512], 512, ABK,
-                        [("OA", c // 2, h)], scale=-1.0, bias=1.0)
-            rk = [(key, e, 2 * c4 + h) for key in ("CA", "CB") for c4 in set([c // 2, min((c + 1) // 2, 3)]) for h in range(2)]
-            mm([(T[bk][:], T.IB[:], CA[:, lo + 1:lo + 513], True, False), (T[bk][:], T.IB[:], CB[:, lo + 1:lo + 513], False, False),
-                (T[bk][:], T.NIB[:], CA[:, lo:lo + 512], False, False), (T[bk][:], T.NIB[:], CB[:, lo:lo + 512], False, True)],
-               2048, rk + ["CA%dz" % e, "CB%dz" % e, "IB", "NIB"], [bk], bk)
+                    o = 256 * x + 128 * h + 32 * c4
+                    act(dst[:, 1024 * c4 + h:1024 * (c4 + n):2], T.CO[:].indirect(IDX[:, o:o + 32 * n]), 0,
+                        ["CO", "COz", ("IDX", e, x)], [(key, e, 2 * cc + h) for cc in range(c4, c4 + n)], gat=512 * n)
+        for hh in range(2 * CADD[v]):
+            c = slice(2048 * hh, 2048 * hh + 2048)
+            dma("G", g, CB[:, c], CA[:, c], 1048576, [("CA", e, cc) for cc in range(4 * hh, 4 * hh + 4)],
+                [("CB", e, cc) for cc in range(4 * hh, 4 * hh + 4)], "cadd%d" % (2 * v + hh), accum_op=ALU.add, max_dma_last_dim=4096)
+        cols = (("CA", CA), ("CB", CB))[CADD[v]:]
+        ABH = [("ABh", e, c) for c in range(8)]
+        for jp in range(8):
+            bk = "pF%d" % (jp % 2)
+            its = []
+            for half in range(2):
+                j = jp + 8 * half
+                its.append((T[bk][:, half:512:2], T.SEL[:, 128 * j:128 * j + 128], T.HI[:], True, False))
+                its.append((T[bk][:, half:512:2], T.SEL[:, 128 * j:128 * j + 128], T.LO[:], False, True))
+            mm(its, 1024, ["SEL", "HI", "LO"], [bk], bk)
+            for h in range(2):
+                j = 2 * jp + h
+                tt(AB[:, j:4096:16], SB[:, jp:2048:8, h], T[bk][:, 256 * h:256 * h + 256], ALU.mult, 256, SBK + [bk], [("AB", e, j)], bk)
+        ABK = [("AB", e, j) for j in range(16)]
+        ns = ONE_S[v]
+        for c, n in runs(0, ns, ONEW[v]):
+            act(AB[:, 512 * c:512 * (c + n)], AB[:, 512 * c:512 * (c + n)], 512 * n, ABK, ABH[c:c + n], bias=1.0)
+        if ns < 8:
+            dma("G", g, AB[:, 512 * ns:4096], T.ONES[:, 0:4096 - 512 * ns], (8 - ns) * 2 * 262144, ABK + ["ONES"], ABH[ns:],
+                "one%d" % v, accum_op=ALU.add, max_dma_last_dim=4096)
+        for c in range(8):
+            bk = "pF%d" % (c % 2)
+            lo = 512 * c
+            its = ([(T[bk][:], I["NIH"], buf[:, lo:lo + 512]) for key, buf in cols]
+                   + [(T[bk][:, 0:511], I["IH"], buf[:, lo + 1:lo + 512]) for key, buf in cols])
+            mm([it + (k == 0, k == len(its) - 1) for k, it in enumerate(its)], 512 * len(its),
+               [(key, e, c // 2 * 2 + h) for key, buf in cols for h in range(2)] + ["IH", "NIH"], [bk], bk)
             back = slice(lo + 511, lo - 1 if lo else None, -1)
-            ok = [("OA", c // 2, 0), ("OA", c // 2, 1)]
-            scan(T.WO[:, back], T[bk][:, ::-1], T.OA[:, back], 0.0, ALU.add, ALU.mult, 512, ok + [bk], [("WO", c)], bk)
+            ok = ABK + [ABH[c]]
+            scan(T.WO[:, back], T[bk][:, ::-1], AB[:, back], 0.0, ALU.add, ALU.mult, 512, ok + [bk], [("WO", c)], bk)
             if not YT_PE[v]:
-                scan(T.WT[:, lo:lo + 512], T.MASK[:, 0:512], T.OA[:, lo:lo + 512], 0.0, ALU.mult, ALU.add, 512, ok + ["MASK"], [("WT", c)])
+                scan(WT[:, lo:lo + 512], T.MASK[:], AB[:, lo:lo + 512], 0.0, ALU.mult, ALU.add, 512,
+                     ok + ["MASK", ("YT", v - 1), ("YC", v - 1)], [("WT", c)])
         yo = slice(128 * v, 128 * v + 128)
-        mm([(T.pC0[:, 0:128], T.IB[:], CA[:, 1:4096:32], True, False), (T.pC0[:, 0:128], T.IB[:], CB[:, 1:4096:32], False, True)], 256,
-           [(key, e, cc) for key in ("CA", "CB") for cc in range(8)] + ["IB"], ["pC0"], "pC0")
-        tt(T.YC[:, yo], T.WO[:, 1:4096:32], T.pC0[:, 0:128], ALU.add, 128, [("WO", c) for c in range(8)] + ["pC0"], [("YC", v)], "pC0")
         if YT_PE[v]:
             for j in range(16):
-                ss = [s for s in (j, j + 16) if s]
-                mm([(T.pL0[:, 0:128], T.IDF[:], T.AB[:, 2048 * (s // 16) + j:2048 * (s // 16) + 2048:16], s == 16, s == 31) for s in ss], 512 * len(ss),
-                   ABK + ["IDF"], ["pL0"], "pL0")
-            act(T.YT[:, yo], T.pL0[:, 0:128], 128, ["pL0"], [("YT", v)], "pL0", scale=8.0)
+                ss = [s for s in (2 * j, 2 * j + 1) if s]
+                mm([(T.pY[:, 0:128], T.IDF[:], AB[:, s:4096:32], s == 1, s == 31) for s in ss], 512 * len(ss), ABK + ABH + ["IDF"], ["pY"], "pY")
+            act(T.YT[:, yo], T.pY[:, 0:128], 128, ["pY"], [("YT", v)], "pY", scale=-8.0, bias=248.0)
         else:
-            act(T.YT[:, yo], T.WT[:, 31:4096:32], 128, [("WT", c) for c in range(8)], [("YT", v)], scale=-8.0, bias=248.0)
+            act(T.YT[:, yo], WT[:, 31:4096:32], 128, [("WT", c) for c in range(8)], [("YT", v)], scale=-8.0, bias=248.0)
+        group(T.pY[:, 128:256], [(I["IH"], buf[:, 1:4096:32], 128) for key, buf in cols], True,
+              [(key, e, cc) for key, buf in cols for cc in range(8)] + ["IH"], ["pYc"], "pY")
+        tt(T.YC[:, yo], T.WO[:, 1:4096:32], T.pY[:, 128:256], ALU.add, 128, [("WO", c) for c in range(8)] + ["pYc"], [("YC", v)], "pY")
         dma("Y", Y, T.yc[:, yo], T.YC[:, yo], 65536, [("YC", v)], [], "dst")
         dma("Y", Y, T.yt[:, yo], T.YT[:, yo], 65536, [("YT", v)], [], "dst")
     return ops, n_out
@@ -531,10 +670,13 @@ def rank_program(g, core, T, topo):
     for i in order:
         o = ops[i]
         q = o["q"]
-        if q == "R":
-            o["at"] = (o["sem"], o["inc"])
-            o["clock"] = {o["sem"]: o["inc"]}
-            count[o["sem"]] = o["inc"]
+        if q == "D":
+            if o["cost"][3] == "send":
+                o["at"] = (o["sem"], o["inc"])
+                o["clock"] = {o["sem"]: o["inc"]}
+                count[o["sem"]] = o["inc"]
+            else:
+                o["at"], o["clock"] = ops[i - 1]["at"], ops[i - 1]["clock"]
             continue
         kn = known[q]
         need = {}

@@ -4,15 +4,14 @@ from concourse.mybir import dt, AluOpType, AxisListType, ActivationFunctionType
 ALU = AluOpType
 ACT = ActivationFunctionType
 NV = 5
-FILL = 4095 * 256
 TOP = 2.0 ** 20 - 1
 M256 = 1.5 * 2.0 ** 31
 M4096 = 2.0 ** 35 + 8192
 VADD = (0, 0, 0, 0, 1)
-VSHARE = (8, 7, 7, 7, 8)
+VSHARE = (8, 8, 8, 8, 8)
 YT_PE = (1, 1, 1, 1, 0)
-ONE_S = (4, 4, 4, 8, 8)
-SGW, COW, ONEW = (2, 2, 2, 2, 1), (1, 1, 1, 1, 1), (2, 2, 2, 2, 1)
+ONE_S = (4, 4, 4, 6, 8)
+SGW, COW, ONEW = (4, 4, 4, 4, 1), (2, 2, 2, 2, 1), (2, 2, 2, 2, 1)
 CADD = (1, 1, 1, 1, 0)
 FLOOR_V = (1, 1, 1, 1)
 
@@ -25,7 +24,9 @@ def _sb(name, shape, d):
 
 
 IDS = {"IB": 1.0, "NIB": -1.0, "I3": 3 * 2.0 ** 20, "I1": 2.0 ** 20, "NI1": -2.0 ** 20, "I28": 2.0 ** 28,
-       "IC": -4.3125 * 2.0 ** 20, "NI8": -0.125, "IW": -2.0 ** 23, "I64": 64.0, "I2": 2.0, "NI2": -2.0}
+       "IC": -4.3125 * 2.0 ** 20, "NI8": -0.125, "IW": -2.0 ** 23, "I64": 64.0, "I2": 2.0,
+       "N21": -2.0 ** 21, "NHALF": -0.5, "I23": 2.0 ** 23, "N128": -128.0}
+EARLY_IDS = ("IB", "I2", "N21", "NHALF")
 IDH = {"IH32": 32.0, "IH": 1.0, "NIH": -1.0}
 
 for _n, _s, _d in [
@@ -33,22 +34,22 @@ for _n, _s, _d in [
     ("LSI", [128], I32), ("RAWF", [256], F32), ("AQ", [256], F32),
     ("FPI", [8], I32), ("FPU", [8], U16), ("OMI", [40], I32), ("OMB", [640], F32),
     ("ONE", [128], F32), ("IDF", [128], F32), ("NIF", [128], F32), ("I15", [128], F32), ("PERM", [128], F32), ("PERM15", [128], F32),
-    ("IDS", [128 * len(IDS)], BF), ("IDH", [128 * len(IDH)], F16), ("SEL", [2048], BF), ("ONES", [2048], BF),
+    ("IDS", [128 * len(IDS)], BF), ("IDH", [128 * len(IDH)], F16), ("ZB", [128], BF), ("SEL", [2048], BF), ("ONES", [2048], BF),
     ("PI", [8], I32), ("PJ", [8], I32), ("PCOL", [8], F32), ("IO8", [8], F32), ("IO144", [144], F32), ("MK", [144], F32),
     ("BLK", [8], F32), ("BLKB", [16], F32), ("RMA", [16], BF), ("RMB", [16], BF),
     ("C1024", [256], BF), ("MI", [512], F32), ("MASK", [512], F32), ("MASKB", [256], BF),
     ("RV", [8, 4, 4], F32), ("RD", [128], F32), ("CP1", [128], BF), ("CP2", [128], BF), ("CP3", [128], BF), ("JC", [128], BF),
     ("GX", [128], F32), ("BDG", [128], BF), ("LI", [72], I32), ("LU", [72], U16),
     ("PG", [128], F32), ("PGS", [8, 16], F32), ("M0", [8, 32], F32), ("K", [8, 32], I32),
-    ("ZF", [8, 32], F32), ("Z0", [8, 33], F32), ("YI", [256], I32), ("YF", [256], F16), ("D0", [256], F16),
+    ("ZF", [8, 33], F32), ("I16", [128], F32), ("I20", [128], F32), ("YI", [256], I32), ("YF", [256], F16), ("D0", [256], F16),
     ("A16", [256], F16), ("B16", [256], F16), ("SLAB", [8, 32], BF), ("IDX0", [512], U16), ("IDX1", [512], U16),
     ("LB", [8, 32], F32), ("W", [256], F32), ("TT", [8, 32], F32), ("SN", [256], BF), ("UU", [256], BF),
     ("LE", [256], F32), ("G", [264], F32),
     ("GI", [8], I32), ("NA", [8], I32), ("NB", [8], I32), ("NM", [8], F32), ("NX", [144], F32),
     ("DF", [8, 32], I32), ("LOW", [8, 32], I32), ("INV", [256], BF), ("EE", [256], F32), ("CI", [256], BF), ("YY", [256], BF),
     ("FL", [1024], BF), ("XP", [8, 32], F32), ("UJ", [128], BF),
-    ("PG2", [128], F32), ("Y2", [128], F32), ("U2", [128], BF), ("T0", [128], F32), ("V2", [128], F32), ("WN", [128], BF),
-    ("TS", [8, 8], F32), ("Q0", [8, 16], F32), ("Q1", [8, 16], F32),
+    ("PG2", [128], F32), ("Y2", [128], F32), ("U2", [128], BF), ("T0", [128], F32), ("WN", [128], BF),
+    ("Q0", [8, 16], F32), ("Q1", [8, 16], F32),
     ("SL", [8, 32], F32), ("HI", [256], BF), ("LO", [256], BF),
     ("SA0", [2048, 2], BF), ("SB0", [2048, 2], BF), ("SA1", [2048, 2], BF), ("SB1", [2048, 2], BF),
     ("CA0", [4096], F16), ("CB0", [4096], F16), ("CA1", [4096], F16), ("CB1", [4096], F16),
@@ -56,23 +57,26 @@ for _n, _s, _d in [
     ("RN", [32], U16), ("NU", [64], U16),
 ]:
     _sb(_n, _s, _d)
-for _v in range(NV - 1):
-    _sb("OUT%d" % _v, [8, 16], F32)
-    _sb("RL%d" % _v, [8, 16], F32)
+for _n in ("OUT", "RL", "TO", "RT"):
+    _sb(_n, [NV - 1, 8, 16], F32)
 for _n in ("pS", "pT", "pI", "pK"):
     SCRATCH[_n] = ("psum", [128, 16, 32], F32)
 for _n in ("pV", "pF0", "pF1", "pY"):
     SCRATCH[_n] = ("psum", [128, 512], F32)
 
 SEMAPHORES = (["cV", "cS", "cP", "cG", "dls", "dfp", "dpx", "dom", "dsg", "dco", "dst", "sent"]
-              + ["add%d" % v for v in range(NV)] + ["one%d" % v for v in range(NV)] + ["cadd%d" % v for v in range(2 * NV)]
-              + ["rn%d" % v for v in range(NV - 1)] + ["rl%d" % v for v in range(NV - 1)])
+              + ["add%d" % v for v in range(NV)] + ["one%d" % v for v in range(2 * NV)] + ["cadd%d" % v for v in range(2 * NV)]
+              + ["rn%d" % v for v in range(NV - 1)] + ["rl%d" % v for v in range(NV - 1)] + ["rt%d" % v for v in range(NV - 1)])
 
-CASES = ((1.0, 1.55, 70.0, 3000.0, 250.0), (1.25, 1.15, 80.0, 3000.0, 300.0), (1.35, 2.0, 90.0, 3500.0, 200.0))
-ROUNDS = 100
-CLIMB = 40000
+CASES = ((1.1, 1.6, 90.0, 2400.0, 400.0), (1.15, 1.2, 70.0, 2600.0, 420.0), (1.4, 2.05, 100.0, 2500.0, 370.0),
+         (1.1, 1.5, 80.0, 3200.0, 280.0))
+EARLY = (2, 3, 4, 5, 6, 8)
+ROUNDS = 60
+CLIMB = 140000
+FRESH = 8
+SEED = 82
 NOISE = 1000.0
-SLACK = 200.0
+SLACK = 150.0
 PLANS = {}
 
 
@@ -82,7 +86,7 @@ def costs(ops, case):
     for o in ops:
         fix, n, gat, kind = o["cost"]
         if kind == "dma":
-            b = fix + n / rate
+            b = fix * way / 2500.0 + n / rate
             l = b + 1000.0
         elif kind == "send":
             b = n / 40.0
@@ -97,12 +101,10 @@ def costs(ops, case):
     return busy, lat
 
 
-def replay(qs, pred, order, busy, lat, first=0, known=None):
+def replay(qs, pred, order, busy, lat):
     free = [0.0] * 8
-    start, done = (list(known[0]), list(known[1])) if first else ([0.0] * len(qs), [0.0] * len(qs))
-    for i in order[max(first - 300, 0):first]:
-        free[qs[i]] = start[i] + busy[i]
-    for i in order[first:]:
+    start, done = [0.0] * len(qs), [0.0] * len(qs)
+    for i in order:
         q = qs[i]
         t = free[q]
         for d in pred[i]:
@@ -111,6 +113,33 @@ def replay(qs, pred, order, busy, lat, first=0, known=None):
         start[i] = t
         free[q] = t + busy[i]
         done[i] = t + lat[i]
+    return max(done), start, done
+
+
+def retime(qs, pred, order, busy, lat, first, reach, known, far, rest, most):
+    free = [0.0] * 8
+    start, done = list(known[0]), list(known[1])
+    for i in order[max(first - 300, 0):first]:
+        free[qs[i]] = start[i] + busy[i]
+    k = first
+    moved = reach
+    for i in order[first:]:
+        if k > reach:
+            break
+        q = qs[i]
+        t = free[q]
+        for d in pred[i]:
+            if done[d] > t:
+                t = done[d]
+        if t != start[i]:
+            if k > moved and t + rest[i] > most:
+                return None
+            start[i] = t
+            done[i] = t + lat[i]
+            if far[i] > reach:
+                reach = far[i]
+        free[q] = t + busy[i]
+        k += 1
     return max(done), start, done
 
 
@@ -172,20 +201,29 @@ def plan(ops):
             pred.append(keep)
         cs = [costs(ops, c) for c in CASES]
         busy, lat = cs[0]
-        seed = [12345]
+        seed = [SEED]
 
         def rnd(m):
             seed[0] = (seed[0] * 1103515245 + 12345) % 2147483648
             return (seed[0] >> 8) % m
 
-        def score(order, first=0, known=None):
-            got = [replay(qs, pred, order, b, l, first, known and known[k]) for k, (b, l) in enumerate(cs)]
+        def score(order):
+            got = [replay(qs, pred, order, b, l) for b, l in cs]
             return sum(r[0] / c[0] for r, c in zip(got, CASES)) / len(cs), [r[1:] for r in got]
 
-        prio = [0.0] * n
-        for i in range(n - 1, -1, -1):
-            prio[i] = lat[i] + max([prio[s] for s in succ[i]] + [0.0])
         best = None
+        for early in EARLY:
+            rank = {"setup": 0, (0, "pixel"): 1}
+            for v in range(NV + 1):
+                for k in ([(v, "merge"), (v, "sg"), (v, "keys")] + [(v - 1, c) for c in range(early)]
+                          + [(v, "seen"), (v, "list"), (v + 1, "pixel")] + [(v - 1, c) for c in range(early, 8)]
+                          + [(v, "co"), (v - 1, "tau"), (v, "a"), (v, "one")]):
+                    rank[k] = len(rank)
+            order, start = sweep(qs, pred, succ, [-n * rank[o["kind"]] - i for i, o in enumerate(ops)], busy, lat, False)
+            end = score(order)[0]
+            if best is None or end < best[0]:
+                best = (end, order, start)
+        prio = [-t for t in best[2]]
         for r in range(ROUNDS):
             order, start = sweep(qs, pred, succ, prio, busy, lat, False)
             end = score(order)[0]
@@ -199,54 +237,90 @@ def plan(ops):
             prio = [st[i] + busy[i] for i in range(n)]
         order = best[1]
         end, starts = score(order)
+        ends = [max(s[1]) for s in starts]
         best = (end, order, starts[0][0])
-        links = None
+        taken = moved = 0
+        pos = [0] * n
+        before = [-1] * n
         for r in range(CLIMB):
-            if links is None:
-                pos = [0] * n
-                before = [-1] * n
+            fresh = taken % FRESH == 0
+            if fresh:
+                taken += 1
+                place = {i: k for k, i in enumerate(order)}
+                order = sorted(order, key=lambda i: (starts[0][0][i], place[i]))
+            if fresh or moved:
+                moved = 0
                 tail = [-1] * 8
                 for k, i in enumerate(order):
                     pos[i] = k
                     before[i] = tail[qs[i]]
                     tail[qs[i]] = i
+                far = [max([pos[s] for s in succ[i]] + [0]) for i in range(n)] if fresh else far
+                for i in range(n) if fresh else order[first:last + 1]:
+                    if not fresh and qs[i] == qs[a]:
+                        far[i] = max(far[i], reach)
+                    for d in pred[i] + [before[i]]:
+                        if d >= 0 and far[d] < pos[i]:
+                            far[d] = pos[i]
+            if fresh:
+                rests = []
+                for b, l in cs:
+                    rest = list(l)
+                    for i in reversed(order):
+                        for d in pred[i]:
+                            if rest[d] < l[d] + rest[i]:
+                                rest[d] = l[d] + rest[i]
+                        d = before[i]
+                        if d >= 0 and rest[d] < b[d] + rest[i]:
+                            rest[d] = b[d] + rest[i]
+                    rests.append(rest)
                 links = []
-                for (st, _d), (b, l) in zip(starts, cs):
-                    i = max(range(n), key=lambda j: st[j] + l[j])
+                for case, ((st, done), (b, l)) in enumerate(zip(starts, cs)):
+                    i = done.index(ends[case])
                     while i >= 0:
                         a = before[i]
                         if a >= 0 and st[a] + b[a] >= st[i] - 1e-6:
                             if a not in pred[i]:
-                                links.append((a, i))
+                                links.append((i, case))
                             i = a
                         else:
-                            i = max(pred[i], key=lambda d: st[d] + l[d]) if pred[i] and st[i] > 0 else -1
-            a, i = links[rnd(len(links))]
-            new = list(order)
+                            i = max(pred[i], key=lambda d: done[d]) if pred[i] and st[i] > 0 else -1
+            i, case = links[rnd(len(links))]
+            a = before[i]
+            if a < 0:
+                continue
             if rnd(2):
                 for _ in range((0, 0, 1, 2, 4, 8, 16, 32)[rnd(8)]):
                     if before[a] >= 0:
                         a = before[a]
-                to = max([pos[a]] + [pos[d] + 1 for d in pred[i]])
-                if to > pos[before[i]]:
+                first = max([pos[a]] + [pos[d] + 1 for d in pred[i]])
+                if first > pos[before[i]]:
                     continue
-                del new[pos[i]]
-                new.insert(to, i)
-                first = to
+                last = pos[i]
+                new = order[:first] + [i] + order[first:last] + order[last + 1:]
             else:
                 to = min([pos[i] + (0, 0, 2, 5, 10, 20, 40, 80)[rnd(8)], n - 1] + [pos[s] - 1 for s in succ[a]])
                 if to < pos[i]:
                     continue
-                del new[pos[a]]
-                new.insert(to, a)
-                first = pos[a]
-            e2, s2 = score(new, first, starts)
-            if e2 <= end + SLACK * (1.0 - r / CLIMB) * rnd(1000) / 1000.0:
-                place = {i: k for k, i in enumerate(new)}
-                end, starts, links = e2, s2, None
-                order = sorted(new, key=lambda i: (s2[0][0][i], place[i]))
+                first, last = pos[a], to
+                new = order[:first] + order[first + 1:to + 1] + [a] + order[to + 1:]
+            room = len(cs) * SLACK * (1.0 - r / CLIMB) * rnd(1000) / 1000.0
+            got = [None] * len(cs)
+            reach = max([last] + [far[j] for j in order[first:last + 1] if qs[j] == qs[i]])
+            for k in range(len(cs)):
+                k = (k + case) % len(cs)
+                got[k] = retime(qs, pred, new, cs[k][0], cs[k][1], first, reach, starts[k], far, rests[k], ends[k] + room * CASES[k][0])
+                if got[k] is None:
+                    break
+                room -= (got[k][0] - ends[k]) / CASES[k][0]
+                if room < 0.0:
+                    break
+            else:
+                taken, moved = taken + 1, 1
+                order, starts, ends = new, [x[1:] for x in got], [x[0] for x in got]
+                end = sum(e / c[0] for e, c in zip(ends, CASES)) / len(cs)
                 if end < best[0]:
-                    best = (end, order, s2[0][0])
+                    best = (end, order, starts[0][0])
         PLANS[key] = best
     for i, o in enumerate(ops):
         o["t"] = PLANS[key][2][i]
@@ -267,6 +341,7 @@ def build(g, core, T, topo):
     V, S, P, Y = g.vector, g.scalar, g.tensor, g.sync
     ops = []
     lastw, readers, bankers = {}, {}, {}
+    kind = ["setup"]
 
     def op(q, fn, cost, r=(), w=(), bank=None, sem=None, inc=1):
         i = len(ops)
@@ -292,7 +367,7 @@ def build(g, core, T, topo):
                 deps.update(b[1])
             b[1].append(i)
         deps.discard(i)
-        ops.append({"q": q, "fn": fn, "cost": cost, "deps": sorted(deps), "sem": sem or "c" + q, "inc": inc, "name": str(w)})
+        ops.append({"q": q, "fn": fn, "cost": cost, "deps": sorted(deps), "sem": sem or "c" + q, "inc": inc, "name": str(w), "kind": kind[0]})
         return i
 
     def ts(out, in0, s1, s2, o0, o1, n, r, w, bank=None):
@@ -336,8 +411,8 @@ def build(g, core, T, topo):
             return op("G", lambda: g.iota(out, pat, base, cm, allow_small_or_imprecise_dtypes=True), (130.0, 2 * n, 0, ""), (), w)
         return op("G", lambda: g.iota(out, pat, base, cm), (130.0, 2 * n, 0, ""), (), w)
 
-    def asel(out, a, pat, base, n, r, w):
-        return op("G", lambda: g.affine_select(out, a, pat, ALU.is_equal, 0.0, base, 1), (170.0, 2 * n, 0, ""), r, w)
+    def asel(out, a, pat, base, n, r, w, fill=0.0, cm=1, keep=ALU.is_equal):
+        return op("G", lambda: g.affine_select(out, a, pat, keep, fill, base, cm), (170.0, 2 * n, 0, ""), r, w)
 
     def send(src, dst, nbytes, r, w, sem):
         op("G", lambda: g.remote_dma(dst, src, T.sem[sem], T.sem.sent, pid, rid, omask), (300.0, 0, 0, "dma"), r, [("sent", sem)], sem="*")
@@ -365,47 +440,53 @@ def build(g, core, T, topo):
     iota(T.LI[:, 64:72], [[32, 8]], 32, 0, 8, ["LI3"], False)
     iota(T.IO8[:], [[1, 8]], 0, 0, 8, ["IO8"])
     iota(T.IO144[:], [[0, 9], [1, 16]], 0, 0, 144, ["IO144"])
-    iota(T.CP2[:], [[0, 8], [128, 16]], 0, 0, 128, ["CP2"])
-    iota(T.CP3[:], [[0, 8], [-128, 16]], 3968, 0, 128, ["CP3"])
+    iota(T.CP2[:], [[0, 8], [128, 16]], -2048, 0, 128, ["CP2"])
+    iota(T.CP3[:], [[0, 8], [-128, 16]], 1920, 0, 128, ["CP3"])
     iota(T.JC[:], [[0, 8], [1, 16]], 8, 0, 128, ["JC"])
     iota(T.GX[:], [[1, 8], [0, 16]], 0, 0, 128, ["GX"])
     for u in range(4):
         iota(T.RV[:, :, u, :], [[0, 8], [4, 2], [8, 2]], (0, 2, 1, 3)[u], 0, 32, [("RV", u)])
     RVK = [("RV", u) for u in range(4)]
+    iota(T.ONES[:], [[0, 2048]], 1, 0, 2048, ["ONES"])
     iota(T.C1024[:], [[0, 256]], 1024, 0, 256, ["C1024"])
     iota(T.MI[:], [[0, 16], [1, 32]], 0, 0, 512, ["MI"])
     act(T.MASK[:], T.MI[:], 512, ["MI"], ["MASK"], func=ACT.Sign)
-    act(T.MASKB[:], T.MI[:, 0:256], 256, ["MI"], ["MASKB"], func=ACT.Sign)
+    asel(T.MASKB[:], T.ONES[:, 0:256], [[0, 8], [1, 32]], 0, 256, ["ONES"], ["MASKB"], 0.0, 0, ALU.not_equal)
     act(T.pT[:, 8:16, :], T.MI[:, 0:256], 256, ["MI"], ["SC"], "pT", scale=2.0 ** -5)
-    iota(T.ONES[:], [[0, 2048]], 1, 0, 2048, ["ONES"])
     asel(T.SEL[:], T.ONES[:], [[-1, 16], [-16, 8], [0, 16]], 0, 2048, ["ONES"], ["SEL"])
     ts(T.PJ[:, 0:1], T.PI[:, 0:1], 15, None, ALU.bitwise_and, None, 1, ["PI"], ["PJ0"])
     ts(T.PJ[:, 1:2], T.PI[:, 0:1], 4, None, ALU.arith_shift_right, None, 1, ["PI"], ["PJ1"])
     cp(T.PCOL[:, 0:2], T.PJ[:, 0:2], 2, ["PJ0", "PJ1"], ["PC0"])
-    ts(T.PCOL[:, 3:4], T.PJ[:, 0:1], 128.0, 2048.0, ALU.mult, ALU.add, 1, ["PJ0"], ["PC3"])
+    ts(T.PCOL[:, 3:4], T.PJ[:, 0:1], 128.0, None, ALU.mult, None, 1, ["PJ0"], ["PC3"])
     cp(T.LU[:], T.LI[:], 72, ["LI0", "LI1", "LI2", "LI3"], ["LU"])
     ms(T.LU[:, 48:49], 7, 1, ["LU"])
     cp(T.FPU[:], T.FPI[:], 8, ["FPI"], ["FPU"])
     ts(T.MK[:], T.IO144[:], T.PCOL[:, 0:1], None, ALU.is_equal, None, 144, ["IO144", "PC0"], ["MK"])
     ts(T.BLK[:], T.IO8[:], T.PCOL[:, 1:2], None, ALU.is_equal, None, 8, ["IO8", "PC0"], ["BLK"])
-    ts(T.BDG[:], T.GX[:], T.PCOL[:, 1:2], 2.0 ** 19, ALU.is_equal, ALU.mult, 128, ["GX", "PC0"], ["BDG"])
+    ts(T.BDG[:], T.GX[:], T.PCOL[:, 1:2], -2.0 ** 19, ALU.is_equal, ALU.mult, 128, ["GX", "PC0"], ["BDG"])
     for buf, key, c0, c1 in ((T.RMA, "RMA", -4096.0, -1.0), (T.RMB, "RMB", -4096.0, 1.0), (T.BLKB, "BLKB", 2.0 ** 36, 0.0)):
         act(buf[:, 0:8], T.BLK[:], 8, ["BLK"], [key + "a"], scale=c0)
         act(buf[:, 8:16], T.BLK[:], 8, ["BLK"], [key + "b"], scale=c1)
+    ms(T.ZB[:], 0.0, 64, ["ZB"])
     for name, c in IDS.items():
-        act(I[name], T.IDF[:], 128, ["IDF"], [name], scale=c)
+        if name in EARLY_IDS:
+            act(I[name], T.IDF[:], 128, ["IDF"], [name], scale=c)
+        else:
+            asel(I[name], T.ZB[:], [[-1, 128]], 0, 128, ["ZB"], [name], c, 1, ALU.not_equal)
     for name, c in IDH.items():
         ts(I[name], T.IDF[:], c, None, ALU.mult, None, 128, ["IDF"], [name])
     act(T.NIF[:], T.IDF[:], 128, ["IDF"], ["NIF"], scale=-1.0)
     act(T.I15[:], T.IDF[:], 128, ["IDF"], ["I15"], scale=15.0)
+    act(T.I16[:], T.IDF[:], 128, ["IDF"], ["I16"], scale=2.0 ** -4)
+    act(T.I20[:], T.IDF[:], 128, ["IDF"], ["I20"], scale=2.0 ** 20)
     act(T.PERM15[:], T.PERM[:], 128, ["PERM"], ["PERM15"], scale=15.0)
     act(T.CP1[:], T.RV[:], 128, RVK, ["CP1"], scale=-2.0 ** 24)
     tt(T.RD[:], T.RV[:], T.IO144[:, 0:128], ALU.subtract, 256, RVK + ["IO144"], ["RD"])
-    ts(T.pV[:, 384:512], T.RD[:], 2.0 ** 20, 128.0, ALU.mult, ALU.add, 128, ["RD"], ["TC"], "pV")
+    ts(T.pV[:, 384:512], T.RD[:], 2.0 ** 20, 64.0, ALU.mult, ALU.add, 128, ["RD"], ["TC"], "pV")
     ts(T.pV[:, 0:8], T.IO8[:], 0.0, None, ALU.mult, None, 8, ["IO8"], ["pVa"], "pV")
     ms(T.SG[:, 4096:4112], 0.5, 16, ["SGz"])
     ms(T.CO[:, 4096:4112], 0.0, 16, ["COz"])
-    for buf, at, c, key in ((T.Z0, 32, 2.0 ** 20, "Z0e"), (T.SLAB, 0, 4224.0, "SLAB0"), (T.LB, 0, 1.0, "LB0"), (T.SL, 0, 1.0, "SL0")):
+    for buf, at, c, key in ((T.ZF, 32, M4096 + 2.0 ** 24, "ZFe"), (T.SLAB, 0, 4224.0, "SLAB0"), (T.LB, 0, 1.0, "LB0"), (T.SL, 0, 1.0, "SL0")):
         act(buf[:, :, at], T.IO8[:], 8, ["IO8"], [key], scale=0.0, bias=c)
     ms(T.G[:, 0:1], 0.0, 1, ["G0"])
     ms(T.LOW[:, :, 0], 0, 8, ["LOW0"])
@@ -421,9 +502,8 @@ def build(g, core, T, topo):
     for c2 in range(2):
         c = slice(512 * c2, 512 * c2 + 512)
         bk = "pF%d" % c2
-        cp(T.PF[:, c], T.PXI[:, c], 512, ["PXI"], [("PF", c2)])
-        act(T.WO[:, c], T.PF[:, c], 512, [("PF", c2)], [("WO", c2)], bias=M256)
-        act(T.WO[:, c], T.WO[:, c], 512, [], [("WO", c2)], bias=-M256)
+        act(T.PF[:, c], T.PXI[:, c], 512, ["PXI"], [("PF", c2)])
+        ts(T.WO[:, c], T.PXI[:, c], M256, -M256, ALU.add, ALU.add, 512, ["PXI"], [("WO", c2)])
         group(T[bk][:], [(T.I15[:], T.WO[:, c], 2048), (T.IDF[:], T.PF[:, c], 2048)], True, [("WO", c2), ("PF", c2), "I15", "IDF"], [bk], bk)
         act(T.PK[:, c], T[bk][:], 512, [bk, "PC3"], [("PK", c2)], bk, bias=T.PCOL[:, 3:4])
     PKK, PFK = [("PK", c2) for c2 in range(2)], [("PF", c2) for c2 in range(2)]
@@ -440,22 +520,27 @@ def build(g, core, T, topo):
         last = v == NV - 1
         AB, WT = T["AB%d" % e], T["AB%d" % (1 - e)]
         IDX, SA, SB, CA, CB = T["IDX%d" % e], T["SA%d" % e], T["SB%d" % e], T["CA%d" % e], T["CB%d" % e]
+        kind[0] = (v, "pixel")
         pix, lane = T.pK[:, 8:16, 0:16], T.pK[:, 0:8, 0:16]
         if v == 0:
+            group(lane, [(T.AQ[:, 0:128], T.I15[:], 512), (T.RAWF[:, 0:128], T.IDF[:], 512), (I["IB"], T.CP2[:], 128)], True,
+                  ["AQ0", "RAW0", "IDF", "I15", "IB", "CP2"], ["pKa"], "pK")
             group(pix, [(T.AQ[:, 128:256], T.PERM15[:], 512), (T.RAWF[:, 128:256], T.PERM[:], 512), (I["IB"], T.CP3[:], 128)], True,
                   ["AQ1", "RAW1", "PERM", "PERM15", "IB", "CP3"], ["pKb"], "pK")
         else:
             act(T.PG[:], T.PK[:].indirect(T.RN[:, 8 * v - 8:8 * v]), 0, PKK + [("RN", v - 1)], ["PG"], gat=128)
             group(pix, [(T.PG[:], T.PERM[:], 512)], True, ["PG", "PERM"], ["pKb"], "pK")
         act(T.PGS[:], pix, 128, ["pKb"], ["PGS"], "pK")
-        if v == 0:
-            group(lane, [(T.AQ[:, 0:128], T.I15[:], 512), (T.RAWF[:, 0:128], T.IDF[:], 512), (I["IB"], T.CP2[:], 128)], True,
-                  ["AQ0", "RAW0", "IDF", "I15", "IB", "CP2"], ["pKa"], "pK")
-        else:
-            RL = T["RL%d" % (v - 1)]
+        kind[0] = (v, "merge")
+        if v:
             group(lane, [(I["IB"], T.CP1[:], 128), (I["IB"], T.CP2[:], 128)], True, ["IB", "CP1", "CP2"], ["pKa"], "pK", False)
-            ts(T.AQ[:, 0:128], RL[:], M256, -M256, ALU.add, ALU.add, 128, [("RL", v - 1)], ["AQ0"])
-            group(lane, [(T.I15[:], T.AQ[:, 0:128], 512), (T.IDF[:], RL[:], 512)], False, ["AQ0", ("RL", v - 1), "I15", "IDF"], ["pKa"], "pK")
+            stage(T.Q1, "Q1", T.RT[:, v - 1, :, 0:8], T.RT[:, v - 1, :, 8:16], 128, [("RT", v - 1)])
+            for dst, dk, src, sk in ((T.Q0, "Q0", T.Q1, "Q1"), (T.Q1, "Q1", T.Q0, "Q0"), (T.Q0, "Q0", T.Q1, "Q1")):
+                stage(dst, dk, src[:, :, 0:8], src[:, :, 8:16], 128, [sk + "a", sk + "b"])
+            tt(T.pV[:, 0:128], T.Q0[:], T.pV[:, 384:512], ALU.add, 128, ["Q0a", "Q0b", "TC"], ["pVa"], "pV")
+            tt(T.Q1[:], T.RL[:, v - 1], T.pV[:, 0:128], ALU.min, 128, [("RL", v - 1), "pVa"], ["Q1a", "Q1b"], "pV")
+            ts(T.AQ[:, 0:128], T.Q1[:], M256, -M256, ALU.add, ALU.add, 128, ["Q1a", "Q1b"], ["AQ0"])
+            group(lane, [(T.I15[:], T.AQ[:, 0:128], 512), (T.IDF[:], T.Q1[:], 512)], False, ["AQ0", "Q1a", "Q1b", "I15", "IDF"], ["pKa"], "pK")
         for k in range(4):
             a, b = k % 2, 16 * (k % 2)
             for hf in range(2):
@@ -472,16 +557,15 @@ def build(g, core, T, topo):
         for x, o in enumerate((ALU.min, ALU.max)):
             tt(T.K[:, :, x:32:2], T.M0[:, :, 16:32], T.pT[:, 0:8, 16:32], o, 128, EVK[1] + ODK[1], ["K" + "ab"[x]], "pT")
         KK = ["Ka", "Kb"]
-        ts(T.ZF[:], T.K[:], -2048.0, M4096, ALU.add, ALU.add, 256, KK, ["ZF"])
+        act(T.ZF[:, :, 0:32], T.K[:], 256, KK, ["ZF"], bias=M4096)
         ts(T.YI[:], T.K[:], 2175, None, ALU.bitwise_and, None, 256, KK, ["YI"])
         ts(T.YF[:], T.YI[:], -1920.0, None, ALU.add, None, 256, ["YI"], ["YF"])
         act(T.SLAB[:, :, 1:32], T.ZF[:, :, 1:32], 248, ["ZF"], ["SLAB"], scale=2.0 ** -19, bias=127.50390625 - M4096 * 2.0 ** -19)
-        act(T.Z0[:, :, 0:32], T.ZF[:], 256, ["ZF"], ["Z0"], scale=2.0 ** -4, bias=-M4096 * 2.0 ** -4)
         ts(T.D0[:], T.YF[:], 0.0, 4096.0, ALU.is_lt, ALU.mult, 128, ["YF"], ["D0"])
-        scan(T.A16[:], T.D0[:], T.YF[:], 0.0, ALU.add, ALU.min, 128, ["D0", "YF"], ["A16"])
-        scan(T.B16[:], T.D0[:], T.YF[:], 128.0, ALU.min, ALU.max, 128, ["D0", "YF"], ["B16"])
-        for x, (src, sk, add, bk, keys) in enumerate(((T.A16, "A16", 61440.0 - 128.0, "pI", [("pI", 0), ("pI", 1)]),
-                                                      (T.B16, "B16", -4096.0 - 128.0, "pS", ["pSa"]))):
+        scan(T.A16[:], T.D0[:], T.YF[:], 128.0, ALU.min, ALU.max, 128, ["D0", "YF"], ["A16"])
+        scan(T.B16[:], T.D0[:], T.YF[:], 0.0, ALU.add, ALU.min, 128, ["D0", "YF"], ["B16"])
+        for x, (src, sk, add, bk, keys) in enumerate(((T.A16, "A16", -4096.0 - 128.0, "pI", [("pI", 0), ("pI", 1)]),
+                                                      (T.B16, "B16", 61440.0 - 128.0, "pS", ["pSa"]))):
             its = []
             for h in range(2):
                 o = T[bk][:, 4 * h:4 * h + 4, :]
@@ -489,14 +573,16 @@ def build(g, core, T, topo):
                 its.append((o, src[:, h:256:2], I["IH32"], False, True))
             mm(its, 512, [sk, "SLAB", "SLAB0", "IB", "IH32"], keys, bk)
             ts(IDX[:, 256 * x:256 * x + 256], T[bk][:, 0:8, :], add, 4096.0, ALU.add, ALU.min, 256, keys, [("IDX", e, x)], bk)
-        group(T.pI[:, 0:8, :], [(T.IDF[:], T.Z0[:, :, 1:33], 1024), (T.NIF[:], T.Z0[:, :, 0:32], 1024)], True,
-              ["Z0", "Z0e", "IDF", "NIF"], [("pI", 0), ("pI", 1)], "pI")
-        act(T.LB[:, :, 1:32], T.pI[:, 0:8, 1:32], 248, [("pI", 0), ("pI", 1)], ["LB"], "pI", scale=65536.0)
+        kind[0] = (v, "keys")
+        group(T.pI[:, 0:8, :], [(T.IDF[:], T.ZF[:, :, 1:33], 1024), (T.NIF[:], T.ZF[:, :, 0:32], 1024)], True,
+              ["ZF", "ZFe", "IDF", "NIF"], [("pI", 0), ("pI", 1)], "pI")
+        act(T.LB[:, :, 1:32], T.pI[:, 0:8, 1:32], 248, [("pI", 0), ("pI", 1)], ["LB"], "pI", scale=4096.0)
         if not last:
-            group(T.pK[:, 8:16, :], [(I["IH"], T.B16[:], 256), (I["NIH"], T.A16[:], 256), (I["NI2"], T.C1024[:], 256)], True,
-                  ["A16", "B16", "IH", "NIH", "NI2", "C1024"], ["pKb"], "pK")
-            group(T.pK[:, 0:8, :], [(T.IDF[:], T.Z0[:, :, 0:32], 1024), (I["IH"], T.A16[:], 256), (I["I2"], T.C1024[:], 256)], True,
-                  ["Z0", "A16", "IDF", "IH", "I2", "C1024"], ["pKa"], "pK", False)
+            group(T.pK[:, 8:16, :], [(I["IH"], T.B16[:], 256), (I["NIH"], T.A16[:], 256), (I["I2"], T.C1024[:], 256)], True,
+                  ["A16", "B16", "IH", "NIH", "I2", "C1024"], ["pKb"], "pK")
+            group(T.pK[:, 0:8, :], [(T.I16[:], T.ZF[:, :, 0:32], 1024), (I["N21"], T.C1024[:], 256), (I["NHALF"], T.C1024[:], 256),
+                                    (I["IH"], T.A16[:], 256)], True, ["ZF", "A16", "I16", "N21", "NHALF", "C1024", "IH"], ["pKa"], "pK", False)
+        kind[0] = (v, "sg")
         def piece(buf, c, n):
             return buf[:, 512 * (c % 4):512 * (c % 4 + n), c // 4]
 
@@ -523,6 +609,7 @@ def build(g, core, T, topo):
                     for s in range(2 - h, 32, 2)], 16 * 64, keys[4 * h:4 * h + 4] + [rk + "a", rk + "b"], ["pSa", "pSb"], "pS")
         if not VADD[v]:
             dma("G", g, SB[:], SA[:], 2 * 1048576, SAK, SBK, "add%d" % v, accum_op=ALU.add, max_dma_last_dim=4096)
+        kind[0] = (v, "seen")
         tt(T.W[:], T.LB[:], T.pS[:, 0:8, :], ALU.mult, 256, ["LB", "LB0", "pSa"], ["W"], "pS")
         if not last:
             ts(T.SN[:], T.pS[:, 8:16, :], 0.5, None, ALU.is_gt, None, 256, ["pSb"], ["SN"], "pS")
@@ -535,10 +622,10 @@ def build(g, core, T, topo):
         hk, lk = [("pI", 0), ("pI", 1)], [("pI", 2), ("pI", 3)]
         mm([(T.pI[:, 4 * h:4 * h + 4, :], T.SL[:, :, h:32:2], T.NIF[:], True, True) for h in range(2)], 1024, ["SL", "SL0", "NIF"], hk, "pI")
         act(T.HI[:], T.pI[:, 0:8, :], 256, hk, ["HI"], "pI")
-        mm([(T.pI[:, 8:16, :], I["NIB"], T.HI[:], True, False)]
-           + [(T.pI[:, 8 + 4 * h:12 + 4 * h, :], T.SL[:, :, h:32:2], T.NIF[:], False, h == 1) for h in range(2)], 1280,
-           ["SL", "SL0", "NIF", "NIB", "HI"], lk, "pI")
-        act(T.LO[:], T.pI[:, 8:16, :], 256, lk, ["LO"], "pI")
+        bk, lk = ("pK", ["pKb"]) if last else ("pI", lk)
+        mm([(T[bk][:, 8 + 4 * h:12 + 4 * h, :], T.SL[:, :, h:32:2], T.NIF[:], h == 0, False) for h in range(2)], 1024, ["SL", "SL0", "NIF"], lk, bk)
+        group(T[bk][:, 8:16, :], [(I["NIB"], T.HI[:], 256)], False, ["NIB", "HI"], lk, bk)
+        act(T.LO[:], T[bk][:, 8:16, :], 256, lk, ["LO"], bk)
         if not last:
             tt(T.LE[:], T.TT[:], T.pK[:, 0:8, :], ALU.min, 256, ["TT", "pKa"], ["LE"], "pK")
             scan(T.G[:, 1:257], T.MASK[:, 0:256], T.LE[:], 0.0, ALU.mult, ALU.max, 256, ["MASK", "LE"], ["G"])
@@ -551,6 +638,7 @@ def build(g, core, T, topo):
                512, ["NX", "BLK"], ["pSa"], "pS")
             cp(T.NU[:, 16 * v:16 * v + 16], T.pS[:, 0, 0:16], 16, ["pSa"], [("NU", v)], "pS")
             send(T.NU[:, 16 * v + 8:16 * v + 16], T.RN[:, 8 * v:8 * v + 8], 2048, [("NU", v)], [("RN", v)], "rn%d" % v)
+            kind[0] = (v, "list")
             tt(T.DF[:], T.G[:, 1:257], T.G[:, 0:256], ALU.subtract, 512, ["G", "G0"], ["DF"])
             ts(T.LOW[:, :, 1:32], T.DF[:, :, 1:32], 255, None, ALU.bitwise_and, None, 248, ["DF"], ["LOW"])
             ts(T.INV[:], T.LOW[:], 0.0, 2.0 ** -5, ALU.is_equal, ALU.mult, 256, ["LOW", "LOW0"], ["INV"])
@@ -578,28 +666,24 @@ def build(g, core, T, topo):
                         dst = T.M0[:, :, d + 8 * x:d + 8 * x + 8] if par else T.pT[:, 0:8, d + 8 * x:d + 8 * x + 8]
                         tt(dst, T.M0[:, :, b + par:b + 16:2], T.pT[:, 0:8, b + par:b + 16:2], o, 64, EVK[a] + ODK[a],
                            (ODK if par else EVK)[1 - a][2 * x:2 * x + 2], "pT")
-            tt(T.pV[:, 0:128], T.M0[:, :, 0:16], T.pT[:, 0:8, 0:16], ALU.min, 128, EVK[0] + ODK[0], ["pVa"], ["pT", "pV"])
-            act(T.PG2[:], T.PF[:].indirect(T.NU[:, 16 * v:16 * v + 8]), 0, PFK + [("NU", v)], ["PG2"], bias=-128.0, gat=128)
-            act(T.Y2[:], T.G[:, 0:257].indirect(T.LU[:, 64:72]), 0, ["G", "G0", "LU"], ["Y2"], bias=-128.0, gat=128)
+            tt(T.OUT[:, v], T.M0[:, :, 0:16], T.pT[:, 0:8, 0:16], ALU.min, 128, EVK[0] + ODK[0], [("OUT", v)], "pT")
+            send(T.OUT[:, v], T.RL[:, v], 65536, [("OUT", v)], [("RL", v)], "rl%d" % v)
+            act(T.PG2[:], T.PF[:].indirect(T.NU[:, 16 * v:16 * v + 8]), 0, PFK + [("NU", v)], ["PG2"], scale=2.0 ** -20, gat=128)
+            act(T.Y2[:], T.G[:, 0:257].indirect(T.LU[:, 64:72]), 0, ["G", "G0", "LU"], ["Y2"], scale=2.0 ** -20, gat=128)
             group(T.pI[:, 0:4, :], [(T.Y2[:], T.NIF[:], 512), (T.IDF[:], T.PG2[:], 512)], True, ["PG2", "Y2", "IDF", "NIF"], [("pI", 0)], "pI")
-            act(T.U2[:], T.pI[:, 0:4, :], 128, [("pI", 0)], ["U2"], "pI", func=ACT.Sign)
-            act(T.V2[:], T.U2[:], 128, ["U2"], ["V2"], func=ACT.Relu, scale=-float(FILL))
+            act(T.U2[:], T.pI[:, 0:4, :], 128, [("pI", 0)], ["U2"], "pI", func=ACT.Sign, scale=-1.0)
             act(T.UJ[:], T.CI[:].indirect(T.LU[:, 40:48]), 0, ["CI", "LU"], ["UJ"], func=ACT.Relu, scale=32.0, bias=-16.0, gat=128)
             ta, tk = T.pI[:, 8:16, 0:16], [("pI", 2), ("pI", 3)]
             for out in (T.pI[:, 8:16, 16:32], ta):
-                group(out, [(I["I1"], T.JC[:], 128), (I["NI1"], T.UJ[:], 128), (T.U2[:], T.BDG[:], 128), (T.U2[:], I["IW"], 128)], True,
-                      ["I1", "NI1", "JC", "UJ", "U2", "BDG", "IW"], tk, "pI", out is not ta)
+                group(out, [(I["I1"], T.JC[:], 128), (I["NI1"], T.UJ[:], 128), (T.U2[:], T.BDG[:], 128), (T.U2[:], I["I23"], 128)], True,
+                      ["I1", "NI1", "JC", "UJ", "U2", "BDG", "I23"], tk, "pI", out is not ta)
             act(T.WN[:], T.pI[:, 8:16, 16:32], 128, tk, ["WN"], "pI", func=ACT.Sign, scale=2.0 ** -20, bias=-7.5)
-            tt(T.T0[:], T.PG2[:], T.V2[:], ALU.max, 256, ["PG2", "V2"], ["T0"])
-            group(ta, [(I["IW"], T.WN[:], 128), (I["I64"], T.WN[:], 128), (T.U2[:], I["I64"], 128), (T.T0[:], T.IDF[:], 512)], False,
-                  ["IW", "I64", "WN", "U2", "T0", "IDF"], tk, "pI")
-            act(T.TS[:], T.pI[:, 8:16, 8:16], 64, tk, ["TS"], "pI")
-            stage(T.Q1, "Q1", T.TS[:], T.pI[:, 8:16, 0:8], 64, tk + ["TS"], "pI")
-            for dst, dk, src, sk in ((T.Q0, "Q0", T.Q1, "Q1"), (T.Q1, "Q1", T.Q0, "Q0"), (T.Q0, "Q0", T.Q1, "Q1")):
-                stage(dst, dk, src[:, :, 0:8], src[:, :, 8:16], 128, [sk + "a", sk + "b"])
-            tt(T.Q1[:], T.Q0[:], T.pV[:, 384:512], ALU.add, 128, ["Q0a", "Q0b", "TC"], ["Q1a", "Q1b"], "pV")
-            tt(T["OUT%d" % v][:], T.Q1[:], T.pV[:, 0:128], ALU.min, 128, ["Q1a", "Q1b", "pVa"], [("OUT", v)], "pV")
-            send(T["OUT%d" % v][:], T["RL%d" % v][:], 65536, [("OUT", v)], [("RL", v)], "rl%d" % v)
+            tt(T.T0[:], T.PG2[:], T.U2[:], ALU.max, 256, ["PG2", "U2"], ["T0"])
+            group(ta, [(I["IW"], T.WN[:], 128), (I["I64"], T.WN[:], 128), (T.U2[:], I["N128"], 128), (I["NI8"], T.C1024[:, 0:128], 128),
+                       (T.T0[:], T.I20[:], 512)], False, ["IW", "I64", "WN", "U2", "N128", "NI8", "C1024", "T0", "I20"], tk, "pI")
+            act(T.TO[:, v], ta, 128, tk, [("TO", v)], "pI")
+            send(T.TO[:, v], T.RT[:, v], 65536, [("TO", v)], [("RT", v)], "rt%d" % v)
+        kind[0] = (v, "co")
         for x, (dst, key) in enumerate(((CA, "CA"), (CB, "CB"))):
             for c4, n in runs(0, 4, COW[v]):
                 for h in range(2):
@@ -611,26 +695,27 @@ def build(g, core, T, topo):
             dma("G", g, CB[:, c], CA[:, c], 1048576, [("CA", e, cc) for cc in range(4 * hh, 4 * hh + 4)],
                 [("CB", e, cc) for cc in range(4 * hh, 4 * hh + 4)], "cadd%d" % (2 * v + hh), accum_op=ALU.add, max_dma_last_dim=4096)
         cols = (("CA", CA), ("CB", CB))[CADD[v]:]
+        kind[0] = (v, "a")
         ABH = [("ABh", e, c) for c in range(8)]
         for jp in range(8):
             bk = "pF%d" % (jp % 2)
-            its = []
-            for half in range(2):
-                j = jp + 8 * half
-                its.append((T[bk][:, half:512:2], T.SEL[:, 128 * j:128 * j + 128], T.HI[:], True, False))
-                its.append((T[bk][:, half:512:2], T.SEL[:, 128 * j:128 * j + 128], T.LO[:], False, True))
+            h, its = jp % 2, []
+            for k in range(4):
+                j = 4 * k + jp // 2
+                its.append((T[bk][:, k:512:4], T.SEL[:, 128 * j:128 * j + 128], T.HI[:, 128 * h:128 * h + 128], True, False))
+                its.append((T[bk][:, k:512:4], T.SEL[:, 128 * j:128 * j + 128], T.LO[:, 128 * h:128 * h + 128], False, True))
             mm(its, 1024, ["SEL", "HI", "LO"], [bk], bk)
-            for h in range(2):
-                j = 2 * jp + h
-                tt(AB[:, j:4096:16], SB[:, jp:2048:8, h], T[bk][:, 256 * h:256 * h + 256], ALU.mult, 256, SBK + [bk], [("AB", e, j)], bk)
-        ABK = [("AB", e, j) for j in range(16)]
+            tt(AB[:, jp:4096:8], SB[:, jp // 2:2048:4, h], T[bk][:], ALU.mult, 512, SBK + [bk], [("AB", e, jp)], bk)
+        ABK = [("AB", e, j) for j in range(8)]
+        kind[0] = (v, "one")
         ns = ONE_S[v]
         for c, n in runs(0, ns, ONEW[v]):
             act(AB[:, 512 * c:512 * (c + n)], AB[:, 512 * c:512 * (c + n)], 512 * n, ABK, ABH[c:c + n], bias=1.0)
-        if ns < 8:
-            dma("G", g, AB[:, 512 * ns:4096], T.ONES[:, 0:4096 - 512 * ns], (8 - ns) * 2 * 262144, ABK + ["ONES"], ABH[ns:],
-                "one%d" % v, accum_op=ALU.add, max_dma_last_dim=4096)
+        for c, n in runs(ns, 8, 4):
+            dma("G", g, AB[:, 512 * c:512 * (c + n)], T.ONES[:, 0:512 * n], n * 2 * 262144, ABK + ["ONES"], ABH[c:c + n],
+                "one%d" % (2 * v + c // 4), accum_op=ALU.add, max_dma_last_dim=4096)
         for c in range(8):
+            kind[0] = (v, c)
             bk = "pF%d" % (c % 2)
             lo = 512 * c
             its = ([(T[bk][:], I["NIH"], buf[:, lo:lo + 512]) for key, buf in cols]
@@ -643,6 +728,7 @@ def build(g, core, T, topo):
             if not YT_PE[v]:
                 scan(WT[:, lo:lo + 512], T.MASK[:], AB[:, lo:lo + 512], 0.0, ALU.mult, ALU.add, 512,
                      ok + ["MASK", ("YT", v - 1), ("YC", v - 1)], [("WT", c)])
+        kind[0] = (v, "tau")
         yo = slice(128 * v, 128 * v + 128)
         if YT_PE[v]:
             for j in range(16):

@@ -4,16 +4,22 @@ from concourse.mybir import dt, AluOpType, AxisListType, ActivationFunctionType
 ALU = AluOpType
 ACT = ActivationFunctionType
 NV = 5
-TOP = 2.0 ** 20 - 1
 M256 = 1.5 * 2.0 ** 31
 M4096 = 2.0 ** 35 + 8192
-VADD = (0, 0, 0, 0, 1)
+VADD = (0, 0, 0, 0, 0)
 VSHARE = (8, 8, 8, 8, 8)
-YT_PE = (1, 1, 1, 1, 0)
-ONE_S = (4, 4, 4, 6, 8)
-SGW, COW, ONEW = (4, 4, 4, 4, 1), (2, 2, 2, 2, 1), (2, 2, 2, 2, 1)
-CADD = (1, 1, 1, 1, 0)
+COV = ((), (), (), (), ((1, 0, 0), (1, 0, 1)))
+APART = ((0, 0), (0, 0), (0, 0), (1, 0), (1, 0))
+ONE_S = (2, 2, 2, 4, 8)
+SGW, COW, ONEW = (4, 4, 4, 4, 4), (1, 1, 1, 1, 1), (2, 2, 2, 2, 2)
+CADD = (2, 2, 2, 2, 1)
+ADDW = (2, 2, 2, 2, 1)
+ON_P = {"TC": 0, "YC": 0}
 FLOOR_V = (1, 1, 1, 1)
+ON_S = {"SN": 1, "INV": 1, "YF": 1, "IDX": 0, "T0": 0, "LV": 1}
+DF_SCAN = 1
+SENDER = 1
+ONE_SPLIT = (0, 0, 0, 0, 0)
 
 F32, BF, I32, U16, F16 = "float32", "bfloat16", "int32", "uint16", "float16"
 SCRATCH = {}
@@ -23,55 +29,58 @@ def _sb(name, shape, d):
     SCRATCH[name] = ("sbuf", [128] + list(shape), d)
 
 
-IDS = {"IB": 1.0, "NIB": -1.0, "I3": 3 * 2.0 ** 20, "I1": 2.0 ** 20, "NI1": -2.0 ** 20, "I28": 2.0 ** 28,
-       "IC": -4.3125 * 2.0 ** 20, "NI8": -0.125, "IW": -2.0 ** 23, "I64": 64.0, "I2": 2.0,
-       "N21": -2.0 ** 21, "NHALF": -0.5, "I23": 2.0 ** 23, "N128": -128.0}
-EARLY_IDS = ("IB", "I2", "N21", "NHALF")
-IDH = {"IH32": 32.0, "IH": 1.0, "NIH": -1.0}
+IDS = {"IB": 1.0, "I6": 6 * 2.0 ** 20, "I1": 2.0 ** 20, "NI1": -2.0 ** 20, "I29": 2.0 ** 29, "I26": 2.0 ** 26,
+       "IQ": 1.5 * 2.0 ** 20, "IC": -8.5 * 2.0 ** 20, "N12": -4096.0, "I2": 2.0, "IS": 0.0625,
+       "N21": -2.0 ** 21, "HALF": 0.5, "I23": 2.0 ** 23, "N128": -128.0, "N5": -0.3125}
+EARLY_IDS = ("IB", "I2", "N21", "N5")
+IDH = {"IH32": 32.0, "IH": 1.0, "NIH": -1.0, "IHH": 0.5}
 
 for _n, _s, _d in [
     ("SG", [4112], BF), ("CO", [4112], BF), ("PXI", [1024], I32), ("PF", [1024], F32), ("PK", [1024], F32),
     ("LSI", [128], I32), ("RAWF", [256], F32), ("AQ", [256], F32),
-    ("FPI", [8], I32), ("FPU", [8], U16), ("OMI", [40], I32), ("OMB", [640], F32),
+    ("FPI", [8], I32), ("FPU", [8], U16), ("OMI", [48], I32), ("OMG", [384], F32), ("BND", [40], F32), ("BD", [256], F32),
     ("ONE", [128], F32), ("IDF", [128], F32), ("NIF", [128], F32), ("I15", [128], F32), ("PERM", [128], F32), ("PERM15", [128], F32),
-    ("IDS", [128 * len(IDS)], BF), ("IDH", [128 * len(IDH)], F16), ("ZB", [128], BF), ("SEL", [2048], BF), ("ONES", [2048], BF),
-    ("PI", [8], I32), ("PJ", [8], I32), ("PCOL", [8], F32), ("IO8", [8], F32), ("IO144", [144], F32), ("MK", [144], F32),
-    ("BLK", [8], F32), ("BLKB", [16], F32), ("RMA", [16], BF), ("RMB", [16], BF),
-    ("C1024", [256], BF), ("MI", [512], F32), ("MASK", [512], F32), ("MASKB", [256], BF),
-    ("RV", [8, 4, 4], F32), ("RD", [128], F32), ("CP1", [128], BF), ("CP2", [128], BF), ("CP3", [128], BF), ("JC", [128], BF),
-    ("GX", [128], F32), ("BDG", [128], BF), ("LI", [72], I32), ("LU", [72], U16),
+    ("IDS", [128 * len(IDS)], BF), ("IDH", [128 * len(IDH)], F16), ("ZB", [128], BF), ("SEL", [1408], BF), ("ONES", [2048], BF),
+    ("CS", [512], BF), ("ZW", [240], F32), ("ZH", [240], F16),
+    ("PI", [8], I32), ("PJ", [8], I32), ("PCOL", [8], F32), ("IO8", [8], F32), ("IO128", [128], F32),
+    ("BLK", [8], F32), ("RMA", [16], BF), ("RMB", [16], BF),
+    ("C1024", [256], BF), ("CZ", [256], BF), ("MI", [512], F32), ("MASK", [512], F32), ("MASKB", [256], BF),
+    ("RV", [8, 4, 4], F32), ("RD", [128], F32), ("CP1", [128], BF), ("CP2", [128], BF), ("CP3", [128], BF), ("CP4", [128], BF),
+    ("JC", [128], BF), ("GX", [128], F32), ("BDG", [128], BF), ("LI", [48], I32), ("LU", [48], U16),
     ("PG", [128], F32), ("PGS", [8, 16], F32), ("M0", [8, 32], F32), ("K", [8, 32], I32),
     ("ZF", [8, 33], F32), ("I16", [128], F32), ("I20", [128], F32), ("YI", [256], I32), ("YF", [256], F16), ("D0", [256], F16),
     ("A16", [256], F16), ("B16", [256], F16), ("SLAB", [8, 32], BF), ("IDX0", [512], U16), ("IDX1", [512], U16),
-    ("LB", [8, 32], F32), ("W", [256], F32), ("TT", [8, 32], F32), ("SN", [256], BF), ("UU", [256], BF),
-    ("LE", [256], F32), ("G", [264], F32),
-    ("GI", [8], I32), ("NA", [8], I32), ("NB", [8], I32), ("NM", [8], F32), ("NX", [144], F32),
-    ("DF", [8, 32], I32), ("LOW", [8, 32], I32), ("INV", [256], BF), ("EE", [256], F32), ("CI", [256], BF), ("YY", [256], BF),
-    ("FL", [1024], BF), ("XP", [8, 32], F32), ("UJ", [128], BF),
+    ("LB", [8, 32], F32), ("W", [264], F32), ("TT", [8, 36], F32), ("SN", [256], BF), ("UU", [256], BF),
+    ("LE", [256], F32), ("LV", [256], BF), ("G", [264], F32), ("MG", [256], F32),
+    ("GI", [8], I32), ("NA", [8], I32), ("NB", [8], I32), ("NM", [16], F32), ("NX", [80], F16),
+    ("DF", [256], I32), ("LOW", [256], I32), ("INV", [256], BF), ("CI", [256], BF), ("YY", [256], BF),
+    ("FL", [1024], BF), ("UJ", [128], BF),
     ("PG2", [128], F32), ("Y2", [128], F32), ("U2", [128], BF), ("T0", [128], F32), ("WN", [128], BF),
-    ("Q0", [8, 16], F32), ("Q1", [8, 16], F32),
-    ("SL", [8, 32], F32), ("HI", [256], BF), ("LO", [256], BF),
+    ("Q0", [8, 16], F32), ("Q1", [8, 16], F32), ("XL", [384], F16),
     ("SA0", [2048, 2], BF), ("SB0", [2048, 2], BF), ("SA1", [2048, 2], BF), ("SB1", [2048, 2], BF),
     ("CA0", [4096], F16), ("CB0", [4096], F16), ("CA1", [4096], F16), ("CB1", [4096], F16),
-    ("AB0", [4096], F32), ("AB1", [4096], F32), ("WO", [4096], F32), ("YC", [640], F32), ("YT", [640], F32),
+    ("AB0", [4096], F32), ("AB1", [4096], F32), ("WO", [4096], F32), ("AC", [4096], F32), ("TCB", [128], BF), ("YC", [640], F32), ("YT", [640], F32),
     ("RN", [32], U16), ("NU", [64], U16),
 ]:
     _sb(_n, _s, _d)
 for _n in ("OUT", "RL", "TO", "RT"):
     _sb(_n, [NV - 1, 8, 16], F32)
-for _n in ("pS", "pT", "pI", "pK"):
+for _n in ("pS", "pI"):
     SCRATCH[_n] = ("psum", [128, 16, 32], F32)
-for _n in ("pV", "pF0", "pF1", "pY"):
+for _n in ("pK", "pV", "pF0", "pF1", "pF2", "pY"):
     SCRATCH[_n] = ("psum", [128, 512], F32)
 
 SEMAPHORES = (["cV", "cS", "cP", "cG", "dls", "dfp", "dpx", "dom", "dsg", "dco", "dst", "sent"]
-              + ["add%d" % v for v in range(NV)] + ["one%d" % v for v in range(2 * NV)] + ["cadd%d" % v for v in range(2 * NV)]
+              + ["add%d" % v for v in range(NV + 1)] + ["one%d" % v for v in range(2 * NV)] + ["cadd%d" % v for v in range(2 * NV)]
               + ["rn%d" % v for v in range(NV - 1)] + ["rl%d" % v for v in range(NV - 1)] + ["rt%d" % v for v in range(NV - 1)])
 
-CASES = ((1.1, 1.6, 90.0, 2400.0, 400.0), (1.15, 1.2, 70.0, 2600.0, 420.0), (1.4, 2.05, 100.0, 2500.0, 370.0),
-         (1.1, 1.5, 80.0, 3200.0, 280.0))
+CASES = ((1.1, 1.6, 90.0, 2400.0, 400.0), (1.15, 1.2, 70.0, 2600.0, 420.0), (1.05, 2.0, 80.0, 2500.0, 370.0),
+         (1.1, 1.5, 80.0, 3200.0, 300.0))
 EARLY = (2, 3, 4, 5, 6, 8)
-ROUNDS = 60
+ROUNDS = 60000
+SIZES = (40, 70, 110, 160)
+NOISES = (0, 100, 300, 800, 2000)
+LEAN = 0.1
 CLIMB = 140000
 FRESH = 8
 SEED = 82
@@ -173,7 +182,7 @@ def sweep(qs, pred, succ, prio, busy, lat, back):
             row.insert(lo, (t, t + b))
             start[c] = t
             for s in succ[c]:
-                u = t + b + lat[s] - busy[s] if back else t + lat[c]
+                u = t + b if qs[s] == qs[c] == 2 else t + b + lat[s] - busy[s] if back else t + lat[c]
                 if u > ready[s]:
                     ready[s] = u
                 left[s] -= 1
@@ -199,6 +208,7 @@ def plan(ops):
                     seen |= above[d] | 1 << d
             above.append(seen)
             pred.append(keep)
+        wait = [[d for d in p if ops[d]["q"] != "P" or o["q"] != "P"] for p, o in zip(pred, ops)]
         cs = [costs(ops, c) for c in CASES]
         busy, lat = cs[0]
         seed = [SEED]
@@ -208,7 +218,7 @@ def plan(ops):
             return (seed[0] >> 8) % m
 
         def score(order):
-            got = [replay(qs, pred, order, b, l) for b, l in cs]
+            got = [replay(qs, wait, order, b, l) for b, l in cs]
             return sum(r[0] / c[0] for r, c in zip(got, CASES)) / len(cs), [r[1:] for r in got]
 
         best = None
@@ -267,7 +277,7 @@ def plan(ops):
                 for b, l in cs:
                     rest = list(l)
                     for i in reversed(order):
-                        for d in pred[i]:
+                        for d in wait[i]:
                             if rest[d] < l[d] + rest[i]:
                                 rest[d] = l[d] + rest[i]
                         d = before[i]
@@ -284,7 +294,7 @@ def plan(ops):
                                 links.append((i, case))
                             i = a
                         else:
-                            i = max(pred[i], key=lambda d: done[d]) if pred[i] and st[i] > 0 else -1
+                            i = max(wait[i], key=lambda d: done[d]) if wait[i] and st[i] > 0 else -1
             i, case = links[rnd(len(links))]
             a = before[i]
             if a < 0:
@@ -309,7 +319,7 @@ def plan(ops):
             reach = max([last] + [far[j] for j in order[first:last + 1] if qs[j] == qs[i]])
             for k in range(len(cs)):
                 k = (k + case) % len(cs)
-                got[k] = retime(qs, pred, new, cs[k][0], cs[k][1], first, reach, starts[k], far, rests[k], ends[k] + room * CASES[k][0])
+                got[k] = retime(qs, wait, new, cs[k][0], cs[k][1], first, reach, starts[k], far, rests[k], ends[k] + room * CASES[k][0])
                 if got[k] is None:
                     break
                 room -= (got[k][0] - ends[k]) / CASES[k][0]
@@ -321,6 +331,120 @@ def plan(ops):
                 end = sum(e / c[0] for e, c in zip(ends, CASES)) / len(cs)
                 if end < best[0]:
                     best = (end, order, starts[0][0])
+        PLANS[key] = best
+    for i, o in enumerate(ops):
+        o["t"] = PLANS[key][2][i]
+    return PLANS[key][1]
+
+
+def reorder(win, after, qs, pred, wait, succ, busy, lat, done, rest, free, rnd):
+    inw = set(win)
+    nx, seen = [0.0] * 8, 0
+    for i in after:
+        if not seen >> qs[i] & 1:
+            seen |= 1 << qs[i]
+            nx[qs[i]] = rest[i]
+    amp, delta = NOISES[rnd(len(NOISES))], rnd(5) / 4.0
+    tail, prio, left, ready, todo, new = {}, {}, {}, {}, [], []
+    for i in reversed(win):
+        t = max(lat[i], busy[i] + nx[qs[i]])
+        for j in succ[i]:
+            u = (busy[i] if qs[i] == qs[j] == 2 else lat[i]) + (tail[j] if j in inw else rest[j])
+            if u > t:
+                t = u
+        tail[i] = t
+    for i in win:
+        prio[i] = tail[i] + amp * rnd(1000) / 1000.0
+        left[i] = sum(d in inw for d in pred[i])
+        ready[i] = max([done[d] for d in wait[i] if d not in inw] + [0.0])
+        if not left[i]:
+            todo.append(i)
+    while todo:
+        end, q = 1e18, 0
+        for i in todo:
+            t = max(ready[i], free[qs[i]]) + busy[i]
+            if t < end:
+                end, q = t, qs[i]
+        lo = max(free[q], min(ready[i] for i in todo if qs[i] == q))
+        cut = lo + delta * (end - lo) + 1e-6
+        c = max((i for i in todo if qs[i] == q and ready[i] <= cut), key=prio.get)
+        todo.remove(c)
+        t = max(ready[c], free[q])
+        free[q] = t + busy[c]
+        new.append(c)
+        for j in succ[c]:
+            if j in inw:
+                if t + lat[c] > ready[j] and not q == qs[j] == 2:
+                    ready[j] = t + lat[c]
+                left[j] -= 1
+                if not left[j]:
+                    todo.append(j)
+    return new
+
+
+def plan(ops):
+    n = len(ops)
+    key = tuple((o["q"], o["cost"], tuple(o["deps"])) for o in ops)
+    if key not in PLANS:
+        qs = ["VSPGYD".index(o["q"]) for o in ops]
+        above, pred, succ = [], [], [[] for _ in range(n)]
+        for i, o in enumerate(ops):
+            seen, keep = 0, []
+            for d in reversed(o["deps"]):
+                if not seen >> d & 1:
+                    keep.append(d)
+                    succ[d].append(i)
+                    seen |= above[d] | 1 << d
+            above.append(seen)
+            pred.append(keep)
+        wait = [[d for d in p if qs[d] != 2 or q != 2] for p, q in zip(pred, qs)]
+        cs = [costs(ops, c) for c in CASES]
+        seed = [SEED]
+
+        def rnd(m):
+            seed[0] = (seed[0] * 1103515245 + 12345) % 2147483648
+            return (seed[0] >> 8) % m
+
+        def score(order):
+            got = [replay(qs, wait, order, b, l) for b, l in cs]
+            return sum((r[0] + LEAN * sum(r[1]) / n) / c[0] for r, c in zip(got, CASES)) / len(cs), got
+
+        rank = {"setup": 0, (0, "pixel"): 1}
+        for v in range(NV + 1):
+            for k in ([(v, "merge"), (v, "sg"), (v, "keys")] + [(v - 1, c) for c in range(4)] + [(v, "seen"), (v, "list"), (v + 1, "pixel")]
+                      + [(v - 1, c) for c in range(4, 8)] + [(v, "co"), (v - 1, "tau"), (v, "a"), (v, "one")]):
+                rank[k] = len(rank)
+        order = sweep(qs, pred, succ, [-n * rank[o["kind"]] - i for i, o in enumerate(ops)], cs[0][0], cs[0][1], False)[0]
+        end, got = score(order)
+        best, rests = (end, order, got[0][1]), {}
+        for r in range(ROUNDS):
+            case = rnd(len(cs))
+            (busy, lat), (start, done) = cs[case], got[case][1:]
+            if case not in rests:
+                od, rest, nx = sorted(order, key=lambda i: start[i]), [0.0] * n, [0.0] * 8
+                for i in reversed(od):
+                    t = max(busy[i] + nx[qs[i]], lat[i])
+                    for j in succ[i]:
+                        if lat[i] + rest[j] > t and not qs[i] == qs[j] == 2:
+                            t = lat[i] + rest[j]
+                    rest[i] = nx[qs[i]] = t
+                rests[case] = (od, rest)
+            od, rest = rests[case]
+            w = SIZES[rnd(len(SIZES))]
+            k0 = rnd(n - 10 + w) - w
+            k0, k1 = max(k0, 0), min(n, k0 + w)
+            free = [0.0] * 8
+            for i in od[max(k0 - 300, 0):k0]:
+                free[qs[i]] = start[i] + busy[i]
+            new = od[:k0] + reorder(od[k0:k1], od[k1:k1 + 300], qs, pred, wait, succ, busy, lat, done, rest, free, rnd) + od[k1:]
+            room = SLACK * (1.0 - r / ROUNDS) * rnd(1000) / 1000.0
+            if replay(qs, wait, new, busy, lat)[0] > got[case][0] + 4 * room * CASES[case][0] + 300.0:
+                continue
+            e2, g2 = score(new)
+            if e2 <= end + room:
+                end, got, order, rests = e2, g2, new, {}
+                if end < best[0]:
+                    best = (end, order, got[0][1])
         PLANS[key] = best
     for i, o in enumerate(ops):
         o["t"] = PLANS[key][2][i]
@@ -426,23 +550,22 @@ def build(g, core, T, topo):
     dma("Y", Y, T.LSI[:], T.ls[:], 65536, (), ["LSI"], "dls")
     dma("S", S, T.FPI[:], T.fp[:], 4096, (), ["FPI"], "dfp")
     dma("Y", Y, T.PXI[:], T.px[:], 524288, (), ["PXI"], "dpx")
-    dma("S", S, T.OMI[:], T.om[:], 20480, (), ["OMI"], "dom")
-    dma("Y", Y, T.SG[:, 0:4096], T.sg[:], 1048576, (), ["SG"], "dsg")
-    dma("Y", Y, T.CO[:, 0:4096], T.co[:], 1048576, (), ["CO"], "dco")
+    dma("S", S, T.OMI[:, 0:40], T.om[:], 20480, (), ["OMI"], "dom")
+    dma("Y", Y, T.SG[:, 16:4112], T.sg[:], 1048576, (), ["SG"], "dsg")
+    dma("Y", Y, T.CO[:, 16:4112], T.co[:], 1048576, (), ["CO"], "dco")
 
     ms(T.ONE[:], 1.0, 128, ["ONE"])
     iota(T.PI[:, 0:1], [[0, 1]], 0, 1, 1, ["PI"], False)
     asel(T.PERM[:], T.ONE[:], [[-16, 8], [1, 16]], -15, 128, ["ONE"], ["PERM"])
     asel(T.IDF[:], T.ONE[:], [[-1, 128]], 0, 128, ["ONE"], ["IDF"])
-    iota(T.LI[:, 0:40], [[1, 40]], 0, 0, 40, ["LI0"], False)
-    iota(T.LI[:, 40:48], [[32, 8]], 31, 0, 8, ["LI1"], False)
-    iota(T.LI[:, 48:64], [[1, 16]], -1, 0, 16, ["LI2"], False)
-    iota(T.LI[:, 64:72], [[32, 8]], 32, 0, 8, ["LI3"], False)
+    iota(T.LI[:, 0:24], [[1, 8], [16, 3]], 0, 0, 24, ["LI0"], False)
+    iota(T.LI[:, 24:32], [[0, 2], [2, 4]], 0, 0, 8, ["LI1"], False)
+    iota(T.LI[:, 32:48], [[1, 2], [32, 8]], 31, 0, 16, ["LI2"], False)
     iota(T.IO8[:], [[1, 8]], 0, 0, 8, ["IO8"])
-    iota(T.IO144[:], [[0, 9], [1, 16]], 0, 0, 144, ["IO144"])
+    iota(T.IO128[:], [[0, 8], [1, 16]], 0, 0, 128, ["IO128"])
     iota(T.CP2[:], [[0, 8], [128, 16]], -2048, 0, 128, ["CP2"])
     iota(T.CP3[:], [[0, 8], [-128, 16]], 1920, 0, 128, ["CP3"])
-    iota(T.JC[:], [[0, 8], [1, 16]], 8, 0, 128, ["JC"])
+    iota(T.JC[:], [[0, 8], [1, 16]], 0, 0, 128, ["JC"])
     iota(T.GX[:], [[1, 8], [0, 16]], 0, 0, 128, ["GX"])
     for u in range(4):
         iota(T.RV[:, :, u, :], [[0, 8], [4, 2], [8, 2]], (0, 2, 1, 3)[u], 0, 32, [("RV", u)])
@@ -451,20 +574,37 @@ def build(g, core, T, topo):
     iota(T.C1024[:], [[0, 256]], 1024, 0, 256, ["C1024"])
     iota(T.MI[:], [[0, 16], [1, 32]], 0, 0, 512, ["MI"])
     act(T.MASK[:], T.MI[:], 512, ["MI"], ["MASK"], func=ACT.Sign)
-    asel(T.MASKB[:], T.ONES[:, 0:256], [[0, 8], [1, 32]], 0, 256, ["ONES"], ["MASKB"], 0.0, 0, ALU.not_equal)
-    act(T.pT[:, 8:16, :], T.MI[:, 0:256], 256, ["MI"], ["SC"], "pT", scale=2.0 ** -5)
-    asel(T.SEL[:], T.ONES[:], [[-1, 16], [-16, 8], [0, 16]], 0, 2048, ["ONES"], ["SEL"])
-    ts(T.PJ[:, 0:1], T.PI[:, 0:1], 15, None, ALU.bitwise_and, None, 1, ["PI"], ["PJ0"])
-    ts(T.PJ[:, 1:2], T.PI[:, 0:1], 4, None, ALU.arith_shift_right, None, 1, ["PI"], ["PJ1"])
+    asel(T.MASKB[:], T.ONES[:, 0:256], [[0, 8], [1, 32]], 0, 256, ["ONES"], ["MASKB"], 2.0 ** -5, 0, ALU.not_equal)
+    asel(T.CZ[:], T.C1024[:], [[0, 8], [1, 32]], 0, 256, ["C1024"], ["CZ"], 2.0 ** 25, 0, ALU.not_equal)
+    act(T.pV[:, 256:512], T.MI[:, 0:256], 256, ["MI"], ["SC"], "pV", scale=2.0 ** -5)
+    act(T.BD[:], T.MI[:, 0:256], 256, ["MI"], ["BD"], scale=0.0)
+    act(T.BD[:, 0:256:32], T.IO8[:], 8, ["IO8"], ["BD"], scale=0.0, bias=2.0 ** 40)
+    ms(T.CS[:], -2.0 ** -13, 256, ["CS"])
+    for u in range(3):
+        n = (4, 4, 3)[u]
+        c = slice(512 * u, 512 * u + 128 * n)
+        asel(T.SEL[:, c], T.CS[:, 0:128 * n], [[-1, n], [-12, 8], [0, 16]], -4 * u, 128 * n, ["CS"], [("SEL", u)])
+        asel(T.SEL[:, c], T.SEL[:, c], [[0, n], [-12, 8], [0, 16]], -11, 128 * n, [("SEL", u)], [("SEL", u)], -2.0 ** -13, 1, ALU.not_equal)
+    for k, (c0, c1, o0, o1) in enumerate(((15, None, ALU.bitwise_and, None), (4, None, ALU.arith_shift_right, None),
+                                          (7, None, ALU.bitwise_and, None), (3, 1, ALU.arith_shift_right, ALU.bitwise_and))):
+        ts(T.PJ[:, k:k + 1], T.PI[:, 0:1], c0, c1, o0, o1, 1, ["PI"], ["PJ%d" % k])
     cp(T.PCOL[:, 0:2], T.PJ[:, 0:2], 2, ["PJ0", "PJ1"], ["PC0"])
     ts(T.PCOL[:, 3:4], T.PJ[:, 0:1], 128.0, None, ALU.mult, None, 1, ["PJ0"], ["PC3"])
-    cp(T.LU[:], T.LI[:], 72, ["LI0", "LI1", "LI2", "LI3"], ["LU"])
-    ms(T.LU[:, 48:49], 7, 1, ["LU"])
+    tt(T.PCOL[:, 4:5], T.PJ[:, 2:3], T.PJ[:, 1:2], ALU.is_equal, 2, ["PJ1", "PJ2"], ["PC4"])
+    ts(T.PCOL[:, 5:6], T.PJ[:, 3:4], -5.0, T.PCOL[:, 4:5], ALU.add, ALU.mult, 1, ["PJ3", "PC4"], ["PC5"])
+    ts(T.PCOL[:, 5:6], T.PCOL[:, 5:6], 8.0, 40.0, ALU.mult, ALU.add, 1, ["PC5"], ["PC5"])
+    ts(T.PCOL[:, 6:7], T.PJ[:, 3:4], -8.0, T.PCOL[:, 4:5], ALU.add, ALU.mult, 1, ["PJ3", "PC4"], ["PC6"])
+    ts(T.PCOL[:, 6:7], T.PCOL[:, 6:7], 8.0, None, ALU.add, None, 1, ["PC6"], ["PC6"])
+    ts(T.LU[:, 0:24], T.LI[:, 0:24], T.PCOL[:, 4:5], T.PCOL[:, 5:6], ALU.mult, ALU.add, 24, ["LI0", "PC4", "PC5"], ["LU0"])
+    ts(T.LU[:, 24:32], T.LI[:, 24:32], T.PCOL[:, 4:5], T.PCOL[:, 6:7], ALU.mult, ALU.add, 8, ["LI1", "PC4", "PC6"], ["LU1"])
+    cp(T.LU[:, 32:48], T.LI[:, 32:48], 16, ["LI2"], ["LU"])
     cp(T.FPU[:], T.FPI[:], 8, ["FPI"], ["FPU"])
-    ts(T.MK[:], T.IO144[:], T.PCOL[:, 0:1], None, ALU.is_equal, None, 144, ["IO144", "PC0"], ["MK"])
+    ms(T.ZW[:], 0.0, 240, ["ZW"])
+    ts(T.ZW[:, 112:128], T.IO128[:, 0:16], T.PCOL[:, 0:1], None, ALU.is_equal, None, 16, ["IO128", "PC0"], ["ZW"])
+    act(T.ZH[:], T.ZW[:], 240, ["ZW"], ["ZH"])
     ts(T.BLK[:], T.IO8[:], T.PCOL[:, 1:2], None, ALU.is_equal, None, 8, ["IO8", "PC0"], ["BLK"])
     ts(T.BDG[:], T.GX[:], T.PCOL[:, 1:2], -2.0 ** 19, ALU.is_equal, ALU.mult, 128, ["GX", "PC0"], ["BDG"])
-    for buf, key, c0, c1 in ((T.RMA, "RMA", -4096.0, -1.0), (T.RMB, "RMB", -4096.0, 1.0), (T.BLKB, "BLKB", 2.0 ** 36, 0.0)):
+    for buf, key, c0, c1 in ((T.RMA, "RMA", -4096.0, -1.0), (T.RMB, "RMB", -4096.0, 1.0)):
         act(buf[:, 0:8], T.BLK[:], 8, ["BLK"], [key + "a"], scale=c0)
         act(buf[:, 8:16], T.BLK[:], 8, ["BLK"], [key + "b"], scale=c1)
     ms(T.ZB[:], 0.0, 64, ["ZB"])
@@ -478,27 +618,33 @@ def build(g, core, T, topo):
     act(T.NIF[:], T.IDF[:], 128, ["IDF"], ["NIF"], scale=-1.0)
     act(T.I15[:], T.IDF[:], 128, ["IDF"], ["I15"], scale=15.0)
     act(T.I16[:], T.IDF[:], 128, ["IDF"], ["I16"], scale=2.0 ** -4)
-    act(T.I20[:], T.IDF[:], 128, ["IDF"], ["I20"], scale=2.0 ** 20)
+    act(T.I20[:], T.IDF[:], 128, ["IDF"], ["I20"], scale=-2.0 ** 20 if ON_S["T0"] else 2.0 ** 20)
     act(T.PERM15[:], T.PERM[:], 128, ["PERM"], ["PERM15"], scale=15.0)
-    act(T.CP1[:], T.RV[:], 128, RVK, ["CP1"], scale=-2.0 ** 24)
-    tt(T.RD[:], T.RV[:], T.IO144[:, 0:128], ALU.subtract, 256, RVK + ["IO144"], ["RD"])
-    ts(T.pV[:, 384:512], T.RD[:], 2.0 ** 20, 64.0, ALU.mult, ALU.add, 128, ["RD"], ["TC"], "pV")
-    ts(T.pV[:, 0:8], T.IO8[:], 0.0, None, ALU.mult, None, 8, ["IO8"], ["pVa"], "pV")
-    ms(T.SG[:, 4096:4112], 0.5, 16, ["SGz"])
-    ms(T.CO[:, 4096:4112], 0.0, 16, ["COz"])
-    for buf, at, c, key in ((T.ZF, 32, M4096 + 2.0 ** 24, "ZFe"), (T.SLAB, 0, 4224.0, "SLAB0"), (T.LB, 0, 1.0, "LB0"), (T.SL, 0, 1.0, "SL0")):
+    act(T.CP1[:], T.RV[:], 128, RVK, ["CP1"], scale=-2.0 ** 25, bias=2.0 ** 28)
+    act(T.CP4[:], T.JC[:], 128, ["JC"], ["CP4"], scale=128.0, bias=-6080.0)
+    act(T.MG[:], T.MASK[:, 0:256], 256, ["MASK"], ["MG"], scale=2.0 ** 22, bias=127.0)
+    act(T.RD[:], T.RV[:], 128, RVK, ["RD"], scale=2.0 ** 21, bias=(ON_S["T0"] - 8.5) * 2.0 ** 20)
+    group(T.pF2[:, 0:128], [(T.IDF[:], T.RD[:], 512), (I["NI1"], T.JC[:], 128)], True, ["IDF", "RD", "NI1", "JC"], ["pF2"], "pF2")
+    act(T.TCB[:], T.pF2[:, 0:128], 128, ["pF2"], ["TCB"], "pF2")
+    ms(T.SG[:, 0:16], 32.0, 16, ["SGz"])
+    ms(T.CO[:, 0:16], 0.0, 16, ["COz"])
+    ms(T.OMI[:, 40:48], 0, 8, ["OMz"])
+    ms(T.NM[:, 8:16], 0.0, 8, ["NMz"])
+    ms(T.W[:, 0:1], 0.0, 1, ["W0"])
+    for buf, at, c, key in ((T.ZF, 32, M4096 + 2.0 ** 24, "ZFe"), (T.SLAB, 0, -8192.0, "SLAB0"), (T.LB, 0, 2.0 ** 35, "LB0")):
         act(buf[:, :, at], T.IO8[:], 8, ["IO8"], [key], scale=0.0, bias=c)
-    ms(T.G[:, 0:1], 0.0, 1, ["G0"])
-    ms(T.LOW[:, :, 0], 0, 8, ["LOW0"])
+    ms(T.G[:, 0:1], 128.0, 1, ["G0"])
+    ms(T.TT[:, :, 32:36], 2.0 ** 36, 32, ["TTe"])
 
     cp(T.RAWF[:, 0:128], T.LSI[:], 128, ["LSI"], ["RAW0"])
     cp(T.RAWF[:, 128:256], T.PXI[:].indirect(T.FPU[:]), 0, ["PXI", "FPU"], ["RAW1"], gat=128)
     for h in range(2):
         c = slice(128 * h, 128 * h + 128)
         ts(T.AQ[:, c], T.RAWF[:, c], M256, -M256, ALU.add, ALU.add, 128, ["RAW%d" % h], ["AQ%d" % h])
-    for v in range(NV):
-        tt(T.OMB[:, 128 * v:128 * v + 128], T.OMI[:].indirect(T.LU[:, 8 * v:8 * v + 8]), T.MK[:, 0:128], ALU.mult, 256,
-           ["OMI", "LU", "MK"], [("OMB", v)])
+    act(T.OMG[:], T.OMI[:].indirect(T.LU[:, 0:24]), 0, ["OMI", "OMz", "LU0"], ["OMG"], scale=2.0 ** 36, gat=384)
+    mm([(T.pY[:, 0:40], T.ZW[:, 112 - 16 * c:240 - 16 * c], T.OMG[:, 48 * c:48 * c + 40], c == 0, c == 7) for c in range(8)], 2048,
+       ["ZW", "OMG"], ["pY"], "pY")
+    act(T.BND[:], T.pY[:, 0:40], 40, ["pY"], ["BND"], "pY")
     for c2 in range(2):
         c = slice(512 * c2, 512 * c2 + 512)
         bk = "pF%d" % c2
@@ -521,67 +667,81 @@ def build(g, core, T, topo):
         AB, WT = T["AB%d" % e], T["AB%d" % (1 - e)]
         IDX, SA, SB, CA, CB = T["IDX%d" % e], T["SA%d" % e], T["SB%d" % e], T["CA%d" % e], T["CB%d" % e]
         kind[0] = (v, "pixel")
-        pix, lane = T.pK[:, 8:16, 0:16], T.pK[:, 0:8, 0:16]
+        pix, lane = T.pI[:, 8:16, 0:16], T.pI[:, 0:8, 0:16]
+        PA, PB = [("pI", 0), ("pI", 1)], [("pI", 2), ("pI", 3)]
         if v == 0:
             group(lane, [(T.AQ[:, 0:128], T.I15[:], 512), (T.RAWF[:, 0:128], T.IDF[:], 512), (I["IB"], T.CP2[:], 128)], True,
-                  ["AQ0", "RAW0", "IDF", "I15", "IB", "CP2"], ["pKa"], "pK")
+                  ["AQ0", "RAW0", "IDF", "I15", "IB", "CP2"], PA, "pI")
             group(pix, [(T.AQ[:, 128:256], T.PERM15[:], 512), (T.RAWF[:, 128:256], T.PERM[:], 512), (I["IB"], T.CP3[:], 128)], True,
-                  ["AQ1", "RAW1", "PERM", "PERM15", "IB", "CP3"], ["pKb"], "pK")
+                  ["AQ1", "RAW1", "PERM", "PERM15", "IB", "CP3"], PB, "pI")
         else:
             act(T.PG[:], T.PK[:].indirect(T.RN[:, 8 * v - 8:8 * v]), 0, PKK + [("RN", v - 1)], ["PG"], gat=128)
-            group(pix, [(T.PG[:], T.PERM[:], 512)], True, ["PG", "PERM"], ["pKb"], "pK")
-        act(T.PGS[:], pix, 128, ["pKb"], ["PGS"], "pK")
+            group(pix, [(T.PG[:], T.PERM[:], 512)], True, ["PG", "PERM"], PB, "pI")
+        act(T.PGS[:], pix, 128, PB, ["PGS"], "pI")
         kind[0] = (v, "merge")
         if v:
-            group(lane, [(I["IB"], T.CP1[:], 128), (I["IB"], T.CP2[:], 128)], True, ["IB", "CP1", "CP2"], ["pKa"], "pK", False)
-            stage(T.Q1, "Q1", T.RT[:, v - 1, :, 0:8], T.RT[:, v - 1, :, 8:16], 128, [("RT", v - 1)])
-            for dst, dk, src, sk in ((T.Q0, "Q0", T.Q1, "Q1"), (T.Q1, "Q1", T.Q0, "Q0"), (T.Q0, "Q0", T.Q1, "Q1")):
-                stage(dst, dk, src[:, :, 0:8], src[:, :, 8:16], 128, [sk + "a", sk + "b"])
-            tt(T.pV[:, 0:128], T.Q0[:], T.pV[:, 384:512], ALU.add, 128, ["Q0a", "Q0b", "TC"], ["pVa"], "pV")
-            tt(T.Q1[:], T.RL[:, v - 1], T.pV[:, 0:128], ALU.min, 128, [("RL", v - 1), "pVa"], ["Q1a", "Q1b"], "pV")
-            ts(T.AQ[:, 0:128], T.Q1[:], M256, -M256, ALU.add, ALU.add, 128, ["Q1a", "Q1b"], ["AQ0"])
-            group(lane, [(T.I15[:], T.AQ[:, 0:128], 512), (T.IDF[:], T.Q1[:], 512)], False, ["AQ0", "Q1a", "Q1b", "I15", "IDF"], ["pKa"], "pK")
+            group(lane, [(I["IB"], T.CP1[:], 128), (I["IB"], T.CP4[:], 128)], True, ["IB", "CP1", "CP4"], PA, "pI", False)
+            lst, lk = T.RL[:, v - 1], [("RL", v - 1)]
+            if not SENDER:
+                stage(T.Q1, "Q1", T.RT[:, v - 1, :, 0:8], T.RT[:, v - 1, :, 8:16], 128, [("RT", v - 1)])
+                for dst, dk, src, sk in ((T.Q0, "Q0", T.Q1, "Q1"), (T.Q1, "Q1", T.Q0, "Q0")):
+                    stage(dst, dk, src[:, :, 0:8], src[:, :, 8:16], 128, [sk + "a", sk + "b"])
+                for x, o in enumerate((ALU.min, ALU.max)):
+                    tt(T.pS[:, 0:8, x:16:2], T.Q1[:, :, 0:8], T.Q1[:, :, 8:16], o, 128, ["Q1a", "Q1b"], EVK[0][2 * x:2 * x + 2], "pS")
+                tt(T.pV[:, 0:128], T.TCB[:], T.pS[:, 0:8, 0:16], ALU.add, 128, EVK[0] + ["TCB"], ["pVa"], ["pV", "pS"])
+                tt(T.Q1[:], T.RL[:, v - 1], T.pV[:, 0:128], ALU.max, 128, [("RL", v - 1), "pVa"], ["Q1a", "Q1b"], "pV")
+                lst, lk = T.Q1[:], ["Q1a", "Q1b"]
+            ts(T.AQ[:, 0:128], lst, M256, -M256, ALU.add, ALU.add, 128, lk, ["AQ0"])
+            group(lane, [(T.I15[:], T.AQ[:, 0:128], 512), (T.IDF[:], lst, 512)], False, ["AQ0", "I15", "IDF"] + lk, PA, "pI")
         for k in range(4):
             a, b = k % 2, 16 * (k % 2)
             for hf in range(2):
                 for x, o in enumerate((ALU.min, ALU.max)):
                     if k == 0:
-                        i0, i1, rk, bk = T.PGS[:, :, 8 * hf:8 * hf + 8], T.pK[:, 0:8, 8 * hf:8 * hf + 8], ["PGS", "pKa"], ["pK"]
+                        i0, i1, rk, bk = T.PGS[:, :, 8 * hf:8 * hf + 8], T.pI[:, 0:8, 8 * hf:8 * hf + 8], ["PGS"] + PA, ["pI"]
                     else:
-                        i0, i1 = T.M0[:, :, 16 - b + 8 * hf:24 - b + 8 * hf], T.pT[:, 0:8, 16 - b + 8 * hf:24 - b + 8 * hf]
-                        rk, bk = EVK[1 - a] + ODK[1 - a], ["pT"]
+                        i0, i1 = T.M0[:, :, 16 - b + 8 * hf:24 - b + 8 * hf], T.pS[:, 0:8, 16 - b + 8 * hf:24 - b + 8 * hf]
+                        rk, bk = EVK[1 - a] + ODK[1 - a], ["pS"]
                     if hf == 0:
-                        tt(T.pT[:, 0:8, b + x:b + 16:2], i0, i1, o, 64, rk, EVK[a][2 * x:2 * x + 2], bk + ["pT"])
+                        tt(T.pS[:, 0:8, b + x:b + 16:2], i0, i1, o, 64, rk, EVK[a][2 * x:2 * x + 2], bk + ["pS"])
                     else:
                         tt(T.M0[:, :, b + x:b + 16:2], i0, i1, o, 64, rk, ODK[a][2 * x:2 * x + 2], bk)
         for x, o in enumerate((ALU.min, ALU.max)):
-            tt(T.K[:, :, x:32:2], T.M0[:, :, 16:32], T.pT[:, 0:8, 16:32], o, 128, EVK[1] + ODK[1], ["K" + "ab"[x]], "pT")
+            tt(T.K[:, :, x:32:2], T.M0[:, :, 16:32], T.pS[:, 0:8, 16:32], o, 128, EVK[1] + ODK[1], ["K" + "ab"[x]], "pS")
         KK = ["Ka", "Kb"]
         act(T.ZF[:, :, 0:32], T.K[:], 256, KK, ["ZF"], bias=M4096)
         ts(T.YI[:], T.K[:], 2175, None, ALU.bitwise_and, None, 256, KK, ["YI"])
-        ts(T.YF[:], T.YI[:], -1920.0, None, ALU.add, None, 256, ["YI"], ["YF"])
+        ts(T.YF[:], T.YI[:], -1088.0, None, ALU.add, None, 256, ["YI"], ["YF"])
+        if ON_S["YF"]:
+            act(T.D0[:], T.YI[:], 256, ["YI"], ["D0"], scale=-2.0, bias=2176.0)
+        else:
+            ts(T.D0[:], T.YF[:], -2.0, None, ALU.mult, None, 128, ["YF"], ["D0"])
         act(T.SLAB[:, :, 1:32], T.ZF[:, :, 1:32], 248, ["ZF"], ["SLAB"], scale=2.0 ** -19, bias=127.50390625 - M4096 * 2.0 ** -19)
-        ts(T.D0[:], T.YF[:], 0.0, 4096.0, ALU.is_lt, ALU.mult, 128, ["YF"], ["D0"])
-        scan(T.A16[:], T.D0[:], T.YF[:], 128.0, ALU.min, ALU.max, 128, ["D0", "YF"], ["A16"])
-        scan(T.B16[:], T.D0[:], T.YF[:], 0.0, ALU.add, ALU.min, 128, ["D0", "YF"], ["B16"])
-        for x, (src, sk, add, bk, keys) in enumerate(((T.A16, "A16", -4096.0 - 128.0, "pI", [("pI", 0), ("pI", 1)]),
-                                                      (T.B16, "B16", 61440.0 - 128.0, "pS", ["pSa"]))):
+        scan(T.A16[:], T.D0[:], T.YF[:], 960.0, ALU.min, ALU.max, 128, ["D0", "YF"], ["A16"])
+        scan(T.B16[:], T.D0[:], T.YF[:], -1088.0, ALU.max, ALU.min, 128, ["D0", "YF"], ["B16"])
+        for x, (src, sk, add, bk, keys) in enumerate(((T.A16, "A16", -30720.0 - 112.0, "pI", [("pI", 0), ("pI", 1)]),
+                                                      (T.B16, "B16", 34816.0 - 112.0, "pS", ["pSa"]))):
             its = []
             for h in range(2):
                 o = T[bk][:, 4 * h:4 * h + 4, :]
                 its.append((o, T.SLAB[:, :, h:32:2], I["IB"], True, False))
                 its.append((o, src[:, h:256:2], I["IH32"], False, True))
             mm(its, 512, [sk, "SLAB", "SLAB0", "IB", "IH32"], keys, bk)
-            ts(IDX[:, 256 * x:256 * x + 256], T[bk][:, 0:8, :], add, 4096.0, ALU.add, ALU.min, 256, keys, [("IDX", e, x)], bk)
+            if ON_S["IDX"] and x == 0:
+                act(IDX[:, 0:256], T[bk][:, 0:8, :], 256, keys, [("IDX", e, x)], bk, func=ACT.Relu, bias=add)
+            else:
+                ts(IDX[:, 256 * x:256 * x + 256], T[bk][:, 0:8, :], add, 0.0, ALU.add, ALU.max, 256, keys, [("IDX", e, x)], bk)
         kind[0] = (v, "keys")
         group(T.pI[:, 0:8, :], [(T.IDF[:], T.ZF[:, :, 1:33], 1024), (T.NIF[:], T.ZF[:, :, 0:32], 1024)], True,
               ["ZF", "ZFe", "IDF", "NIF"], [("pI", 0), ("pI", 1)], "pI")
         act(T.LB[:, :, 1:32], T.pI[:, 0:8, 1:32], 248, [("pI", 0), ("pI", 1)], ["LB"], "pI", scale=4096.0)
+        asel(T.BD[:, 1:256:32], T.BND[:, 8 * v:8 * v + 8], [[0, 8]], 0, 8, ["BND"], ["BD"], 0.0, 0)
         if not last:
-            group(T.pK[:, 8:16, :], [(I["IH"], T.B16[:], 256), (I["NIH"], T.A16[:], 256), (I["I2"], T.C1024[:], 256)], True,
+            group(T.pK[:, 256:512], [(I["IH"], T.B16[:], 256), (I["NIH"], T.A16[:], 256), (I["I2"], T.C1024[:], 256)], True,
                   ["A16", "B16", "IH", "NIH", "I2", "C1024"], ["pKb"], "pK")
-            group(T.pK[:, 0:8, :], [(T.I16[:], T.ZF[:, :, 0:32], 1024), (I["N21"], T.C1024[:], 256), (I["NHALF"], T.C1024[:], 256),
-                                    (I["IH"], T.A16[:], 256)], True, ["ZF", "A16", "I16", "N21", "NHALF", "C1024", "IH"], ["pKa"], "pK", False)
+            group(T.pK[:, 0:256], [(T.I16[:], T.ZF[:, :, 0:32], 1024), (I["N21"], T.CZ[:], 256), (I["N5"], T.C1024[:], 256),
+                                    (I["IHH"], T.A16[:], 256), (I["IHH"], T.B16[:], 256)], True,
+                  ["ZF", "A16", "B16", "I16", "N21", "N5", "C1024", "CZ", "IHH"], ["pKa"], "pK", False)
         kind[0] = (v, "sg")
         def piece(buf, c, n):
             return buf[:, 512 * (c % 4):512 * (c % 4 + n), c // 4]
@@ -600,148 +760,206 @@ def build(g, core, T, topo):
                 act(piece(SB, c, n), src, 0, rk, wk, gat=512 * n)
         SAK, SBK = [("SA", e, c) for c in range(8)], [("SB", e, c) for c in range(8)]
         nr = 8 if last else 16
-        mm([(T.pS[:, 0:nr, 0], T.OMB[:, 128 * v:128 * v + 128], T.BLKB[:, 0:nr], True, False)], 256,
-           [("OMB", v), "BLKBa", "BLKBb"], ["pSa", "pSb"], "pS")
+        mm([(T.pS[:, 0:nr, 0], T.C1024[:, 0:128], T.RMA[:, 0:nr], True, False)], 64, ["C1024", "RMAa", "RMAb"], ["pSa", "pSb"], "pS")
         sums = ((SA, SAK, T.RMA, "RMA"), (SB, SBK, T.RMB, "RMB"))[VADD[v]:]
         for h in range(2):
             for x, (src, keys, rm, rk) in enumerate(sums):
                 mm([(T.pS[:, 0:nr, s], src[:, s // 2:2048:16, h], rm[:, 0:nr], False, x == len(sums) - 1 and s == 31)
                     for s in range(2 - h, 32, 2)], 16 * 64, keys[4 * h:4 * h + 4] + [rk + "a", rk + "b"], ["pSa", "pSb"], "pS")
-        if not VADD[v]:
-            dma("G", g, SB[:], SA[:], 2 * 1048576, SAK, SBK, "add%d" % v, accum_op=ALU.add, max_dma_last_dim=4096)
+        for hf, n in runs(0, 2 * (1 - VADD[v]), ADDW[v]):
+            c, pk = slice(1024 * hf, 1024 * (hf + n)), [4 * h + u for h in range(2) for u in range(2 * hf, 2 * (hf + n))]
+            dma("G", g, SB[:, c, :], SA[:, c, :], n * 1048576, [SAK[u] for u in pk], [SBK[u] for u in pk], "add%d" % (v + hf),
+                accum_op=ALU.add, max_dma_last_dim=4096)
         kind[0] = (v, "seen")
-        tt(T.W[:], T.LB[:], T.pS[:, 0:8, :], ALU.mult, 256, ["LB", "LB0", "pSa"], ["W"], "pS")
+        tt(T.W[:, 1:257], T.LB[:], T.pS[:, 0:8, :], ALU.mult, 256, ["LB", "LB0", "pSa"], ["W"], "pS")
+        if not last and ON_S["SN"]:
+            act(T.SN[:], T.pS[:, 8:16, :], 256, ["pSb"], ["SN"], "pS", func=ACT.Sign, bias=-0.5)
+        elif not last:
+            ts(T.SN[:], T.pS[:, 8:16, :], 0.5, 0.5, ALU.is_gt, ALU.subtract, 256, ["pSb"], ["SN"], "pS")
+        scan(T.pV[:, 0:256], T.W[:, 0:256], T.BD[:], 0.0, ALU.add, ALU.max, 256, ["BD", "W", "W0"], ["pVa"], "pV")
         if not last:
-            ts(T.SN[:], T.pS[:, 8:16, :], 0.5, None, ALU.is_gt, None, 256, ["pSb"], ["SN"], "pS")
-        scan(T.pV[:, 1:257], T.MASK[:, 0:256], T.W[:], 0.0, ALU.mult, ALU.add, 256, ["MASK", "W"], ["pVa"], "pV")
+            tt(T.UU[:], T.SN[:], T.pK[:, 256:512], ALU.mult, 256, ["SN", "pKb"], ["UU"], "pK")
+            group(T.pK[:, 0:256], [(I["HALF" if ON_S["SN"] else "IB"], T.UU[:], 256)], False, ["IB", "HALF", "UU"], ["pKa"], "pK", not ON_S["LV"])
+        tt(T.TT[:, :, 0:32], T.LB[:], T.pV[:, 0:256], ALU.min, 256, ["LB", "LB0", "pVa"], ["TT"], "pV")
+        hk = [("pI", 0), ("pI", 1), ("pI", 2)]
+        mm([(T.pI[0:96, 4 * h:4 * h + 4, :], T.TT[:, :, h:36:3], T.IDF[:], True, True) for h in range(3)], 1536, ["TT", "TTe", "IDF"], hk, "pI")
+        act(T.XL[0:96], T.pI[0:96, 0:12, :], 384, hk, ["XL"], "pI", scale=2.0 ** -28, bias=-128.0)
         if not last:
-            tt(T.UU[:], T.SN[:], T.pK[:, 8:16, :], ALU.mult, 256, ["SN", "pKb"], ["UU"], "pK")
-            group(T.pK[:, 0:8, :], [(I["IB"], T.UU[:], 256)], False, ["IB", "UU"], ["pKa"], "pK")
-        tt(T.TT[:], T.LB[:], T.pV[:, 0:256], ALU.min, 256, ["LB", "LB0", "pVa"], ["TT"], "pV")
-        act(T.SL[:, :, 1:32], T.TT[:, :, 1:32], 248, ["TT"], ["SL"], func=ACT.Relu, scale=2.0 ** -41)
-        hk, lk = [("pI", 0), ("pI", 1)], [("pI", 2), ("pI", 3)]
-        mm([(T.pI[:, 4 * h:4 * h + 4, :], T.SL[:, :, h:32:2], T.NIF[:], True, True) for h in range(2)], 1024, ["SL", "SL0", "NIF"], hk, "pI")
-        act(T.HI[:], T.pI[:, 0:8, :], 256, hk, ["HI"], "pI")
-        bk, lk = ("pK", ["pKb"]) if last else ("pI", lk)
-        mm([(T[bk][:, 8 + 4 * h:12 + 4 * h, :], T.SL[:, :, h:32:2], T.NIF[:], h == 0, False) for h in range(2)], 1024, ["SL", "SL0", "NIF"], lk, bk)
-        group(T[bk][:, 8:16, :], [(I["NIB"], T.HI[:], 256)], False, ["NIB", "HI"], lk, bk)
-        act(T.LO[:], T[bk][:, 8:16, :], 256, lk, ["LO"], bk)
-        if not last:
-            tt(T.LE[:], T.TT[:], T.pK[:, 0:8, :], ALU.min, 256, ["TT", "pKa"], ["LE"], "pK")
-            scan(T.G[:, 1:257], T.MASK[:, 0:256], T.LE[:], 0.0, ALU.mult, ALU.max, 256, ["MASK", "LE"], ["G"])
+            if ON_S["LV"]:
+                act(T.LV[:], T.TT[:, :, 0:32], 256, ["TT"], ["LV"], func=ACT.Relu, scale=-1.0, bias=1.0)
+                group(T.pK[:, 0:256], [(I["N21"], T.LV[:], 256)], False, ["N21", "LV"], ["pKa"], "pK")
+                scan(T.G[:, 1:257], T.MG[:], T.pK[:, 0:256], 127.0, ALU.min, ALU.max, 256, ["MG", "pKa"], ["G"], "pK")
+            else:
+                tt(T.LE[:], T.TT[:, :, 0:32], T.pK[:, 0:256], ALU.min, 256, ["TT", "pKa"], ["LE"], "pK")
+                scan(T.G[:, 1:257], T.MG[:], T.LE[:], 127.0, ALU.min, ALU.max, 256, ["MG", "LE"], ["G"])
             ts(T.GI[:], T.G[:, 32:257:32], 8.0, None, ALU.mult, None, 8, ["G"], ["GI"])
             ts(T.NB[:], T.GI[:], 0x3F8, None, ALU.bitwise_and, None, 8, ["GI"], ["NB"])
             ts(T.NA[:], T.GI[:], 20, None, ALU.arith_shift_right, None, 8, ["GI"], ["NA"])
-            tt(T.NM[:], T.NA[:], T.NB[:], ALU.add, 16, ["NA", "NB"], ["NM"])
-            tt(T.NX[:], T.NM[:].indirect(T.LU[:, 48:57]), T.MK[:], ALU.mult, 288, ["NM", "LU", "MK"], ["NX"])
-            mm([(T.pS[:, 0, 0:8], T.NX[:, 16:144], T.BLK[:], True, True), (T.pS[:, 0, 8:16], T.NX[:, 0:128], T.BLK[:], True, True)],
-               512, ["NX", "BLK"], ["pSa"], "pS")
+            tt(T.NM[:, 0:8], T.NA[:], T.NB[:], ALU.add, 16, ["NA", "NB"], ["NM"])
+            act(T.NX[:], T.NM[:].indirect(T.LU[:, 24:29]), 0, ["NM", "NMz", "LU1"], ["NX"], gat=80)
+            mm([(T.pS[:, 0, 0:16], T.ZH[:, 112 - 16 * ((b + 1) % 8):240 - 16 * ((b + 1) % 8)], T.NX[:, 8 * b:8 * b + 16], b == 0, b == 7)
+                for b in range(8)], 512, ["NX", "ZH"], ["pSa"], "pS")
             cp(T.NU[:, 16 * v:16 * v + 16], T.pS[:, 0, 0:16], 16, ["pSa"], [("NU", v)], "pS")
-            send(T.NU[:, 16 * v + 8:16 * v + 16], T.RN[:, 8 * v:8 * v + 8], 2048, [("NU", v)], [("RN", v)], "rn%d" % v)
+            send(T.NU[:, 16 * v:16 * v + 8], T.RN[:, 8 * v:8 * v + 8], 2048, [("NU", v)], [("RN", v)], "rn%d" % v)
             kind[0] = (v, "list")
-            tt(T.DF[:], T.G[:, 1:257], T.G[:, 0:256], ALU.subtract, 512, ["G", "G0"], ["DF"])
-            ts(T.LOW[:, :, 1:32], T.DF[:, :, 1:32], 255, None, ALU.bitwise_and, None, 248, ["DF"], ["LOW"])
-            ts(T.INV[:], T.LOW[:], 0.0, 2.0 ** -5, ALU.is_equal, ALU.mult, 256, ["LOW", "LOW0"], ["INV"])
-            tt(T.pV[:, 0:256], T.LOW[:], T.pT[:, 8:16, :], ALU.min, 256, ["LOW", "LOW0", "SC"], ["pVa"], ["pV", "pT"])
-            act(T.EE[:], T.INV[:], 256, ["INV"], ["EE"], scale=32.0 * TOP)
-            scan(T.CI[:], T.MASKB[:], T.INV[:], 0.0, ALU.mult, ALU.add, 128, ["MASKB", "INV"], ["CI"])
+            if DF_SCAN:
+                scan(T.DF[:], T.G[:, 1:257], T.G[:, 0:256], 0.0, ALU.max, ALU.subtract, 256, ["G", "G0"], ["DF"])
+            else:
+                tt(T.DF[:], T.G[:, 1:257], T.G[:, 0:256], ALU.subtract, 512, ["G", "G0"], ["DF"])
+            ts(T.LOW[:], T.DF[:], 255, None, ALU.bitwise_and, None, 256, ["DF"], ["LOW"])
+            if ON_S["INV"]:
+                act(T.INV[:], T.LOW[:], 256, ["LOW"], ["INV"], func=ACT.Relu, scale=-2.0 ** -5, bias=2.0 ** -5)
+            else:
+                ts(T.INV[:], T.LOW[:], 0.0, 2.0 ** -5, ALU.is_equal, ALU.mult, 256, ["LOW"], ["INV"])
+            tt(T.pV[:, 0:256], T.LOW[:], T.pV[:, 256:512], ALU.min, 256, ["LOW", "SC"], ["pVa"], "pV")
+            scan(T.CI[:], T.MASKB[:], T.INV[:], 1.0, ALU.min, ALU.add, 128, ["MASKB", "INV"], ["CI"])
             tt(T.YY[:], T.pV[:, 0:256], T.CI[:], ALU.subtract, 256, ["pVa", "CI"], ["YY"], "pV")
-            tt(T.XP[:], T.EE[:], T.pK[:, 0:8, :], ALU.max, 256, ["EE", "pKa"], ["XP"], "pK")
             R = T.pS[:, 8:16, :]
-            group(R, [(I["IC"], T.C1024[:], 256)], True, ["IC", "C1024"], ["pSb"], "pS", False)
-            group(R, [(I["I28"], T.YY[:], 256)], False, ["I28", "YY"], ["pSb"], "pS", False)
-            for k, (c1, c0, ident) in enumerate(((-64.0, 769.0, "I3"), (-16.0, 384.75, "I3"), (-4.0, 192.4375, "I3"), (-4.0, 384.9375, "I1"))):
+            group(R, [(I["IC"], T.C1024[:], 256), (I["I26"], T.INV[:], 256)], True, ["IC", "C1024", "I26", "INV"], ["pSb"], "pS", False)
+            group(R, [(I["I29"], T.YY[:], 256)], False, ["I29", "YY"], ["pSb"], "pS", False)
+            for k, (c1, c0, ident) in enumerate(((-64.0, 769.0, "I6"), (-16.0, 384.75, "I6"), (-4.0, 192.4375, "I6"), (-4.0, 416.9375, "IQ"))):
                 f = T.FL[:, 256 * k:256 * k + 256]
                 if FLOOR_V[k]:
                     ts(f, T.YY[:], c1, c0, ALU.mult, ALU.add, 128, ["YY"], [("FL", k)])
                 else:
                     act(f, T.YY[:], 256, ["YY"], [("FL", k)], scale=c1, bias=c0)
-                group(R, [(I[ident], f, 256)] + [(I["NI8"], T.C1024[:], 256)] * (k == 3), False, [ident, ("FL", k), "NI8"], ["pSb"], "pS", k == 3)
-            tt(T.pT[:, 0:8, 0:16], T.XP[:, :, 0:32:2], T.pS[:, 8:16, 0:32:2], ALU.add, 128, ["XP", "pSb"], EVK[0], ["pS", "pT"])
-            tt(T.M0[:, :, 0:16], T.XP[:, :, 1:32:2], T.pS[:, 8:16, 1:32:2], ALU.add, 128, ["XP", "pSb"], ODK[0], "pS")
+                group(R, [(I[ident], f, 256)] + [(I["IS"], T.CZ[:], 256), (I["N12"], T.INV[:], 256)] * (k == 3), False,
+                      [ident, ("FL", k), "IS", "CZ", "N12", "INV"], ["pSb"], "pS", k == 3)
+            tt(T.pS[:, 0:8, 0:16], T.G[:, 1:257:2], T.pS[:, 8:16, 0:32:2], ALU.add, 128, ["G", "pSb"], EVK[0], "pS")
+            tt(T.M0[:, :, 0:16], T.G[:, 2:257:2], T.pS[:, 8:16, 1:32:2], ALU.add, 128, ["G", "pSb"], ODK[0], "pS")
             for k in range(4):
                 a, b, d = k % 2, 16 * (k % 2), 16 - 16 * (k % 2)
                 for par in range(2):
                     for x, o in enumerate((ALU.min, ALU.max)):
-                        dst = T.M0[:, :, d + 8 * x:d + 8 * x + 8] if par else T.pT[:, 0:8, d + 8 * x:d + 8 * x + 8]
-                        tt(dst, T.M0[:, :, b + par:b + 16:2], T.pT[:, 0:8, b + par:b + 16:2], o, 64, EVK[a] + ODK[a],
-                           (ODK if par else EVK)[1 - a][2 * x:2 * x + 2], "pT")
-            tt(T.OUT[:, v], T.M0[:, :, 0:16], T.pT[:, 0:8, 0:16], ALU.min, 128, EVK[0] + ODK[0], [("OUT", v)], "pT")
-            send(T.OUT[:, v], T.RL[:, v], 65536, [("OUT", v)], [("RL", v)], "rl%d" % v)
-            act(T.PG2[:], T.PF[:].indirect(T.NU[:, 16 * v:16 * v + 8]), 0, PFK + [("NU", v)], ["PG2"], scale=2.0 ** -20, gat=128)
-            act(T.Y2[:], T.G[:, 0:257].indirect(T.LU[:, 64:72]), 0, ["G", "G0", "LU"], ["Y2"], scale=2.0 ** -20, gat=128)
+                        dst = T.M0[:, :, d + 8 * x:d + 8 * x + 8] if par else T.pS[:, 0:8, d + 8 * x:d + 8 * x + 8]
+                        tt(dst, T.M0[:, :, b + par:b + 16:2], T.pS[:, 0:8, b + par:b + 16:2], o, 64, EVK[a] + ODK[a],
+                           (ODK if par else EVK)[1 - a][2 * x:2 * x + 2], "pS")
+            tt(T.OUT[:, v], T.M0[:, :, 0:16], T.pS[:, 0:8, 0:16], ALU.min, 128, EVK[0] + ODK[0], [("OUT", v)], "pS")
+            if not SENDER:
+                send(T.OUT[:, v], T.RL[:, v], 65536, [("OUT", v)], [("RL", v)], "rl%d" % v)
+            act(T.PG2[:], T.PF[:].indirect(T.NU[:, 16 * v + 8:16 * v + 16]), 0, PFK + [("NU", v)], ["PG2"], scale=2.0 ** -20, gat=128)
+            act(T.Y2[:], T.G[:, 0:257].indirect(T.LU[:, 40:48]), 0, ["G", "G0", "LU"], ["Y2"], scale=2.0 ** -20, gat=128)
             group(T.pI[:, 0:4, :], [(T.Y2[:], T.NIF[:], 512), (T.IDF[:], T.PG2[:], 512)], True, ["PG2", "Y2", "IDF", "NIF"], [("pI", 0)], "pI")
             act(T.U2[:], T.pI[:, 0:4, :], 128, [("pI", 0)], ["U2"], "pI", func=ACT.Sign, scale=-1.0)
-            act(T.UJ[:], T.CI[:].indirect(T.LU[:, 40:48]), 0, ["CI", "LU"], ["UJ"], func=ACT.Relu, scale=32.0, bias=-16.0, gat=128)
+            act(T.UJ[:], T.CI[:].indirect(T.LU[:, 32:40]), 0, ["CI", "LU"], ["UJ"], func=ACT.Relu, scale=32.0, bias=-16.0, gat=128)
             ta, tk = T.pI[:, 8:16, 0:16], [("pI", 2), ("pI", 3)]
-            for out in (T.pI[:, 8:16, 16:32], ta):
+            for out in (T.pI[:, 8:16, 16:32],):
                 group(out, [(I["I1"], T.JC[:], 128), (I["NI1"], T.UJ[:], 128), (T.U2[:], T.BDG[:], 128), (T.U2[:], I["I23"], 128)], True,
                       ["I1", "NI1", "JC", "UJ", "U2", "BDG", "I23"], tk, "pI", out is not ta)
-            act(T.WN[:], T.pI[:, 8:16, 16:32], 128, tk, ["WN"], "pI", func=ACT.Sign, scale=2.0 ** -20, bias=-7.5)
-            tt(T.T0[:], T.PG2[:], T.U2[:], ALU.max, 256, ["PG2", "U2"], ["T0"])
-            group(ta, [(I["IW"], T.WN[:], 128), (I["I64"], T.WN[:], 128), (T.U2[:], I["N128"], 128), (I["NI8"], T.C1024[:, 0:128], 128),
-                       (T.T0[:], T.I20[:], 512)], False, ["IW", "I64", "WN", "U2", "N128", "NI8", "C1024", "T0", "I20"], tk, "pI")
-            act(T.TO[:, v], ta, 128, tk, [("TO", v)], "pI")
-            send(T.TO[:, v], T.RT[:, v], 65536, [("TO", v)], [("RT", v)], "rt%d" % v)
+            act(T.WN[:], T.pI[:, 8:16, 16:32], 128, tk, ["WN"], "pI", func=ACT.Sign, scale=2.0 ** -20, bias=0.5)
+            if ON_S["T0"]:
+                group(T.pI[:, 4:8, :], [(T.IDF[:], T.PG2[:], 512), (I["IB"], T.U2[:], 128)], True, ["PG2", "U2", "IDF", "IB"], [("pI", 1)], "pI")
+                act(T.T0[:], T.pI[:, 4:8, :], 128, [("pI", 1)], ["T0"], "pI", func=ACT.Relu, scale=-1.0)
+            else:
+                tt(T.T0[:], T.PG2[:], T.U2[:], ALU.max, 256, ["PG2", "U2"], ["T0"])
+            for out, stop in ((ta, False),):
+                group(out, [(I["I1"], T.JC[:], 128), (I["NI1"], T.UJ[:], 128), (T.U2[:], T.BDG[:], 128), (T.U2[:], I["I23"], 128)], True,
+                      ["I1", "NI1", "JC", "UJ", "U2", "BDG", "I23"], tk, "pI", stop)
+            group(ta, [(I["IC"], T.WN[:], 128), (T.U2[:], I["N128"], 128), (I["IS"], T.C1024[:, 0:128], 128),
+                       (T.T0[:], T.I20[:], 512)], False, ["IC", "WN", "U2", "N128", "IS", "C1024", "T0", "I20"], tk, "pI")
+            if SENDER:
+                act(T.Q0[:, :, 0:8], T.pI[:, 8:16, 0:8], 64, tk, ["Q0a", "Q0b"], "pI")
+                stage(T.Q1, "Q1", T.Q0[:, :, 0:8], T.pI[:, 8:16, 8:16], 64, ["Q0a", "Q0b"] + tk, "pI")
+                for dst, dk, src, sk in ((T.Q0, "Q0", T.Q1, "Q1"), (T.Q1, "Q1", T.Q0, "Q0")):
+                    stage(dst, dk, src[:, :, 0:8], src[:, :, 8:16], 128, [sk + "a", sk + "b"])
+                for x, o in enumerate((ALU.min, ALU.max)):
+                    tt(T.pI[:, 8:16, 16 + x:32:2], T.Q1[:, :, 0:8], T.Q1[:, :, 8:16], o, 128, ["Q1a", "Q1b"], [("pIs", x)], "pI")
+                tt(T.pV[:, 0:128], T.TCB[:], T.pI[:, 8:16, 16:32], ALU.add, 128, [("pIs", 0), ("pIs", 1), "TCB"], ["pVa"], ["pV", "pI"])
+                tt(T.TO[:, v], T.OUT[:, v], T.pV[:, 0:128], ALU.max, 128, [("OUT", v), "pVa"], [("TO", v)], "pV")
+                send(T.TO[:, v], T.RL[:, v], 65536, [("TO", v)], [("RL", v)], "rl%d" % v)
+            else:
+                act(T.TO[:, v], ta, 128, tk, [("TO", v)], "pI")
+                send(T.TO[:, v], T.RT[:, v], 65536, [("TO", v)], [("RT", v)], "rt%d" % v)
         kind[0] = (v, "co")
         for x, (dst, key) in enumerate(((CA, "CA"), (CB, "CB"))):
             for c4, n in runs(0, 4, COW[v]):
                 for h in range(2):
                     o = 256 * x + 128 * h + 32 * c4
-                    act(dst[:, 1024 * c4 + h:1024 * (c4 + n):2], T.CO[:].indirect(IDX[:, o:o + 32 * n]), 0,
+                    (cp if (x, c4, h) in COV[v] else act)(
+                        dst[:, 1024 * c4 + h:1024 * (c4 + n):2], T.CO[:].indirect(IDX[:, o:o + 32 * n]), 0,
                         ["CO", "COz", ("IDX", e, x)], [(key, e, 2 * cc + h) for cc in range(c4, c4 + n)], gat=512 * n)
-        for hh in range(2 * CADD[v]):
+        for hh in range(CADD[v]):
             c = slice(2048 * hh, 2048 * hh + 2048)
             dma("G", g, CB[:, c], CA[:, c], 1048576, [("CA", e, cc) for cc in range(4 * hh, 4 * hh + 4)],
                 [("CB", e, cc) for cc in range(4 * hh, 4 * hh + 4)], "cadd%d" % (2 * v + hh), accum_op=ALU.add, max_dma_last_dim=4096)
-        cols = (("CA", CA), ("CB", CB))[CADD[v]:]
         kind[0] = (v, "a")
         ABH = [("ABh", e, c) for c in range(8)]
+        yo = slice(128 * v, 128 * v + 128)
+        apart = APART[v]
         for jp in range(8):
-            bk = "pF%d" % (jp % 2)
-            h, its = jp % 2, []
-            for k in range(4):
-                j = 4 * k + jp // 2
-                its.append((T[bk][:, k:512:4], T.SEL[:, 128 * j:128 * j + 128], T.HI[:, 128 * h:128 * h + 128], True, False))
-                its.append((T[bk][:, k:512:4], T.SEL[:, 128 * j:128 * j + 128], T.LO[:, 128 * h:128 * h + 128], False, True))
-            mm(its, 1024, ["SEL", "HI", "LO"], [bk], bk)
-            tt(AB[:, jp:4096:8], SB[:, jp // 2:2048:4, h], T[bk][:], ALU.mult, 512, SBK + [bk], [("AB", e, jp)], bk)
+            bk = "pF%d" % ((16 * v + jp) % 3)
+            hf, jq, h = jp // 4, jp % 4, jp % 2
+            its = []
+            for k in range(8):
+                j, c = divmod(4 * k + jq, 3)
+                its.append((T[bk][:, k:512:8], T.SEL[0:96, 128 * j:128 * j + 128], T.XL[0:96, 128 * c + 64 * hf:128 * c + 64 * hf + 64], True, True))
+            mm(its, 512, [("SEL", u) for u in range(3)] + ["XL"], [bk], bk)
+            lo = 2048 * hf
+            tt(AB[:, lo + jq:lo + 2048:4], SB[:, lo // 2 + jq // 2:lo // 2 + 1024:2, h], T[bk][:], ALU.mult, 512,
+               [("SB", e, 4 * h + 2 * hf + u) for u in range(2)] + [bk], [("AB", e, jp)], bk)
+            if apart[hf]:
+                ss = [s for s in range(jq, 32, 4) if s]
+                tb = ("pK", "pV")[hf] if last else "pY"
+                to = T[tb][:, 0:64] if last else T.pY[:, 64 * hf:64 * hf + 64]
+                for u in range(0, len(ss), 4):
+                    mm([(to, T.IDF[:], AB[:, lo + s:lo + 2048:32], s == 4, s == 31) for s in ss[u:u + 4]], 256 * len(ss[u:u + 4]),
+                       [("AB", e, jp), "IDF"], [("tau", hf)], tb)
+                if jq == 3:
+                    act(T.YT[:, 128 * v + 64 * hf:128 * v + 64 * hf + 64], to, 64, [("tau", hf)], [("YT", v, hf)], tb, scale=-8.0)
         ABK = [("AB", e, j) for j in range(8)]
+        free = [("YT", v - 1, 0), ("YT", v - 1, 1), ("YC", v - 1)]
         kind[0] = (v, "one")
-        ns = ONE_S[v]
-        for c, n in runs(0, ns, ONEW[v]):
-            act(AB[:, 512 * c:512 * (c + n)], AB[:, 512 * c:512 * (c + n)], 512 * n, ABK, ABH[c:c + n], bias=1.0)
-        for c, n in runs(ns, 8, 4):
-            dma("G", g, AB[:, 512 * c:512 * (c + n)], T.ONES[:, 0:512 * n], n * 2 * 262144, ABK + ["ONES"], ABH[c:c + n],
-                "one%d" % (2 * v + c // 4), accum_op=ALU.add, max_dma_last_dim=4096)
+        for hf in range(2):
+            ns = 4 * hf + (ONE_S[v] + hf) // 2
+            rk = ABK[4 * hf:4 * hf + 4]
+            for c, n in runs(4 * hf, ns, ONEW[v]) if ONE_SPLIT[v] else runs(min(4 * hf, ONE_S[v]), min(4 * hf + 4, ONE_S[v]), ONEW[v]):
+                c0 = slice(512 * c, 512 * (c + n))
+                act((T.AC if apart[hf] else AB)[:, c0], AB[:, c0], 512 * n, rk, ABH[c:c + n] + [("AC", u) for u in range(c, c + n)] * apart[hf], bias=1.0)
+            for c, n in runs(ns, 4 * hf + 4, 4) if ONE_SPLIT[v] else runs(max(4 * hf, ONE_S[v]), max(4 * hf + 4, ONE_S[v]), 4):
+                dma("G", g, AB[:, 512 * c:512 * (c + n)], T.ONES[:, 0:512 * n], n * 2 * 262144, rk + ["ONES"], ABH[c:c + n],
+                    "one%d" % (2 * v + hf), accum_op=ALU.add, max_dma_last_dim=4096)
         for c in range(8):
             kind[0] = (v, c)
-            bk = "pF%d" % (c % 2)
+            bk = "pF%d" % ((16 * v + 8 + c) % 3)
             lo = 512 * c
+            cols = (("CA", CA), ("CB", CB))[c // 4 < CADD[v]:]
             its = ([(T[bk][:], I["NIH"], buf[:, lo:lo + 512]) for key, buf in cols]
                    + [(T[bk][:, 0:511], I["IH"], buf[:, lo + 1:lo + 512]) for key, buf in cols])
             mm([it + (k == 0, k == len(its) - 1) for k, it in enumerate(its)], 512 * len(its),
                [(key, e, c // 2 * 2 + h) for key, buf in cols for h in range(2)] + ["IH", "NIH"], [bk], bk)
             back = slice(lo + 511, lo - 1 if lo else None, -1)
-            ok = ABK + [ABH[c]]
-            scan(T.WO[:, back], T[bk][:, ::-1], AB[:, back], 0.0, ALU.add, ALU.mult, 512, ok + [bk], [("WO", c)], bk)
-            if not YT_PE[v]:
-                scan(WT[:, lo:lo + 512], T.MASK[:], AB[:, lo:lo + 512], 0.0, ALU.mult, ALU.add, 512,
-                     ok + ["MASK", ("YT", v - 1), ("YC", v - 1)], [("WT", c)])
+            ok = ABK[c // 4 * 4:c // 4 * 4 + 4] + [ABH[c]]
+            scan(T.WO[:, back], T[bk][:, ::-1], (T.AC if apart[c // 4] else AB)[:, back], 0.0, ALU.add, ALU.mult, 512,
+                 ok + [bk] + [("AC", c)] * apart[c // 4], [("WO", c)], bk)
+            if last and not apart[c // 4]:
+                scan(WT[:, lo:lo + 512], T.MASK[:], AB[:, lo:lo + 512], 0.0, ALU.mult, ALU.add, 512, ok + ["MASK"] + free, [("WT", c)])
         kind[0] = (v, "tau")
-        yo = slice(128 * v, 128 * v + 128)
-        if YT_PE[v]:
-            for j in range(16):
-                ss = [s for s in (2 * j, 2 * j + 1) if s]
-                mm([(T.pY[:, 0:128], T.IDF[:], AB[:, s:4096:32], s == 1, s == 31) for s in ss], 512 * len(ss), ABK + ABH + ["IDF"], ["pY"], "pY")
-            act(T.YT[:, yo], T.pY[:, 0:128], 128, ["pY"], [("YT", v)], "pY", scale=-8.0, bias=248.0)
+        if not last and sum(apart) < 2:
+            a0, w = 64 * apart[0], 4 if apart[0] else 2
+            for j in range(0, 32, w):
+                ss = [s for s in range(j, j + w) if s]
+                mm([(T.pY[:, a0:128], T.IDF[:], AB[:, 32 * a0 + s:4096:32], s == 1, s == 31) for s in ss], 1024 // w * len(ss),
+                   ABK[a0 // 16:] + ABH[a0 // 16:] + ["IDF"], [("tau", 0), ("tau", 1)], "pY")
+            act(T.YT[:, 128 * v + a0:128 * v + 128], T.pY[:, a0:128], 128 - a0, [("tau", 0), ("tau", 1)], [("YT", v, u) for u in range(apart[0], 2)], "pY",
+                scale=-8.0, bias=248.0)
+        for hf in range(2):
+            if last and not apart[hf]:
+                act(T.YT[:, 128 * v + 64 * hf:128 * v + 64 * hf + 64], WT[:, 2048 * hf + 31:2048 * hf + 2048:32], 64,
+                    [("WT", c) for c in range(4 * hf, 4 * hf + 4)], [("YT", v, hf)], scale=-8.0, bias=248.0)
+        WOK = [("WO", c) for c in range(8)]
+        onp = ON_P["YC"] and not last
+        na = 64 * CADD[v]
+        group(T.pY[:, 128:256], [(I["IH"], CB[:, 1:4096:32], 128)], True, [("CB", e, cc) for cc in range(8)] + ["IH"], ["pYc"], "pY",
+              na == 128 and not onp)
+        if na < 128:
+            group(T.pY[:, 128 + na:256], [(I["IH"], CA[:, 32 * na + 1:4096:32], 128)], False, [("CA", e, cc) for cc in range(8)] + ["IH"], ["pYc"], "pY", not onp)
+        if onp:
+            group(T.pY[:, 128:256], [(T.IDF[:], T.WO[:, 1:4096:32], 512)], False, WOK + ["IDF"], ["pYc"], "pY")
+            act(T.YC[:, yo], T.pY[:, 128:256], 128, ["pYc"], [("YC", v)], "pY")
         else:
-            act(T.YT[:, yo], WT[:, 31:4096:32], 128, [("WT", c) for c in range(8)], [("YT", v)], scale=-8.0, bias=248.0)
-        group(T.pY[:, 128:256], [(I["IH"], buf[:, 1:4096:32], 128) for key, buf in cols], True,
-              [(key, e, cc) for key, buf in cols for cc in range(8)] + ["IH"], ["pYc"], "pY")
-        tt(T.YC[:, yo], T.WO[:, 1:4096:32], T.pY[:, 128:256], ALU.add, 128, [("WO", c) for c in range(8)] + ["pYc"], [("YC", v)], "pY")
+            tt(T.YC[:, yo], T.WO[:, 1:4096:32], T.pY[:, 128:256], ALU.add, 128, WOK + ["pYc"], [("YC", v)], "pY")
         dma("Y", Y, T.yc[:, yo], T.YC[:, yo], 65536, [("YC", v)], [], "dst")
-        dma("Y", Y, T.yt[:, yo], T.YT[:, yo], 65536, [("YT", v)], [], "dst")
+        dma("Y", Y, T.yt[:, yo], T.YT[:, yo], 65536, [("YT", v, 0), ("YT", v, 1)], [], "dst")
     return ops, n_out
 
 

from concourse.bass import DstId, RemoteDMATransfer
from concourse.mybir import dt, AluOpType, AxisListType, ActivationFunctionType

ALU = AluOpType
ACT = ActivationFunctionType
NV = 5
M256 = 1.5 * 2.0 ** 31
M4096 = 2.0 ** 35 + 8192
VADD = (0, 0, 0, 0, 0)
VSHARE = (8, 8, 8, 8, 8)
COV = ((), (), (), (), ((1, 0, 0), (1, 0, 1)))
APART = ((0, 0), (0, 0), (0, 0), (1, 0), (1, 0))
ONE_S = (2, 2, 2, 4, 8)
SGW, COW, ONEW = (4, 4, 4, 4, 4), (1, 1, 1, 1, 1), (2, 2, 2, 2, 2)
CADD = (2, 2, 2, 2, 1)
ADDW = (2, 2, 2, 2, 1)
ON_P = {"TC": 0, "YC": 0}
FLOOR_V = (1, 1, 1, 1)
ON_S = {"SN": 1, "INV": 1, "YF": 1, "IDX": 0, "T0": 0, "LV": 1}
DF_SCAN = 1
SENDER = 1
ONE_SPLIT = (0, 0, 0, 0, 0)

F32, BF, I32, U16, F16 = "float32", "bfloat16", "int32", "uint16", "float16"
SCRATCH = {}


def _sb(name, shape, d):
    SCRATCH[name] = ("sbuf", [128] + list(shape), d)


IDS = {"IB": 1.0, "I6": 6 * 2.0 ** 20, "I1": 2.0 ** 20, "NI1": -2.0 ** 20, "I29": 2.0 ** 29, "I26": 2.0 ** 26,
       "IQ": 1.5 * 2.0 ** 20, "IC": -8.5 * 2.0 ** 20, "N12": -4096.0, "I2": 2.0, "IS": 0.0625,
       "N21": -2.0 ** 21, "HALF": 0.5, "I23": 2.0 ** 23, "N128": -128.0, "N5": -0.3125}
EARLY_IDS = ("IB", "I2", "N21", "N5")
IDH = {"IH32": 32.0, "IH": 1.0, "NIH": -1.0, "IHH": 0.5}

for _n, _s, _d in [
    ("SG", [4112], BF), ("CO", [4112], BF), ("PXI", [1024], I32), ("PF", [1024], F32), ("PK", [1024], F32),
    ("LSI", [128], I32), ("RAWF", [256], F32), ("AQ", [256], F32),
    ("FPI", [8], I32), ("FPU", [8], U16), ("OMI", [48], I32), ("OMG", [384], F32), ("BND", [40], F32), ("BD", [256], F32),
    ("ONE", [128], F32), ("IDF", [128], F32), ("NIF", [128], F32), ("I15", [128], F32), ("PERM", [128], F32), ("PERM15", [128], F32),
    ("IDS", [128 * len(IDS)], BF), ("IDH", [128 * len(IDH)], F16), ("ZB", [128], BF), ("SEL", [1408], BF), ("ONES", [2048], BF),
    ("CS", [512], BF), ("ZW", [240], F32), ("ZH", [240], F16),
    ("PI", [8], I32), ("PJ", [8], I32), ("PCOL", [8], F32), ("IO8", [8], F32), ("IO128", [128], F32),
    ("BLK", [8], F32), ("RMA", [16], BF), ("RMB", [16], BF),
    ("C1024", [256], BF), ("CZ", [256], BF), ("MI", [512], F32), ("MASK", [512], F32), ("MASKB", [256], BF),
    ("RV", [8, 4, 4], F32), ("RD", [128], F32), ("CP1", [128], BF), ("CP2", [128], BF), ("CP3", [128], BF), ("CP4", [128], BF),
    ("JC", [128], BF), ("GX", [128], F32), ("BDG", [128], BF), ("LI", [48], I32), ("LU", [48], U16),
    ("PG", [128], F32), ("PGS", [8, 16], F32), ("M0", [8, 32], F32), ("K", [8, 32], I32),
    ("ZF", [8, 33], F32), ("I16", [128], F32), ("I20", [128], F32), ("YI", [256], I32), ("YF", [256], F16), ("D0", [256], F16),
    ("A16", [256], F16), ("B16", [256], F16), ("SLAB", [8, 32], BF), ("IDX0", [512], U16), ("IDX1", [512], U16),
    ("LB", [8, 32], F32), ("W", [264], F32), ("TT", [8, 36], F32), ("SN", [256], BF), ("UU", [256], BF),
    ("LE", [256], F32), ("LV", [256], BF), ("G", [264], F32), ("MG", [256], F32),
    ("GI", [8], I32), ("NA", [8], I32), ("NB", [8], I32), ("NM", [16], F32), ("NX", [80], F16),
    ("DF", [256], I32), ("LOW", [256], I32), ("INV", [256], BF), ("CI", [256], BF), ("YY", [256], BF),
    ("FL", [1024], BF), ("UJ", [128], BF),
    ("PG2", [128], F32), ("Y2", [128], F32), ("U2", [128], BF), ("T0", [128], F32), ("WN", [128], BF),
    ("Q0", [8, 16], F32), ("Q1", [8, 16], F32), ("XL", [384], F16),
    ("SA0", [2048, 2], BF), ("SB0", [2048, 2], BF), ("SA1", [2048, 2], BF), ("SB1", [2048, 2], BF),
    ("CA0", [4096], F16), ("CB0", [4096], F16), ("CA1", [4096], F16), ("CB1", [4096], F16),
    ("AB0", [4096], F32), ("AB1", [4096], F32), ("WO", [4096], F32), ("AC", [4096], F32), ("TCB", [128], BF), ("YC", [640], F32), ("YT", [640], F32),
    ("RN", [32], U16), ("NU", [64], U16),
]:
    _sb(_n, _s, _d)
for _n in ("OUT", "RL", "TO", "RT"):
    _sb(_n, [NV - 1, 8, 16], F32)
for _n in ("pS", "pI"):
    SCRATCH[_n] = ("psum", [128, 16, 32], F32)
for _n in ("pK", "pV", "pF0", "pF1", "pF2", "pY"):
    SCRATCH[_n] = ("psum", [128, 512], F32)

SEMAPHORES = (["cV", "cS", "cP", "cG", "dls", "dfp", "dpx", "dom", "dsg", "dco", "dst", "sent"]
              + ["add%d" % v for v in range(NV + 1)] + ["one%d" % v for v in range(2 * NV)] + ["cadd%d" % v for v in range(2 * NV)]
              + ["rn%d" % v for v in range(NV - 1)] + ["rl%d" % v for v in range(NV - 1)] + ["rt%d" % v for v in range(NV - 1)])

CASES = ((1.1, 1.6, 90.0, 2400.0, 400.0), (1.15, 1.2, 70.0, 2600.0, 420.0), (1.05, 2.0, 80.0, 2500.0, 370.0),
         (1.1, 1.5, 80.0, 3200.0, 300.0))
EARLY = (2, 3, 4, 5, 6, 8)
ROUNDS = 60000
SIZES = (40, 70, 110, 160)
NOISES = (0, 100, 300, 800, 2000)
LEAN = 0.1
CLIMB = 140000
FRESH = 8
SEED = 82
NOISE = 1000.0
SLACK = 150.0
PLANS = {}


def costs(ops, case):
    f, ga, hop, way, rate = case
    busy, lat = [], []
    for o in ops:
        fix, n, gat, kind = o["cost"]
        if kind == "dma":
            b = fix * way / 2500.0 + n / rate
            l = b + 1000.0
        elif kind == "send":
            b = n / 40.0
            l = b + way - 1300.0
        elif kind == "pe":
            b = f * (fix + 0.42 * n)
            l = b + 70.0
        else:
            b = l = f * (fix + 0.83 * max(n + gat * ga, 32))
        busy.append(b)
        lat.append(l + hop)
    return busy, lat


def replay(qs, pred, order, busy, lat):
    free = [0.0] * 8
    start, done = [0.0] * len(qs), [0.0] * len(qs)
    for i in order:
        q = qs[i]
        t = free[q]
        for d in pred[i]:
            if done[d] > t:
                t = done[d]
        start[i] = t
        free[q] = t + busy[i]
        done[i] = t + lat[i]
    return max(done), start, done


def retime(qs, pred, order, busy, lat, first, reach, known, far, rest, most):
    free = [0.0] * 8
    start, done = list(known[0]), list(known[1])
    for i in order[max(first - 300, 0):first]:
        free[qs[i]] = start[i] + busy[i]
    k = first
    moved = reach
    for i in order[first:]:
        if k > reach:
            break
        q = qs[i]
        t = free[q]
        for d in pred[i]:
            if done[d] > t:
                t = done[d]
        if t != start[i]:
            if k > moved and t + rest[i] > most:
                return None
            start[i] = t
            done[i] = t + lat[i]
            if far[i] > reach:
                reach = far[i]
        free[q] = t + busy[i]
        k += 1
    return max(done), start, done


def sweep(qs, pred, succ, prio, busy, lat, back):
    n = len(qs)
    left = [len(p) for p in pred]
    ready = [lat[i] - busy[i] if back else 0.0 for i in range(n)]
    start = [0.0] * n
    slots = {}
    held = [False] * n
    for first in sorted(range(n), key=lambda i: -prio[i]):
        if left[first]:
            held[first] = True
            continue
        todo = [first]
        while todo:
            todo.sort(key=lambda i: prio[i])
            c = todo.pop()
            row = slots.setdefault(qs[c], [])
            t, b = ready[c], busy[c]
            lo, hi = 0, len(row)
            while lo < hi:
                m = (lo + hi) // 2
                if row[m][1] <= t:
                    lo = m + 1
                else:
                    hi = m
            while lo < len(row) and row[lo][0] < t + b:
                t = max(t, row[lo][1])
                lo += 1
            row.insert(lo, (t, t + b))
            start[c] = t
            for s in succ[c]:
                u = t + b if qs[s] == qs[c] == 2 else t + b + lat[s] - busy[s] if back else t + lat[c]
                if u > ready[s]:
                    ready[s] = u
                left[s] -= 1
                if left[s] == 0 and held[s]:
                    todo.append(s)
    return sorted(range(n), key=lambda i: (start[i], i)), start


def plan(ops):
    n = len(ops)
    key = tuple((o["q"], o["cost"], tuple(o["deps"])) for o in ops)
    if key not in PLANS:
        qs = ["VSPGYD".index(o["q"]) for o in ops]
        above = []
        pred = []
        succ = [[] for _ in range(n)]
        for i, o in enumerate(ops):
            seen, keep = 0, []
            for d in reversed(o["deps"]):
                if not seen >> d & 1:
                    keep.append(d)
                    succ[d].append(i)
                    seen |= above[d] | 1 << d
            above.append(seen)
            pred.append(keep)
        wait = [[d for d in p if ops[d]["q"] != "P" or o["q"] != "P"] for p, o in zip(pred, ops)]
        cs = [costs(ops, c) for c in CASES]
        busy, lat = cs[0]
        seed = [SEED]

        def rnd(m):
            seed[0] = (seed[0] * 1103515245 + 12345) % 2147483648
            return (seed[0] >> 8) % m

        def score(order):
            got = [replay(qs, wait, order, b, l) for b, l in cs]
            return sum(r[0] / c[0] for r, c in zip(got, CASES)) / len(cs), [r[1:] for r in got]

        best = None
        for early in EARLY:
            rank = {"setup": 0, (0, "pixel"): 1}
            for v in range(NV + 1):
                for k in ([(v, "merge"), (v, "sg"), (v, "keys")] + [(v - 1, c) for c in range(early)]
                          + [(v, "seen"), (v, "list"), (v + 1, "pixel")] + [(v - 1, c) for c in range(early, 8)]
                          + [(v, "co"), (v - 1, "tau"), (v, "a"), (v, "one")]):
                    rank[k] = len(rank)
            order, start = sweep(qs, pred, succ, [-n * rank[o["kind"]] - i for i, o in enumerate(ops)], busy, lat, False)
            end = score(order)[0]
            if best is None or end < best[0]:
                best = (end, order, start)
        prio = [-t for t in best[2]]
        for r in range(ROUNDS):
            order, start = sweep(qs, pred, succ, prio, busy, lat, False)
            end = score(order)[0]
            if best is None or end < best[0]:
                best = (end, order, start)
            if r % 4 == 3:
                start = best[2]
            amp = (0.0, NOISE, 0.0, 4.0 * NOISE)[r % 4]
            back = [start[i] + busy[i] + amp * rnd(1000) / 1000.0 for i in range(n)]
            _o, st = sweep(qs, succ, pred, back, busy, lat, True)
            prio = [st[i] + busy[i] for i in range(n)]
        order = best[1]
        end, starts = score(order)
        ends = [max(s[1]) for s in starts]
        best = (end, order, starts[0][0])
        taken = moved = 0
        pos = [0] * n
        before = [-1] * n
        for r in range(CLIMB):
            fresh = taken % FRESH == 0
            if fresh:
                taken += 1
                place = {i: k for k, i in enumerate(order)}
                order = sorted(order, key=lambda i: (starts[0][0][i], place[i]))
            if fresh or moved:
                moved = 0
                tail = [-1] * 8
                for k, i in enumerate(order):
                    pos[i] = k
                    before[i] = tail[qs[i]]
                    tail[qs[i]] = i
                far = [max([pos[s] for s in succ[i]] + [0]) for i in range(n)] if fresh else far
                for i in range(n) if fresh else order[first:last + 1]:
                    if not fresh and qs[i] == qs[a]:
                        far[i] = max(far[i], reach)
                    for d in pred[i] + [before[i]]:
                        if d >= 0 and far[d] < pos[i]:
                            far[d] = pos[i]
            if fresh:
                rests = []
                for b, l in cs:
                    rest = list(l)
                    for i in reversed(order):
                        for d in wait[i]:
                            if rest[d] < l[d] + rest[i]:
                                rest[d] = l[d] + rest[i]
                        d = before[i]
                        if d >= 0 and rest[d] < b[d] + rest[i]:
                            rest[d] = b[d] + rest[i]
                    rests.append(rest)
                links = []
                for case, ((st, done), (b, l)) in enumerate(zip(starts, cs)):
                    i = done.index(ends[case])
                    while i >= 0:
                        a = before[i]
                        if a >= 0 and st[a] + b[a] >= st[i] - 1e-6:
                            if a not in pred[i]:
                                links.append((i, case))
                            i = a
                        else:
                            i = max(wait[i], key=lambda d: done[d]) if wait[i] and st[i] > 0 else -1
            i, case = links[rnd(len(links))]
            a = before[i]
            if a < 0:
                continue
            if rnd(2):
                for _ in range((0, 0, 1, 2, 4, 8, 16, 32)[rnd(8)]):
                    if before[a] >= 0:
                        a = before[a]
                first = max([pos[a]] + [pos[d] + 1 for d in pred[i]])
                if first > pos[before[i]]:
                    continue
                last = pos[i]
                new = order[:first] + [i] + order[first:last] + order[last + 1:]
            else:
                to = min([pos[i] + (0, 0, 2, 5, 10, 20, 40, 80)[rnd(8)], n - 1] + [pos[s] - 1 for s in succ[a]])
                if to < pos[i]:
                    continue
                first, last = pos[a], to
                new = order[:first] + order[first + 1:to + 1] + [a] + order[to + 1:]
            room = len(cs) * SLACK * (1.0 - r / CLIMB) * rnd(1000) / 1000.0
            got = [None] * len(cs)
            reach = max([last] + [far[j] for j in order[first:last + 1] if qs[j] == qs[i]])
            for k in range(len(cs)):
                k = (k + case) % len(cs)
                got[k] = retime(qs, wait, new, cs[k][0], cs[k][1], first, reach, starts[k], far, rests[k], ends[k] + room * CASES[k][0])
                if got[k] is None:
                    break
                room -= (got[k][0] - ends[k]) / CASES[k][0]
                if room < 0.0:
                    break
            else:
                taken, moved = taken + 1, 1
                order, starts, ends = new, [x[1:] for x in got], [x[0] for x in got]
                end = sum(e / c[0] for e, c in zip(ends, CASES)) / len(cs)
                if end < best[0]:
                    best = (end, order, starts[0][0])
        PLANS[key] = best
    for i, o in enumerate(ops):
        o["t"] = PLANS[key][2][i]
    return PLANS[key][1]


def reorder(win, after, qs, pred, wait, succ, busy, lat, done, rest, free, rnd):
    inw = set(win)
    nx, seen = [0.0] * 8, 0
    for i in after:
        if not seen >> qs[i] & 1:
            seen |= 1 << qs[i]
            nx[qs[i]] = rest[i]
    amp, delta = NOISES[rnd(len(NOISES))], rnd(5) / 4.0
    tail, prio, left, ready, todo, new = {}, {}, {}, {}, [], []
    for i in reversed(win):
        t = max(lat[i], busy[i] + nx[qs[i]])
        for j in succ[i]:
            u = (busy[i] if qs[i] == qs[j] == 2 else lat[i]) + (tail[j] if j in inw else rest[j])
            if u > t:
                t = u
        tail[i] = t
    for i in win:
        prio[i] = tail[i] + amp * rnd(1000) / 1000.0
        left[i] = sum(d in inw for d in pred[i])
        ready[i] = max([done[d] for d in wait[i] if d not in inw] + [0.0])
        if not left[i]:
            todo.append(i)
    while todo:
        end, q = 1e18, 0
        for i in todo:
            t = max(ready[i], free[qs[i]]) + busy[i]
            if t < end:
                end, q = t, qs[i]
        lo = max(free[q], min(ready[i] for i in todo if qs[i] == q))
        cut = lo + delta * (end - lo) + 1e-6
        c = max((i for i in todo if qs[i] == q and ready[i] <= cut), key=prio.get)
        todo.remove(c)
        t = max(ready[c], free[q])
        free[q] = t + busy[c]
        new.append(c)
        for j in succ[c]:
            if j in inw:
                if t + lat[c] > ready[j] and not q == qs[j] == 2:
                    ready[j] = t + lat[c]
                left[j] -= 1
                if not left[j]:
                    todo.append(j)
    return new


def plan(ops):
    n = len(ops)
    key = tuple((o["q"], o["cost"], tuple(o["deps"])) for o in ops)
    if key not in PLANS:
        qs = ["VSPGYD".index(o["q"]) for o in ops]
        above, pred, succ = [], [], [[] for _ in range(n)]
        for i, o in enumerate(ops):
            seen, keep = 0, []
            for d in reversed(o["deps"]):
                if not seen >> d & 1:
                    keep.append(d)
                    succ[d].append(i)
                    seen |= above[d] | 1 << d
            above.append(seen)
            pred.append(keep)
        wait = [[d for d in p if qs[d] != 2 or q != 2] for p, q in zip(pred, qs)]
        cs = [costs(ops, c) for c in CASES]
        seed = [SEED]

        def rnd(m):
            seed[0] = (seed[0] * 1103515245 + 12345) % 2147483648
            return (seed[0] >> 8) % m

        def score(order):
            got = [replay(qs, wait, order, b, l) for b, l in cs]
            return sum((r[0] + LEAN * sum(r[1]) / n) / c[0] for r, c in zip(got, CASES)) / len(cs), got

        rank = {"setup": 0, (0, "pixel"): 1}
        for v in range(NV + 1):
            for k in ([(v, "merge"), (v, "sg"), (v, "keys")] + [(v - 1, c) for c in range(4)] + [(v, "seen"), (v, "list"), (v + 1, "pixel")]
                      + [(v - 1, c) for c in range(4, 8)] + [(v, "co"), (v - 1, "tau"), (v, "a"), (v, "one")]):
                rank[k] = len(rank)
        order = sweep(qs, pred, succ, [-n * rank[o["kind"]] - i for i, o in enumerate(ops)], cs[0][0], cs[0][1], False)[0]
        end, got = score(order)
        best, rests = (end, order, got[0][1]), {}
        for r in range(ROUNDS):
            case = rnd(len(cs))
            (busy, lat), (start, done) = cs[case], got[case][1:]
            if case not in rests:
                od, rest, nx = sorted(order, key=lambda i: start[i]), [0.0] * n, [0.0] * 8
                for i in reversed(od):
                    t = max(busy[i] + nx[qs[i]], lat[i])
                    for j in succ[i]:
                        if lat[i] + rest[j] > t and not qs[i] == qs[j] == 2:
                            t = lat[i] + rest[j]
                    rest[i] = nx[qs[i]] = t
                rests[case] = (od, rest)
            od, rest = rests[case]
            w = SIZES[rnd(len(SIZES))]
            k0 = rnd(n - 10 + w) - w
            k0, k1 = max(k0, 0), min(n, k0 + w)
            free = [0.0] * 8
            for i in od[max(k0 - 300, 0):k0]:
                free[qs[i]] = start[i] + busy[i]
            new = od[:k0] + reorder(od[k0:k1], od[k1:k1 + 300], qs, pred, wait, succ, busy, lat, done, rest, free, rnd) + od[k1:]
            room = SLACK * (1.0 - r / ROUNDS) * rnd(1000) / 1000.0
            if replay(qs, wait, new, busy, lat)[0] > got[case][0] + 4 * room * CASES[case][0] + 300.0:
                continue
            e2, g2 = score(new)
            if e2 <= end + room:
                end, got, order, rests = e2, g2, new, {}
                if end < best[0]:
                    best = (end, order, got[0][1])
        PLANS[key] = best
    for i, o in enumerate(ops):
        o["t"] = PLANS[key][2][i]
    return PLANS[key][1]


def runs(a, b, w):
    cuts = [a] + [c for c in range(a + 1, b) if c % w == 0] + [b]
    return [(c, d - c) for c, d in zip(cuts, cuts[1:]) if d > c]


def build(g, core, T, topo):
    rank = T.rank_of(core)
    nxt = T.cores[(rank + 1) % len(T.cores)]
    prv = T.cores[(rank - 1) % len(T.cores)]
    rid, pid, _ = topo.addr(nxt)
    omask, n_out, n_in = topo.mask(core, nxt), len(topo.engines(core, nxt)), len(topo.engines(prv, core))
    V, S, P, Y = g.vector, g.scalar, g.tensor, g.sync
    ops = []
    lastw, readers, bankers = {}, {}, {}
    kind = ["setup"]

    def op(q, fn, cost, r=(), w=(), bank=None, sem=None, inc=1):
        i = len(ops)
        deps = set()
        for k in r:
            if k in lastw:
                deps.add(lastw[k])
        for k in w:
            if k in lastw:
                deps.add(lastw[k])
            deps.update(readers.get(k, ()))
        for k in r:
            readers.setdefault(k, []).append(i)
        for k in w:
            lastw[k] = i
            readers[k] = []
        for bank1 in sorted(set([] if bank is None else bank if isinstance(bank, list) else [bank])):
            b = bankers.setdefault(bank1, [None, [], []])
            if b[0] != q:
                b[:] = [q, [], b[1]]
            deps.update(b[2])
            if q == "P":
                deps.update(b[1])
            b[1].append(i)
        deps.discard(i)
        ops.append({"q": q, "fn": fn, "cost": cost, "deps": sorted(deps), "sem": sem or "c" + q, "inc": inc, "name": str(w), "kind": kind[0]})
        return i

    def ts(out, in0, s1, s2, o0, o1, n, r, w, bank=None):
        if o1 is None:
            return op("V", lambda: V.tensor_scalar(out, in0, s1, None, o0), (50.0, n, 0, ""), r, w, bank)
        return op("V", lambda: V.tensor_scalar(out, in0, s1, s2, o0, o1), (50.0, n, 0, ""), r, w, bank)

    def tt(out, a, b, o, n, r, w, bank=None):
        return op("V", lambda: V.tensor_tensor(out, a, b, o), (50.0, n, 0, ""), r, w, bank)

    def cp(out, a, n, r, w, bank=None, gat=0):
        return op("V", lambda: V.tensor_copy(out, a), (50.0, n, gat, ""), r, w, bank)

    def ms(ap, c, n, w):
        return op("V", lambda: V.memset(ap, c), (50.0, n, 0, ""), (), w)

    def scan(out, d0, d1, init, o0, o1, n, r, w, bank=None):
        return op("V", lambda: V.tensor_tensor_scan(out, d0, d1, init, o0, o1), (50.0, n, 0, ""), r, w, bank)

    def act(out, a, n, r, w, bank=None, func=ACT.Identity, scale=1.0, bias=0.0, gat=0):
        return op("S", lambda: S.activation(out, a, func, bias=bias, scale=scale), (65.0, n, gat, ""), r, w, bank)

    def mm(items, cyc, r, w, bank):
        def fn():
            for it in items:
                ins = P.matmul(*it)
            return ins
        return op("P", fn, (30.0, cyc, 0, "pe"), r, w, bank)

    def group(out, terms, start, r, w, bank, stop=True):
        its = [(out, a, b, start and k == 0, stop and k == len(terms) - 1) for k, (a, b, c) in enumerate(terms)]
        return mm(its, sum(c for a, b, c in terms), r, w, bank)

    def dma(q, eng, out, a, nbytes, r, w, sem, **kw):
        key = ("dma", len(ops))
        op(q, lambda: eng.dma_start(out, a, **kw), (1000.0 if q == "G" else 60.0, 0, 0, "dma"), r, list(w) + [key], sem=sem, inc=16)
        op("D", None, (0.0, nbytes, 0, "dma"), list(r) + [key], w)

    def iota(out, pat, base, cm, n, w, small=True):
        if small:
            return op("G", lambda: g.iota(out, pat, base, cm, allow_small_or_imprecise_dtypes=True), (130.0, 2 * n, 0, ""), (), w)
        return op("G", lambda: g.iota(out, pat, base, cm), (130.0, 2 * n, 0, ""), (), w)

    def asel(out, a, pat, base, n, r, w, fill=0.0, cm=1, keep=ALU.is_equal):
        return op("G", lambda: g.affine_select(out, a, pat, keep, fill, base, cm), (170.0, 2 * n, 0, ""), r, w)

    def send(src, dst, nbytes, r, w, sem):
        op("G", lambda: g.remote_dma(dst, src, T.sem[sem], T.sem.sent, pid, rid, omask), (300.0, 0, 0, "dma"), r, [("sent", sem)], sem="*")
        op("D", None, (0.0, nbytes, 0, "send"), [("sent", sem)], w, sem=sem, inc=n_in)

    I = {}
    for names, buf in ((IDS, T.IDS), (IDH, T.IDH)):
        for k, name in enumerate(names):
            I[name] = buf[:, 128 * k:128 * k + 128]

    dma("Y", Y, T.LSI[:], T.ls[:], 65536, (), ["LSI"], "dls")
    dma("S", S, T.FPI[:], T.fp[:], 4096, (), ["FPI"], "dfp")
    dma("Y", Y, T.PXI[:], T.px[:], 524288, (), ["PXI"], "dpx")
    dma("S", S, T.OMI[:, 0:40], T.om[:], 20480, (), ["OMI"], "dom")
    dma("Y", Y, T.SG[:, 16:4112], T.sg[:], 1048576, (), ["SG"], "dsg")
    dma("Y", Y, T.CO[:, 16:4112], T.co[:], 1048576, (), ["CO"], "dco")

    ms(T.ONE[:], 1.0, 128, ["ONE"])
    iota(T.PI[:, 0:1], [[0, 1]], 0, 1, 1, ["PI"], False)
    asel(T.PERM[:], T.ONE[:], [[-16, 8], [1, 16]], -15, 128, ["ONE"], ["PERM"])
    asel(T.IDF[:], T.ONE[:], [[-1, 128]], 0, 128, ["ONE"], ["IDF"])
    iota(T.LI[:, 0:24], [[1, 8], [16, 3]], 0, 0, 24, ["LI0"], False)
    iota(T.LI[:, 24:32], [[0, 2], [2, 4]], 0, 0, 8, ["LI1"], False)
    iota(T.LI[:, 32:48], [[1, 2], [32, 8]], 31, 0, 16, ["LI2"], False)
    iota(T.IO8[:], [[1, 8]], 0, 0, 8, ["IO8"])
    iota(T.IO128[:], [[0, 8], [1, 16]], 0, 0, 128, ["IO128"])
    iota(T.CP2[:], [[0, 8], [128, 16]], -2048, 0, 128, ["CP2"])
    iota(T.CP3[:], [[0, 8], [-128, 16]], 1920, 0, 128, ["CP3"])
    iota(T.JC[:], [[0, 8], [1, 16]], 0, 0, 128, ["JC"])
    iota(T.GX[:], [[1, 8], [0, 16]], 0, 0, 128, ["GX"])
    for u in range(4):
        iota(T.RV[:, :, u, :], [[0, 8], [4, 2], [8, 2]], (0, 2, 1, 3)[u], 0, 32, [("RV", u)])
    RVK = [("RV", u) for u in range(4)]
    iota(T.ONES[:], [[0, 2048]], 1, 0, 2048, ["ONES"])
    iota(T.C1024[:], [[0, 256]], 1024, 0, 256, ["C1024"])
    iota(T.MI[:], [[0, 16], [1, 32]], 0, 0, 512, ["MI"])
    act(T.MASK[:], T.MI[:], 512, ["MI"], ["MASK"], func=ACT.Sign)
    asel(T.MASKB[:], T.ONES[:, 0:256], [[0, 8], [1, 32]], 0, 256, ["ONES"], ["MASKB"], 2.0 ** -5, 0, ALU.not_equal)
    asel(T.CZ[:], T.C1024[:], [[0, 8], [1, 32]], 0, 256, ["C1024"], ["CZ"], 2.0 ** 25, 0, ALU.not_equal)
    act(T.pV[:, 256:512], T.MI[:, 0:256], 256, ["MI"], ["SC"], "pV", scale=2.0 ** -5)
    act(T.BD[:], T.MI[:, 0:256], 256, ["MI"], ["BD"], scale=0.0)
    act(T.BD[:, 0:256:32], T.IO8[:], 8, ["IO8"], ["BD"], scale=0.0, bias=2.0 ** 40)
    ms(T.CS[:], -2.0 ** -13, 256, ["CS"])
    for u in range(3):
        n = (4, 4, 3)[u]
        c = slice(512 * u, 512 * u + 128 * n)
        asel(T.SEL[:, c], T.CS[:, 0:128 * n], [[-1, n], [-12, 8], [0, 16]], -4 * u, 128 * n, ["CS"], [("SEL", u)])
        asel(T.SEL[:, c], T.SEL[:, c], [[0, n], [-12, 8], [0, 16]], -11, 128 * n, [("SEL", u)], [("SEL", u)], -2.0 ** -13, 1, ALU.not_equal)
    for k, (c0, c1, o0, o1) in enumerate(((15, None, ALU.bitwise_and, None), (4, None, ALU.arith_shift_right, None),
                                          (7, None, ALU.bitwise_and, None), (3, 1, ALU.arith_shift_right, ALU.bitwise_and))):
        ts(T.PJ[:, k:k + 1], T.PI[:, 0:1], c0, c1, o0, o1, 1, ["PI"], ["PJ%d" % k])
    cp(T.PCOL[:, 0:2], T.PJ[:, 0:2], 2, ["PJ0", "PJ1"], ["PC0"])
    ts(T.PCOL[:, 3:4], T.PJ[:, 0:1], 128.0, None, ALU.mult, None, 1, ["PJ0"], ["PC3"])
    tt(T.PCOL[:, 4:5], T.PJ[:, 2:3], T.PJ[:, 1:2], ALU.is_equal, 2, ["PJ1", "PJ2"], ["PC4"])
    ts(T.PCOL[:, 5:6], T.PJ[:, 3:4], -5.0, T.PCOL[:, 4:5], ALU.add, ALU.mult, 1, ["PJ3", "PC4"], ["PC5"])
    ts(T.PCOL[:, 5:6], T.PCOL[:, 5:6], 8.0, 40.0, ALU.mult, ALU.add, 1, ["PC5"], ["PC5"])
    ts(T.PCOL[:, 6:7], T.PJ[:, 3:4], -8.0, T.PCOL[:, 4:5], ALU.add, ALU.mult, 1, ["PJ3", "PC4"], ["PC6"])
    ts(T.PCOL[:, 6:7], T.PCOL[:, 6:7], 8.0, None, ALU.add, None, 1, ["PC6"], ["PC6"])
    ts(T.LU[:, 0:24], T.LI[:, 0:24], T.PCOL[:, 4:5], T.PCOL[:, 5:6], ALU.mult, ALU.add, 24, ["LI0", "PC4", "PC5"], ["LU0"])
    ts(T.LU[:, 24:32], T.LI[:, 24:32], T.PCOL[:, 4:5], T.PCOL[:, 6:7], ALU.mult, ALU.add, 8, ["LI1", "PC4", "PC6"], ["LU1"])
    cp(T.LU[:, 32:48], T.LI[:, 32:48], 16, ["LI2"], ["LU"])
    cp(T.FPU[:], T.FPI[:], 8, ["FPI"], ["FPU"])
    ms(T.ZW[:], 0.0, 240, ["ZW"])
    ts(T.ZW[:, 112:128], T.IO128[:, 0:16], T.PCOL[:, 0:1], None, ALU.is_equal, None, 16, ["IO128", "PC0"], ["ZW"])
    act(T.ZH[:], T.ZW[:], 240, ["ZW"], ["ZH"])
    ts(T.BLK[:], T.IO8[:], T.PCOL[:, 1:2], None, ALU.is_equal, None, 8, ["IO8", "PC0"], ["BLK"])
    ts(T.BDG[:], T.GX[:], T.PCOL[:, 1:2], -2.0 ** 19, ALU.is_equal, ALU.mult, 128, ["GX", "PC0"], ["BDG"])
    for buf, key, c0, c1 in ((T.RMA, "RMA", -4096.0, -1.0), (T.RMB, "RMB", -4096.0, 1.0)):
        act(buf[:, 0:8], T.BLK[:], 8, ["BLK"], [key + "a"], scale=c0)
        act(buf[:, 8:16], T.BLK[:], 8, ["BLK"], [key + "b"], scale=c1)
    ms(T.ZB[:], 0.0, 64, ["ZB"])
    for name, c in IDS.items():
        if name in EARLY_IDS:
            act(I[name], T.IDF[:], 128, ["IDF"], [name], scale=c)
        else:
            asel(I[name], T.ZB[:], [[-1, 128]], 0, 128, ["ZB"], [name], c, 1, ALU.not_equal)
    for name, c in IDH.items():
        ts(I[name], T.IDF[:], c, None, ALU.mult, None, 128, ["IDF"], [name])
    act(T.NIF[:], T.IDF[:], 128, ["IDF"], ["NIF"], scale=-1.0)
    act(T.I15[:], T.IDF[:], 128, ["IDF"], ["I15"], scale=15.0)
    act(T.I16[:], T.IDF[:], 128, ["IDF"], ["I16"], scale=2.0 ** -4)
    act(T.I20[:], T.IDF[:], 128, ["IDF"], ["I20"], scale=-2.0 ** 20 if ON_S["T0"] else 2.0 ** 20)
    act(T.PERM15[:], T.PERM[:], 128, ["PERM"], ["PERM15"], scale=15.0)
    act(T.CP1[:], T.RV[:], 128, RVK, ["CP1"], scale=-2.0 ** 25, bias=2.0 ** 28)
    act(T.CP4[:], T.JC[:], 128, ["JC"], ["CP4"], scale=128.0, bias=-6080.0)
    act(T.MG[:], T.MASK[:, 0:256], 256, ["MASK"], ["MG"], scale=2.0 ** 22, bias=127.0)
    act(T.RD[:], T.RV[:], 128, RVK, ["RD"], scale=2.0 ** 21, bias=(ON_S["T0"] - 8.5) * 2.0 ** 20)
    group(T.pF2[:, 0:128], [(T.IDF[:], T.RD[:], 512), (I["NI1"], T.JC[:], 128)], True, ["IDF", "RD", "NI1", "JC"], ["pF2"], "pF2")
    act(T.TCB[:], T.pF2[:, 0:128], 128, ["pF2"], ["TCB"], "pF2")
    ms(T.SG[:, 0:16], 32.0, 16, ["SGz"])
    ms(T.CO[:, 0:16], 0.0, 16, ["COz"])
    ms(T.OMI[:, 40:48], 0, 8, ["OMz"])
    ms(T.NM[:, 8:16], 0.0, 8, ["NMz"])
    ms(T.W[:, 0:1], 0.0, 1, ["W0"])
    for buf, at, c, key in ((T.ZF, 32, M4096 + 2.0 ** 24, "ZFe"), (T.SLAB, 0, -8192.0, "SLAB0"), (T.LB, 0, 2.0 ** 35, "LB0")):
        act(buf[:, :, at], T.IO8[:], 8, ["IO8"], [key], scale=0.0, bias=c)
    ms(T.G[:, 0:1], 128.0, 1, ["G0"])
    ms(T.TT[:, :, 32:36], 2.0 ** 36, 32, ["TTe"])

    cp(T.RAWF[:, 0:128], T.LSI[:], 128, ["LSI"], ["RAW0"])
    cp(T.RAWF[:, 128:256], T.PXI[:].indirect(T.FPU[:]), 0, ["PXI", "FPU"], ["RAW1"], gat=128)
    for h in range(2):
        c = slice(128 * h, 128 * h + 128)
        ts(T.AQ[:, c], T.RAWF[:, c], M256, -M256, ALU.add, ALU.add, 128, ["RAW%d" % h], ["AQ%d" % h])
    act(T.OMG[:], T.OMI[:].indirect(T.LU[:, 0:24]), 0, ["OMI", "OMz", "LU0"], ["OMG"], scale=2.0 ** 36, gat=384)
    mm([(T.pY[:, 0:40], T.ZW[:, 112 - 16 * c:240 - 16 * c], T.OMG[:, 48 * c:48 * c + 40], c == 0, c == 7) for c in range(8)], 2048,
       ["ZW", "OMG"], ["pY"], "pY")
    act(T.BND[:], T.pY[:, 0:40], 40, ["pY"], ["BND"], "pY")
    for c2 in range(2):
        c = slice(512 * c2, 512 * c2 + 512)
        bk = "pF%d" % c2
        act(T.PF[:, c], T.PXI[:, c], 512, ["PXI"], [("PF", c2)])
        ts(T.WO[:, c], T.PXI[:, c], M256, -M256, ALU.add, ALU.add, 512, ["PXI"], [("WO", c2)])
        group(T[bk][:], [(T.I15[:], T.WO[:, c], 2048), (T.IDF[:], T.PF[:, c], 2048)], True, [("WO", c2), ("PF", c2), "I15", "IDF"], [bk], bk)
        act(T.PK[:, c], T[bk][:], 512, [bk, "PC3"], [("PK", c2)], bk, bias=T.PCOL[:, 3:4])
    PKK, PFK = [("PK", c2) for c2 in range(2)], [("PF", c2) for c2 in range(2)]

    def stage(dst, dk, lo, hi, n, rk, bank=None):
        tt(dst[:, :, 0:16:2], lo, hi, ALU.min, n, rk, [dk + "a"], bank)
        tt(dst[:, :, 1:16:2], lo, hi, ALU.max, n, rk, [dk + "b"], bank)

    EVK = [[("pTa", a, x) for x in range(4)] for a in range(2)]
    ODK = [[("M", a, x) for x in range(4)] for a in range(2)]

    for v in range(NV):
        e = v % 2
        last = v == NV - 1
        AB, WT = T["AB%d" % e], T["AB%d" % (1 - e)]
        IDX, SA, SB, CA, CB = T["IDX%d" % e], T["SA%d" % e], T["SB%d" % e], T["CA%d" % e], T["CB%d" % e]
        kind[0] = (v, "pixel")
        pix, lane = T.pI[:, 8:16, 0:16], T.pI[:, 0:8, 0:16]
        PA, PB = [("pI", 0), ("pI", 1)], [("pI", 2), ("pI", 3)]
        if v == 0:
            group(lane, [(T.AQ[:, 0:128], T.I15[:], 512), (T.RAWF[:, 0:128], T.IDF[:], 512), (I["IB"], T.CP2[:], 128)], True,
                  ["AQ0", "RAW0", "IDF", "I15", "IB", "CP2"], PA, "pI")
            group(pix, [(T.AQ[:, 128:256], T.PERM15[:], 512), (T.RAWF[:, 128:256], T.PERM[:], 512), (I["IB"], T.CP3[:], 128)], True,
                  ["AQ1", "RAW1", "PERM", "PERM15", "IB", "CP3"], PB, "pI")
        else:
            act(T.PG[:], T.PK[:].indirect(T.RN[:, 8 * v - 8:8 * v]), 0, PKK + [("RN", v - 1)], ["PG"], gat=128)
            group(pix, [(T.PG[:], T.PERM[:], 512)], True, ["PG", "PERM"], PB, "pI")
        act(T.PGS[:], pix, 128, PB, ["PGS"], "pI")
        kind[0] = (v, "merge")
        if v:
            group(lane, [(I["IB"], T.CP1[:], 128), (I["IB"], T.CP4[:], 128)], True, ["IB", "CP1", "CP4"], PA, "pI", False)
            lst, lk = T.RL[:, v - 1], [("RL", v - 1)]
            if not SENDER:
                stage(T.Q1, "Q1", T.RT[:, v - 1, :, 0:8], T.RT[:, v - 1, :, 8:16], 128, [("RT", v - 1)])
                for dst, dk, src, sk in ((T.Q0, "Q0", T.Q1, "Q1"), (T.Q1, "Q1", T.Q0, "Q0")):
                    stage(dst, dk, src[:, :, 0:8], src[:, :, 8:16], 128, [sk + "a", sk + "b"])
                for x, o in enumerate((ALU.min, ALU.max)):
                    tt(T.pS[:, 0:8, x:16:2], T.Q1[:, :, 0:8], T.Q1[:, :, 8:16], o, 128, ["Q1a", "Q1b"], EVK[0][2 * x:2 * x + 2], "pS")
                tt(T.pV[:, 0:128], T.TCB[:], T.pS[:, 0:8, 0:16], ALU.add, 128, EVK[0] + ["TCB"], ["pVa"], ["pV", "pS"])
                tt(T.Q1[:], T.RL[:, v - 1], T.pV[:, 0:128], ALU.max, 128, [("RL", v - 1), "pVa"], ["Q1a", "Q1b"], "pV")
                lst, lk = T.Q1[:], ["Q1a", "Q1b"]
            ts(T.AQ[:, 0:128], lst, M256, -M256, ALU.add, ALU.add, 128, lk, ["AQ0"])
            group(lane, [(T.I15[:], T.AQ[:, 0:128], 512), (T.IDF[:], lst, 512)], False, ["AQ0", "I15", "IDF"] + lk, PA, "pI")
        for k in range(4):
            a, b = k % 2, 16 * (k % 2)
            for hf in range(2):
                for x, o in enumerate((ALU.min, ALU.max)):
                    if k == 0:
                        i0, i1, rk, bk = T.PGS[:, :, 8 * hf:8 * hf + 8], T.pI[:, 0:8, 8 * hf:8 * hf + 8], ["PGS"] + PA, ["pI"]
                    else:
                        i0, i1 = T.M0[:, :, 16 - b + 8 * hf:24 - b + 8 * hf], T.pS[:, 0:8, 16 - b + 8 * hf:24 - b + 8 * hf]
                        rk, bk = EVK[1 - a] + ODK[1 - a], ["pS"]
                    if hf == 0:
                        tt(T.pS[:, 0:8, b + x:b + 16:2], i0, i1, o, 64, rk, EVK[a][2 * x:2 * x + 2], bk + ["pS"])
                    else:
                        tt(T.M0[:, :, b + x:b + 16:2], i0, i1, o, 64, rk, ODK[a][2 * x:2 * x + 2], bk)
        for x, o in enumerate((ALU.min, ALU.max)):
            tt(T.K[:, :, x:32:2], T.M0[:, :, 16:32], T.pS[:, 0:8, 16:32], o, 128, EVK[1] + ODK[1], ["K" + "ab"[x]], "pS")
        KK = ["Ka", "Kb"]
        act(T.ZF[:, :, 0:32], T.K[:], 256, KK, ["ZF"], bias=M4096)
        ts(T.YI[:], T.K[:], 2175, None, ALU.bitwise_and, None, 256, KK, ["YI"])
        ts(T.YF[:], T.YI[:], -1088.0, None, ALU.add, None, 256, ["YI"], ["YF"])
        if ON_S["YF"]:
            act(T.D0[:], T.YI[:], 256, ["YI"], ["D0"], scale=-2.0, bias=2176.0)
        else:
            ts(T.D0[:], T.YF[:], -2.0, None, ALU.mult, None, 128, ["YF"], ["D0"])
        act(T.SLAB[:, :, 1:32], T.ZF[:, :, 1:32], 248, ["ZF"], ["SLAB"], scale=2.0 ** -19, bias=127.50390625 - M4096 * 2.0 ** -19)
        scan(T.A16[:], T.D0[:], T.YF[:], 960.0, ALU.min, ALU.max, 128, ["D0", "YF"], ["A16"])
        scan(T.B16[:], T.D0[:], T.YF[:], -1088.0, ALU.max, ALU.min, 128, ["D0", "YF"], ["B16"])
        for x, (src, sk, add, bk, keys) in enumerate(((T.A16, "A16", -30720.0 - 112.0, "pI", [("pI", 0), ("pI", 1)]),
                                                      (T.B16, "B16", 34816.0 - 112.0, "pS", ["pSa"]))):
            its = []
            for h in range(2):
                o = T[bk][:, 4 * h:4 * h + 4, :]
                its.append((o, T.SLAB[:, :, h:32:2], I["IB"], True, False))
                its.append((o, src[:, h:256:2], I["IH32"], False, True))
            mm(its, 512, [sk, "SLAB", "SLAB0", "IB", "IH32"], keys, bk)
            if ON_S["IDX"] and x == 0:
                act(IDX[:, 0:256], T[bk][:, 0:8, :], 256, keys, [("IDX", e, x)], bk, func=ACT.Relu, bias=add)
            else:
                ts(IDX[:, 256 * x:256 * x + 256], T[bk][:, 0:8, :], add, 0.0, ALU.add, ALU.max, 256, keys, [("IDX", e, x)], bk)
        kind[0] = (v, "keys")
        group(T.pI[:, 0:8, :], [(T.IDF[:], T.ZF[:, :, 1:33], 1024), (T.NIF[:], T.ZF[:, :, 0:32], 1024)], True,
              ["ZF", "ZFe", "IDF", "NIF"], [("pI", 0), ("pI", 1)], "pI")
        act(T.LB[:, :, 1:32], T.pI[:, 0:8, 1:32], 248, [("pI", 0), ("pI", 1)], ["LB"], "pI", scale=4096.0)
        asel(T.BD[:, 1:256:32], T.BND[:, 8 * v:8 * v + 8], [[0, 8]], 0, 8, ["BND"], ["BD"], 0.0, 0)
        if not last:
            group(T.pK[:, 256:512], [(I["IH"], T.B16[:], 256), (I["NIH"], T.A16[:], 256), (I["I2"], T.C1024[:], 256)], True,
                  ["A16", "B16", "IH", "NIH", "I2", "C1024"], ["pKb"], "pK")
            group(T.pK[:, 0:256], [(T.I16[:], T.ZF[:, :, 0:32], 1024), (I["N21"], T.CZ[:], 256), (I["N5"], T.C1024[:], 256),
                                    (I["IHH"], T.A16[:], 256), (I["IHH"], T.B16[:], 256)], True,
                  ["ZF", "A16", "B16", "I16", "N21", "N5", "C1024", "CZ", "IHH"], ["pKa"], "pK", False)
        kind[0] = (v, "sg")
        def piece(buf, c, n):
            return buf[:, 512 * (c % 4):512 * (c % 4 + n), c // 4]

        for c, n in runs(0, 8, SGW[v]):
            act(piece(SA, c, n), T.SG[:].indirect(IDX[:, 32 * c:32 * (c + n)]), 0, ["SG", "SGz", ("IDX", e, 0)],
                [("SA", e, cc) for cc in range(c, c + n)], gat=512 * n)
        for c, n in runs(0, VSHARE[v], SGW[v]) + runs(VSHARE[v], 8, SGW[v]):
            src, rk = T.SG[:].indirect(IDX[:, 256 + 32 * c:256 + 32 * (c + n)]), ["SG", "SGz", ("IDX", e, 1)]
            wk = [("SB", e, cc) for cc in range(c, c + n)]
            if VADD[v]:
                tt(piece(SB, c, n), src, piece(SA, c, n), ALU.add, 1024 * n, rk + [("SA", e, cc) for cc in range(c, c + n)], wk)
            elif c < VSHARE[v]:
                cp(piece(SB, c, n), src, 0, rk, wk, gat=512 * n)
            else:
                act(piece(SB, c, n), src, 0, rk, wk, gat=512 * n)
        SAK, SBK = [("SA", e, c) for c in range(8)], [("SB", e, c) for c in range(8)]
        nr = 8 if last else 16
        mm([(T.pS[:, 0:nr, 0], T.C1024[:, 0:128], T.RMA[:, 0:nr], True, False)], 64, ["C1024", "RMAa", "RMAb"], ["pSa", "pSb"], "pS")
        sums = ((SA, SAK, T.RMA, "RMA"), (SB, SBK, T.RMB, "RMB"))[VADD[v]:]
        for h in range(2):
            for x, (src, keys, rm, rk) in enumerate(sums):
                mm([(T.pS[:, 0:nr, s], src[:, s // 2:2048:16, h], rm[:, 0:nr], False, x == len(sums) - 1 and s == 31)
                    for s in range(2 - h, 32, 2)], 16 * 64, keys[4 * h:4 * h + 4] + [rk + "a", rk + "b"], ["pSa", "pSb"], "pS")
        for hf, n in runs(0, 2 * (1 - VADD[v]), ADDW[v]):
            c, pk = slice(1024 * hf, 1024 * (hf + n)), [4 * h + u for h in range(2) for u in range(2 * hf, 2 * (hf + n))]
            dma("G", g, SB[:, c, :], SA[:, c, :], n * 1048576, [SAK[u] for u in pk], [SBK[u] for u in pk], "add%d" % (v + hf),
                accum_op=ALU.add, max_dma_last_dim=4096)
        kind[0] = (v, "seen")
        tt(T.W[:, 1:257], T.LB[:], T.pS[:, 0:8, :], ALU.mult, 256, ["LB", "LB0", "pSa"], ["W"], "pS")
        if not last and ON_S["SN"]:
            act(T.SN[:], T.pS[:, 8:16, :], 256, ["pSb"], ["SN"], "pS", func=ACT.Sign, bias=-0.5)
        elif not last:
            ts(T.SN[:], T.pS[:, 8:16, :], 0.5, 0.5, ALU.is_gt, ALU.subtract, 256, ["pSb"], ["SN"], "pS")
        scan(T.pV[:, 0:256], T.W[:, 0:256], T.BD[:], 0.0, ALU.add, ALU.max, 256, ["BD", "W", "W0"], ["pVa"], "pV")
        if not last:
            tt(T.UU[:], T.SN[:], T.pK[:, 256:512], ALU.mult, 256, ["SN", "pKb"], ["UU"], "pK")
            group(T.pK[:, 0:256], [(I["HALF" if ON_S["SN"] else "IB"], T.UU[:], 256)], False, ["IB", "HALF", "UU"], ["pKa"], "pK", not ON_S["LV"])
        tt(T.TT[:, :, 0:32], T.LB[:], T.pV[:, 0:256], ALU.min, 256, ["LB", "LB0", "pVa"], ["TT"], "pV")
        hk = [("pI", 0), ("pI", 1), ("pI", 2)]
        mm([(T.pI[0:96, 4 * h:4 * h + 4, :], T.TT[:, :, h:36:3], T.IDF[:], True, True) for h in range(3)], 1536, ["TT", "TTe", "IDF"], hk, "pI")
        act(T.XL[0:96], T.pI[0:96, 0:12, :], 384, hk, ["XL"], "pI", scale=2.0 ** -28, bias=-128.0)
        if not last:
            if ON_S["LV"]:
                act(T.LV[:], T.TT[:, :, 0:32], 256, ["TT"], ["LV"], func=ACT.Relu, scale=-1.0, bias=1.0)
                group(T.pK[:, 0:256], [(I["N21"], T.LV[:], 256)], False, ["N21", "LV"], ["pKa"], "pK")
                scan(T.G[:, 1:257], T.MG[:], T.pK[:, 0:256], 127.0, ALU.min, ALU.max, 256, ["MG", "pKa"], ["G"], "pK")
            else:
                tt(T.LE[:], T.TT[:, :, 0:32], T.pK[:, 0:256], ALU.min, 256, ["TT", "pKa"], ["LE"], "pK")
                scan(T.G[:, 1:257], T.MG[:], T.LE[:], 127.0, ALU.min, ALU.max, 256, ["MG", "LE"], ["G"])
            ts(T.GI[:], T.G[:, 32:257:32], 8.0, None, ALU.mult, None, 8, ["G"], ["GI"])
            ts(T.NB[:], T.GI[:], 0x3F8, None, ALU.bitwise_and, None, 8, ["GI"], ["NB"])
            ts(T.NA[:], T.GI[:], 20, None, ALU.arith_shift_right, None, 8, ["GI"], ["NA"])
            tt(T.NM[:, 0:8], T.NA[:], T.NB[:], ALU.add, 16, ["NA", "NB"], ["NM"])
            act(T.NX[:], T.NM[:].indirect(T.LU[:, 24:29]), 0, ["NM", "NMz", "LU1"], ["NX"], gat=80)
            mm([(T.pS[:, 0, 0:16], T.ZH[:, 112 - 16 * ((b + 1) % 8):240 - 16 * ((b + 1) % 8)], T.NX[:, 8 * b:8 * b + 16], b == 0, b == 7)
                for b in range(8)], 512, ["NX", "ZH"], ["pSa"], "pS")
            cp(T.NU[:, 16 * v:16 * v + 16], T.pS[:, 0, 0:16], 16, ["pSa"], [("NU", v)], "pS")
            send(T.NU[:, 16 * v:16 * v + 8], T.RN[:, 8 * v:8 * v + 8], 2048, [("NU", v)], [("RN", v)], "rn%d" % v)
            kind[0] = (v, "list")
            if DF_SCAN:
                scan(T.DF[:], T.G[:, 1:257], T.G[:, 0:256], 0.0, ALU.max, ALU.subtract, 256, ["G", "G0"], ["DF"])
            else:
                tt(T.DF[:], T.G[:, 1:257], T.G[:, 0:256], ALU.subtract, 512, ["G", "G0"], ["DF"])
            ts(T.LOW[:], T.DF[:], 255, None, ALU.bitwise_and, None, 256, ["DF"], ["LOW"])
            if ON_S["INV"]:
                act(T.INV[:], T.LOW[:], 256, ["LOW"], ["INV"], func=ACT.Relu, scale=-2.0 ** -5, bias=2.0 ** -5)
            else:
                ts(T.INV[:], T.LOW[:], 0.0, 2.0 ** -5, ALU.is_equal, ALU.mult, 256, ["LOW"], ["INV"])
            tt(T.pV[:, 0:256], T.LOW[:], T.pV[:, 256:512], ALU.min, 256, ["LOW", "SC"], ["pVa"], "pV")
            scan(T.CI[:], T.MASKB[:], T.INV[:], 1.0, ALU.min, ALU.add, 128, ["MASKB", "INV"], ["CI"])
            tt(T.YY[:], T.pV[:, 0:256], T.CI[:], ALU.subtract, 256, ["pVa", "CI"], ["YY"], "pV")
            R = T.pS[:, 8:16, :]
            group(R, [(I["IC"], T.C1024[:], 256), (I["I26"], T.INV[:], 256)], True, ["IC", "C1024", "I26", "INV"], ["pSb"], "pS", False)
            group(R, [(I["I29"], T.YY[:], 256)], False, ["I29", "YY"], ["pSb"], "pS", False)
            for k, (c1, c0, ident) in enumerate(((-64.0, 769.0, "I6"), (-16.0, 384.75, "I6"), (-4.0, 192.4375, "I6"), (-4.0, 416.9375, "IQ"))):
                f = T.FL[:, 256 * k:256 * k + 256]
                if FLOOR_V[k]:
                    ts(f, T.YY[:], c1, c0, ALU.mult, ALU.add, 128, ["YY"], [("FL", k)])
                else:
                    act(f, T.YY[:], 256, ["YY"], [("FL", k)], scale=c1, bias=c0)
                group(R, [(I[ident], f, 256)] + [(I["IS"], T.CZ[:], 256), (I["N12"], T.INV[:], 256)] * (k == 3), False,
                      [ident, ("FL", k), "IS", "CZ", "N12", "INV"], ["pSb"], "pS", k == 3)
            tt(T.pS[:, 0:8, 0:16], T.G[:, 1:257:2], T.pS[:, 8:16, 0:32:2], ALU.add, 128, ["G", "pSb"], EVK[0], "pS")
            tt(T.M0[:, :, 0:16], T.G[:, 2:257:2], T.pS[:, 8:16, 1:32:2], ALU.add, 128, ["G", "pSb"], ODK[0], "pS")
            for k in range(4):
                a, b, d = k % 2, 16 * (k % 2), 16 - 16 * (k % 2)
                for par in range(2):
                    for x, o in enumerate((ALU.min, ALU.max)):
                        dst = T.M0[:, :, d + 8 * x:d + 8 * x + 8] if par else T.pS[:, 0:8, d + 8 * x:d + 8 * x + 8]
                        tt(dst, T.M0[:, :, b + par:b + 16:2], T.pS[:, 0:8, b + par:b + 16:2], o, 64, EVK[a] + ODK[a],
                           (ODK if par else EVK)[1 - a][2 * x:2 * x + 2], "pS")
            tt(T.OUT[:, v], T.M0[:, :, 0:16], T.pS[:, 0:8, 0:16], ALU.min, 128, EVK[0] + ODK[0], [("OUT", v)], "pS")
            if not SENDER:
                send(T.OUT[:, v], T.RL[:, v], 65536, [("OUT", v)], [("RL", v)], "rl%d" % v)
            act(T.PG2[:], T.PF[:].indirect(T.NU[:, 16 * v + 8:16 * v + 16]), 0, PFK + [("NU", v)], ["PG2"], scale=2.0 ** -20, gat=128)
            act(T.Y2[:], T.G[:, 0:257].indirect(T.LU[:, 40:48]), 0, ["G", "G0", "LU"], ["Y2"], scale=2.0 ** -20, gat=128)
            group(T.pI[:, 0:4, :], [(T.Y2[:], T.NIF[:], 512), (T.IDF[:], T.PG2[:], 512)], True, ["PG2", "Y2", "IDF", "NIF"], [("pI", 0)], "pI")
            act(T.U2[:], T.pI[:, 0:4, :], 128, [("pI", 0)], ["U2"], "pI", func=ACT.Sign, scale=-1.0)
            act(T.UJ[:], T.CI[:].indirect(T.LU[:, 32:40]), 0, ["CI", "LU"], ["UJ"], func=ACT.Relu, scale=32.0, bias=-16.0, gat=128)
            ta, tk = T.pI[:, 8:16, 0:16], [("pI", 2), ("pI", 3)]
            for out in (T.pI[:, 8:16, 16:32],):
                group(out, [(I["I1"], T.JC[:], 128), (I["NI1"], T.UJ[:], 128), (T.U2[:], T.BDG[:], 128), (T.U2[:], I["I23"], 128)], True,
                      ["I1", "NI1", "JC", "UJ", "U2", "BDG", "I23"], tk, "pI", out is not ta)
            act(T.WN[:], T.pI[:, 8:16, 16:32], 128, tk, ["WN"], "pI", func=ACT.Sign, scale=2.0 ** -20, bias=0.5)
            if ON_S["T0"]:
                group(T.pI[:, 4:8, :], [(T.IDF[:], T.PG2[:], 512), (I["IB"], T.U2[:], 128)], True, ["PG2", "U2", "IDF", "IB"], [("pI", 1)], "pI")
                act(T.T0[:], T.pI[:, 4:8, :], 128, [("pI", 1)], ["T0"], "pI", func=ACT.Relu, scale=-1.0)
            else:
                tt(T.T0[:], T.PG2[:], T.U2[:], ALU.max, 256, ["PG2", "U2"], ["T0"])
            for out, stop in ((ta, False),):
                group(out, [(I["I1"], T.JC[:], 128), (I["NI1"], T.UJ[:], 128), (T.U2[:], T.BDG[:], 128), (T.U2[:], I["I23"], 128)], True,
                      ["I1", "NI1", "JC", "UJ", "U2", "BDG", "I23"], tk, "pI", stop)
            group(ta, [(I["IC"], T.WN[:], 128), (T.U2[:], I["N128"], 128), (I["IS"], T.C1024[:, 0:128], 128),
                       (T.T0[:], T.I20[:], 512)], False, ["IC", "WN", "U2", "N128", "IS", "C1024", "T0", "I20"], tk, "pI")
            if SENDER:
                act(T.Q0[:, :, 0:8], T.pI[:, 8:16, 0:8], 64, tk, ["Q0a", "Q0b"], "pI")
                stage(T.Q1, "Q1", T.Q0[:, :, 0:8], T.pI[:, 8:16, 8:16], 64, ["Q0a", "Q0b"] + tk, "pI")
                for dst, dk, src, sk in ((T.Q0, "Q0", T.Q1, "Q1"), (T.Q1, "Q1", T.Q0, "Q0")):
                    stage(dst, dk, src[:, :, 0:8], src[:, :, 8:16], 128, [sk + "a", sk + "b"])
                for x, o in enumerate((ALU.min, ALU.max)):
                    tt(T.pI[:, 8:16, 16 + x:32:2], T.Q1[:, :, 0:8], T.Q1[:, :, 8:16], o, 128, ["Q1a", "Q1b"], [("pIs", x)], "pI")
                tt(T.pV[:, 0:128], T.TCB[:], T.pI[:, 8:16, 16:32], ALU.add, 128, [("pIs", 0), ("pIs", 1), "TCB"], ["pVa"], ["pV", "pI"])
                tt(T.TO[:, v], T.OUT[:, v], T.pV[:, 0:128], ALU.max, 128, [("OUT", v), "pVa"], [("TO", v)], "pV")
                send(T.TO[:, v], T.RL[:, v], 65536, [("TO", v)], [("RL", v)], "rl%d" % v)
            else:
                act(T.TO[:, v], ta, 128, tk, [("TO", v)], "pI")
                send(T.TO[:, v], T.RT[:, v], 65536, [("TO", v)], [("RT", v)], "rt%d" % v)
        kind[0] = (v, "co")
        for x, (dst, key) in enumerate(((CA, "CA"), (CB, "CB"))):
            for c4, n in runs(0, 4, COW[v]):
                for h in range(2):
                    o = 256 * x + 128 * h + 32 * c4
                    (cp if (x, c4, h) in COV[v] else act)(
                        dst[:, 1024 * c4 + h:1024 * (c4 + n):2], T.CO[:].indirect(IDX[:, o:o + 32 * n]), 0,
                        ["CO", "COz", ("IDX", e, x)], [(key, e, 2 * cc + h) for cc in range(c4, c4 + n)], gat=512 * n)
        for hh in range(CADD[v]):
            c = slice(2048 * hh, 2048 * hh + 2048)
            dma("G", g, CB[:, c], CA[:, c], 1048576, [("CA", e, cc) for cc in range(4 * hh, 4 * hh + 4)],
                [("CB", e, cc) for cc in range(4 * hh, 4 * hh + 4)], "cadd%d" % (2 * v + hh), accum_op=ALU.add, max_dma_last_dim=4096)
        kind[0] = (v, "a")
        ABH = [("ABh", e, c) for c in range(8)]
        yo = slice(128 * v, 128 * v + 128)
        apart = APART[v]
        for jp in range(8):
            bk = "pF%d" % ((16 * v + jp) % 3)
            hf, jq, h = jp // 4, jp % 4, jp % 2
            its = []
            for k in range(8):
                j, c = divmod(4 * k + jq, 3)
                its.append((T[bk][:, k:512:8], T.SEL[0:96, 128 * j:128 * j + 128], T.XL[0:96, 128 * c + 64 * hf:128 * c + 64 * hf + 64], True, True))
            mm(its, 512, [("SEL", u) for u in range(3)] + ["XL"], [bk], bk)
            lo = 2048 * hf
            tt(AB[:, lo + jq:lo + 2048:4], SB[:, lo // 2 + jq // 2:lo // 2 + 1024:2, h], T[bk][:], ALU.mult, 512,
               [("SB", e, 4 * h + 2 * hf + u) for u in range(2)] + [bk], [("AB", e, jp)], bk)
            if apart[hf]:
                ss = [s for s in range(jq, 32, 4) if s]
                tb = ("pK", "pV")[hf] if last else "pY"
                to = T[tb][:, 0:64] if last else T.pY[:, 64 * hf:64 * hf + 64]
                for u in range(0, len(ss), 4):
                    mm([(to, T.IDF[:], AB[:, lo + s:lo + 2048:32], s == 4, s == 31) for s in ss[u:u + 4]], 256 * len(ss[u:u + 4]),
                       [("AB", e, jp), "IDF"], [("tau", hf)], tb)
                if jq == 3:
                    act(T.YT[:, 128 * v + 64 * hf:128 * v + 64 * hf + 64], to, 64, [("tau", hf)], [("YT", v, hf)], tb, scale=-8.0)
        ABK = [("AB", e, j) for j in range(8)]
        free = [("YT", v - 1, 0), ("YT", v - 1, 1), ("YC", v - 1)]
        kind[0] = (v, "one")
        for hf in range(2):
            ns = 4 * hf + (ONE_S[v] + hf) // 2
            rk = ABK[4 * hf:4 * hf + 4]
            for c, n in runs(4 * hf, ns, ONEW[v]) if ONE_SPLIT[v] else runs(min(4 * hf, ONE_S[v]), min(4 * hf + 4, ONE_S[v]), ONEW[v]):
                c0 = slice(512 * c, 512 * (c + n))
                act((T.AC if apart[hf] else AB)[:, c0], AB[:, c0], 512 * n, rk, ABH[c:c + n] + [("AC", u) for u in range(c, c + n)] * apart[hf], bias=1.0)
            for c, n in runs(ns, 4 * hf + 4, 4) if ONE_SPLIT[v] else runs(max(4 * hf, ONE_S[v]), max(4 * hf + 4, ONE_S[v]), 4):
                dma("G", g, AB[:, 512 * c:512 * (c + n)], T.ONES[:, 0:512 * n], n * 2 * 262144, rk + ["ONES"], ABH[c:c + n],
                    "one%d" % (2 * v + hf), accum_op=ALU.add, max_dma_last_dim=4096)
        for c in range(8):
            kind[0] = (v, c)
            bk = "pF%d" % ((16 * v + 8 + c) % 3)
            lo = 512 * c
            cols = (("CA", CA), ("CB", CB))[c // 4 < CADD[v]:]
            its = ([(T[bk][:], I["NIH"], buf[:, lo:lo + 512]) for key, buf in cols]
                   + [(T[bk][:, 0:511], I["IH"], buf[:, lo + 1:lo + 512]) for key, buf in cols])
            mm([it + (k == 0, k == len(its) - 1) for k, it in enumerate(its)], 512 * len(its),
               [(key, e, c // 2 * 2 + h) for key, buf in cols for h in range(2)] + ["IH", "NIH"], [bk], bk)
            back = slice(lo + 511, lo - 1 if lo else None, -1)
            ok = ABK[c // 4 * 4:c // 4 * 4 + 4] + [ABH[c]]
            scan(T.WO[:, back], T[bk][:, ::-1], (T.AC if apart[c // 4] else AB)[:, back], 0.0, ALU.add, ALU.mult, 512,
                 ok + [bk] + [("AC", c)] * apart[c // 4], [("WO", c)], bk)
            if last and not apart[c // 4]:
                scan(WT[:, lo:lo + 512], T.MASK[:], AB[:, lo:lo + 512], 0.0, ALU.mult, ALU.add, 512, ok + ["MASK"] + free, [("WT", c)])
        kind[0] = (v, "tau")
        if not last and sum(apart) < 2:
            a0, w = 64 * apart[0], 4 if apart[0] else 2
            for j in range(0, 32, w):
                ss = [s for s in range(j, j + w) if s]
                mm([(T.pY[:, a0:128], T.IDF[:], AB[:, 32 * a0 + s:4096:32], s == 1, s == 31) for s in ss], 1024 // w * len(ss),
                   ABK[a0 // 16:] + ABH[a0 // 16:] + ["IDF"], [("tau", 0), ("tau", 1)], "pY")
            act(T.YT[:, 128 * v + a0:128 * v + 128], T.pY[:, a0:128], 128 - a0, [("tau", 0), ("tau", 1)], [("YT", v, u) for u in range(apart[0], 2)], "pY",
                scale=-8.0, bias=248.0)
        for hf in range(2):
            if last and not apart[hf]:
                act(T.YT[:, 128 * v + 64 * hf:128 * v + 64 * hf + 64], WT[:, 2048 * hf + 31:2048 * hf + 2048:32], 64,
                    [("WT", c) for c in range(4 * hf, 4 * hf + 4)], [("YT", v, hf)], scale=-8.0, bias=248.0)
        WOK = [("WO", c) for c in range(8)]
        onp = ON_P["YC"] and not last
        na = 64 * CADD[v]
        group(T.pY[:, 128:256], [(I["IH"], CB[:, 1:4096:32], 128)], True, [("CB", e, cc) for cc in range(8)] + ["IH"], ["pYc"], "pY",
              na == 128 and not onp)
        if na < 128:
            group(T.pY[:, 128 + na:256], [(I["IH"], CA[:, 32 * na + 1:4096:32], 128)], False, [("CA", e, cc) for cc in range(8)] + ["IH"], ["pYc"], "pY", not onp)
        if onp:
            group(T.pY[:, 128:256], [(T.IDF[:], T.WO[:, 1:4096:32], 512)], False, WOK + ["IDF"], ["pYc"], "pY")
            act(T.YC[:, yo], T.pY[:, 128:256], 128, ["pYc"], [("YC", v)], "pY")
        else:
            tt(T.YC[:, yo], T.WO[:, 1:4096:32], T.pY[:, 128:256], ALU.add, 128, WOK + ["pYc"], [("YC", v)], "pY")
        dma("Y", Y, T.yc[:, yo], T.YC[:, yo], 65536, [("YC", v)], [], "dst")
        dma("Y", Y, T.yt[:, yo], T.YT[:, yo], 65536, [("YT", v, 0), ("YT", v, 1)], [], "dst")
    return ops, n_out


def rank_program(g, core, T, topo):
    if T.rank_of(core) is None:
        return
    ops, n_out = build(g, core, T, topo)
    order = plan(ops)
    queues = {"V": g.vector, "S": g.scalar, "P": g.tensor, "G": g, "Y": g.sync}
    count = {}
    known = {q: {} for q in queues}
    for i in order:
        o = ops[i]
        q = o["q"]
        if q == "D":
            if o["cost"][3] == "send":
                o["at"] = (o["sem"], o["inc"])
                o["clock"] = {o["sem"]: o["inc"]}
                count[o["sem"]] = o["inc"]
            else:
                o["at"], o["clock"] = ops[i - 1]["at"], ops[i - 1]["clock"]
            continue
        kn = known[q]
        need = {}
        for d in o["deps"]:
            od = ops[d]
            if q == "P" and od["q"] == "P":
                continue
            s, c = od["at"]
            if kn.get(s, 0) < c and need.get(s, (0, 0))[0] < c:
                need[s] = (c, d)
        for s, (c, d) in sorted(need.items(), key=lambda x: -ops[x[1][1]]["t"]):
            if kn.get(s, 0) >= c:
                continue
            queues[q].wait_ge(T.sem[s], c)
            for s2, c2 in ops[d]["clock"].items():
                if kn.get(s2, 0) < c2:
                    kn[s2] = c2
        ins = o["fn"]()
        if o["sem"] == "*":
            count["sent"] = count.get("sent", 0) + n_out
            continue
        ins.then_inc(T.sem[o["sem"]], o["inc"])
        count[o["sem"]] = count.get(o["sem"], 0) + o["inc"]
        o["at"] = (o["sem"], count[o["sem"]])
        o["clock"] = dict(kn)
        o["clock"][o["sem"]] = count[o["sem"]]
    for s, c in count.items():
        g.wait_ge(T.sem[s], c)
